import numpy as np, ml_dtypes
CORES = [16,17,18,19,32,33,34,35]
N = 8
import mx_ref
BF = ml_dtypes.bfloat16
def gcols(t, e):
    v = np.concatenate([t.reshape(8, 16, -1, 4), np.zeros((8, 16, 1, 4), BF)], axis=2)
    return np.ascontiguousarray(np.stack([v[g][:, e[g]] for g in range(8)])).reshape(128, -1)
def tile(rs):
    return np.stack(rs, axis=2).reshape(128, -1).astype(BF)
def cut(t, i, w=512):
    return t[:, w * i:w * i + w]
def pick(q, e):
    c = np.concatenate([q[0].reshape(128, -1, 4), np.zeros((128, 1, 4), np.uint8)], axis=1); s = np.concatenate([q[1], np.ones((16, 1), np.uint8)], axis=1)
    return (np.ascontiguousarray(c[:, e].reshape(128, -1)), np.ascontiguousarray(s[:, e]))
def join(*qs):
    return (np.concatenate([q[0] for q in qs], axis=1), np.concatenate([q[1] for q in qs], axis=1))
def put(q, e, v):
    c, s = q[0].reshape(128, -1, 4).copy(), q[1].copy(); c[:, e] = v[0].reshape(128, -1, 4); s[:, e] = v[1]
    return (c.reshape(128, -1), s)
def pk(c, s):
    return (np.ascontiguousarray(c), mx_ref.live(s))
def emit(q):
    return q[0], q[1]
def packed(v, rng):
    q = [mx_ref.quantize(np.ascontiguousarray(v[r])) for r in range(N)]
    return np.stack([a for a, b in q]), np.stack([mx_ref.plane(b, rng) for a, b in q])
def values_of_codes():
    e, c = np.zeros((128, 128, 4), np.float32), np.zeros((128, 2, 4), np.uint8)
    e[np.arange(128), np.arange(128), 0] = 1
    c[:127, :, 0] = np.arange(256).reshape(2, 128).T[:127]
    return mx_ref.matmul(mx_ref.quantize(e.reshape(128, 512).astype(BF)), (c.reshape(128, 8), np.full((16, 2), 127, np.uint8))).T.reshape(-1).astype(np.float64)
CODE_VALUE, SCALE_VALUE = values_of_codes(), 2.0 ** (np.arange(256) - 127.0)
def decode(q):
    return (CODE_VALUE[q[0]].reshape(16, 8, -1, 4) * SCALE_VALUE[q[1]][:, None, :, None] + 0.0).reshape(128, -1).astype(np.float32)
def f(rng, *shape):
    return mx_ref.flush((rng.standard_normal(shape, dtype=np.float32) * np.exp2(rng.integers(-2, 3, shape[:-1] + (1,)))).astype(BF))
def wide(rng, *shape, cols=0):
    v = rng.standard_normal(shape, dtype=np.float32) * np.exp2(rng.integers(-12, 13, shape)).astype(np.float32)
    if cols: v *= np.repeat(np.exp2(rng.integers(-cols, cols + 1, shape[:-2] + (1, shape[-1] // 4))) * (rng.random(shape[:-2] + (1, shape[-1] // 4)) > 0.0625), 4, axis=-1).astype(np.float32)
    return mx_ref.flush(v.astype(BF))
C, K, R = 256, 96, 3
STEP = [1, 2, 4]
PAIRS = np.array([(i, j) for i in range(K) for j in range(K) if (i + 1) * (j + 1) <= K])
PI, PJ = PAIRS[:, 0], PAIRS[:, 1]
def partner(r, t):
    return r ^ STEP[t]
def best(s, n):
    return np.argsort(-s, axis=1, kind="stable")[:, :n]
def big(v):
    v = v.astype(np.float32)
    v[np.abs(v) < np.float32(2.0 ** -16)] = 0
    return v.astype(BF)
def numbers_of(rng):
    return {"x": big(f(rng, N, 128, 4 * C)), "u": np.array(f(rng, N, 128, 512)), "v": np.array(f(rng, N, 128, 512))}
def weights(rng, w):
    c, p = packed(w, rng)
    return {"wc": c, "ws": p}
def signs(rng):
    return np.stack([rng.permutation(8) % 2 * 2.0 - 1.0 for r in range(N)])
def half(rng):
    return (np.arange(N) >> int(rng.integers(1, N.bit_length() - 1))) & 1 == int(rng.integers(2))
def setup_inputs(rng):
    return {**numbers_of(rng), **weights(rng, big(f(rng, N, 128, 2048)))}
def setup_inputs_ties(rng):
    d = numbers_of(rng)
    e = rng.permutation(N)
    x = d["x"].reshape(N, 8, 16, C, 4)
    for r in range(N):
        k = np.zeros(C, int) if r == e[0] else rng.permutation(C) % 3
        a = x[r][:, :8, :3].copy()
        a[:, :, 2] = 0
        x[r][:, :8] = a[:, :, k]
    x[e[1]] = 0
    u = d["u"].reshape(N, 8, 16, 128, 4)
    u[:, :, 8:, ::16] = 0
    w = big(f(rng, N, 128, 2048)).reshape(N, 8, 16, 4, 8, 16, 4)
    w[:, :, 8:, :, :, :8] = 0
    return {"x": x.reshape(N, 128, 4 * C), "u": u.reshape(N, 128, 512), "v": d["v"], **weights(rng, w.reshape(N, 128, 2048))}
def setup_inputs_near(rng):
    d = numbers_of(rng)
    x = d["x"].astype(np.float32).reshape(N, 8, 16, C, 4)
    a, low = signs(rng), half(rng)
    m = low[:, None] & (a < 0)
    s = np.arange(C) // 2
    s = np.where(m[:, :, None], C // 2 - 1 - s, s)
    g = ((s[:, :, :, None] >> np.arange(8)) & 1) * np.exp2(np.arange(8) - 23.0) * np.where(m, -1.0, 1.0)[:, :, None, None] + 0.0
    x[:, :, 0] = 0
    x[:, :, 0, :, 0] = np.where(low[:, None], 0.0, a)[:, :, None]
    x[:, :, 8] = g[:, :, :, :4]
    x[:, :, 9] = g[:, :, :, 4:]
    x[:, :, 10:] = rng.integers(4, 8, (N, 8, 6, C, 4)) * rng.choice([-1.0, 1.0], (N, 8, 6, C, 4)) * 2.0 ** -20
    x[low, :, 8:] *= np.float32(2.0 ** -4)
    u = d["u"].reshape(N, 128, 128, 4)
    k = np.where(low, 2.0 ** -30, 1.0).astype(np.float32).astype(BF)
    u[:, :, ::16] = 0
    for h in range(0, 128, 16):
        u[:, h, h, 0] = k
        u[:, h + 8:h + 10, h] = k[:, None, None]
    w = big(f(rng, N, 128, 2048)).reshape(N, 128, 4, 8, 16, 4)
    w[:, :, :, :, 0] = 0
    w[:, :, :, :, 8:] = 0
    return {"x": x.reshape(N, 128, 4 * C).astype(BF), "u": u.reshape(N, 128, 512), "v": d["v"], **weights(rng, w.reshape(N, 128, 2048))}
def setup_inputs_huge(rng):
    d = numbers_of(rng)
    x = 2.0 ** 30 * (0.9 + 0.1 * rng.random((N, 128, C, 4)))
    c = np.stack([np.where(rng.permutation(C) % 4 == 0, 1.0, -1.0) for r in range(N)])
    c[half(rng)] = 1
    x *= c[:, None, :, None]
    u = d["u"].reshape(N, 128, 128, 4)
    a = 2.0 ** 30 * (0.9 + 0.1 * rng.random((N, 128, 8, 4))) * signs(rng)[np.arange(N) // 2][:, None, :, None]
    u[:, :, ::16] = a.astype(np.float32).astype(BF)
    w = np.zeros((N, 128, 4, 128, 4), np.float32)
    i = np.arange(128)
    for b in range(4): w[:, i, b, i, b] = -4
    return {"x": x.astype(np.float32).reshape(N, 128, 4 * C).astype(BF), "u": u.reshape(N, 128, 512), "v": d["v"], **weights(rng, w.reshape(N, 128, 2048).astype(BF))}
def setup_inputs_steep(rng):
    d = numbers_of(rng)
    x = d["x"].astype(np.float32).reshape(N, 8, 16, C, 4)
    k = np.argsort(rng.random((N, 8, C)), axis=2)
    x[:, :, 0] = 0
    x[:, :, 0, :, 0] = k // 16 * 16
    x[:, :, 0, :, 1] = k % 16
    x[:, :, 0, :, 2] = 256
    flat = np.arange(N) % 2 == int(rng.integers(2))
    x[flat, :, :8] *= np.float32(2.0 ** -10)
    for r in range(N):
        for g in rng.permutation(8)[:4]: x[r, g, 0, int(rng.integers(C)), 0] = 2.0 ** 30
    u = d["u"].reshape(N, 128, 128, 4)
    u[:, :, ::16] = 0
    for h in range(0, 128, 16): u[:, h, h, :2] = 1
    w = big(f(rng, N, 128, 2048))
    w[:, ::16] = 0
    return {"x": x.reshape(N, 128, 4 * C).astype(BF), "u": u.reshape(N, 128, 512), "v": d["v"], **weights(rng, w)}
def setup_inputs_spread(rng):
    d = setup_inputs(rng)
    d["x"] = big(wide(rng, N, 128, 4 * C, cols=6))
    return d
def check_inputs(d):
    b = []
    for k in ("x", "u", "v"):
        a = np.abs(d[k].astype(np.float32))
        if not (np.isfinite(a).all() and ((a == 0) | (a >= 2.0 ** -30) & (a <= 2.0 ** 30)).all()): b.append("a value of " + k)
    return b
def reference(x, u, v, wc, ws):
    qu = [mx_ref.quantize(u[r]) for r in range(N)]
    lay = [pk(wc[r], ws[r]) for r in range(N)]
    now = [x[r] for r in range(N)]
    taken = [None] * N
    for t in range(R):
        first, score, sent = [], [], []
        for r in range(N):
            s = mx_ref.matmul(qu[r], mx_ref.quantize(now[r]))[::16] + np.float32(0.0)
            o = best(s, K)
            first.append(o)
            score.append(np.take_along_axis(s, o, axis=1))
            sent.append(mx_ref.quantize(gcols(now[r], o)))
        came = decode(join(*sent)).astype(BF)
        for r in range(N):
            e = partner(r, t)
            n = best(score[r][:, PI] + score[e][:, PJ], C)
            taken[r] = n
            one = gcols(now[r], np.take_along_axis(first[r], PI[n], axis=1))
            two = gcols(cut(came, e, 4 * K), PJ[n])
            z = ((one.astype(np.float32) + two.astype(np.float32)) * np.float32(0.5)).astype(BF)
            q, zf = mx_ref.quantize(z), z.astype(np.float32)
            now[r] = tile([np.maximum(mx_ref.matmul(pick(lay[r], np.arange(128 * b, 128 * b + 128)), q), np.float32(0.0)) * np.float32(0.03125) + zf[:, b::4] for b in range(4)])
    y, ol = np.zeros((N, 128, C), np.float32), np.zeros((N, 8, C), np.float32)
    oc, osc = np.zeros((N, 128, 4 * C), np.uint8), np.zeros((N, 16, C), np.uint8)
    for r in range(N):
        q = mx_ref.quantize(now[r])
        y[r] = mx_ref.matmul(mx_ref.quantize(v[r]), q)
        ol[r] = taken[r]
        oc[r], osc[r] = emit(q)
    return {"y": y, "ol": ol, "oc": oc, "osc": osc}

@@ -1,0 +1,495 @@
+from concourse.bass import DstId, RemoteDMATransfer
+from concourse.mybir import dt, AluOpType, ActivationFunctionType
+
+C, K, R = 256, 96, 3
+STEP = [1, 2, 4]
+ROWS = [K // (i + 1) for i in range(K)]
+NP = 464
+NV = 256
+F32, BF, I32, U16, X4, U8 = "float32", "bfloat16", "int32", "uint16", "float8_e4m3fn_x4", "uint8"
+BIG, SMALL = float(2 ** 23), 4096.0
+
+LEN2 = {m: 16 * m for m in range(3, 18)}
+LEN2.update({18: 288, 19: 288, 20: 320, 21: 320, 22: 320})
+LEN2.update({m: 368 for m in range(23, 29)})
+TILES1 = [(256, [15, 14, 13, None]), (192, [12, 11, 10, 9]), (128, [8, 7, 6, 5]), (128, [4, 3, 2, 1])]
+TILES2 = [(368, [28, 27, 26, 25]), (368, [24, 23, 22, 21]), (320, [20, 19, 18, 17]), (272, [16, 15, 14, None]),
+          (208, [13, 12, 11, 10]), (144, [9, 8, 7, 6]), (128, [5, 4, 3])]
+LEN1 = {m: 16 * m for m in range(1, 16)}
+W1 = sum(w for w, s in TILES1)
+W2 = sum(w for w, s in TILES2)
+
+SCRATCH = {}
+for _n, _w, _d in [
+    ("tt", 1024, BF), ("zz", 1024, BF), ("ut", 512, BF), ("vt", 512, BF),
+    ("uq", 128, X4), ("us", 128, U8), ("vq", 128, X4), ("vs", 128, U8), ("wq", 512, X4), ("wp", 512, U8),
+    ("urq", 128, X4), ("urs", 128, U8), ("ucq", 16, X4), ("ucs", 16, U8),
+    ("ruq", 8, X4), ("rus", 8, U8), ("rtq", 128, X4), ("rts", 128, U8),
+    ("zq", 256, X4), ("zs", 256, U8), ("fq", 256, X4), ("fs", 256, U8),
+    ("pcol", 8, I32), ("fcol", 8, F32), ("l32", 18, I32), ("l16", 18, U16),
+    ("rr", 368, BF), ("oh", 256, BF), ("sg", 368, BF), ("sq", 368, BF), ("gm", 256, BF), ("rs", 256, BF), ("mst", 256, BF), ("md", NP, F32),
+    ("gi", 128, BF), ("wt", 1024, BF), ("wcq", 256, X4), ("wcs", 256, U8),
+    ("et", 520, BF), ("eq", 512, X4), ("es", 512, U8), ("zero", 520, BF),
+    ("cidx", 256, F32), ("crow", 48, F32), ("cb", 48, F32), ("bb", 48, F32), ("rsum", 48, F32), ("dg", 32, F32),
+    ("p0", NP, F32), ("nn", NP, F32), ("pk", NP, F32), ("ijl", 32, U16),
+    ("c1", 4 * W1, BF), ("c2", 4 * W2, BF), ("j1", 4 * W1, BF), ("j2", 4 * W2, BF),
+    ("cq1", W1, X4), ("cs1", W1, U8), ("cq2", W2, X4), ("cs2", W2, U8),
+    ("ssb", 256, F32), ("spb", 256, F32), ("xm", NP, F32), ("hh", NP, F32), ("ir", 256, BF), ("sc", NP, F32),
+    ("off2", 30, U16), ("orep", 256, F32), ("prep", NP, F32), ("o4", 24, U16),
+    ("ss", 112, F32), ("ee", 256, F32), ("si", NV, F32), ("vv", 368, F32),
+    ("ap", 384, BF), ("ep", 384, BF), ("dp", 1024, BF), ("ag", 1024, BF), ("rl", 1024, F32),
+    ("x32", 48, I32), ("il", 16, U16), ("jl", 16, U16), ("nb", 768, F32), ("ysb", 256, F32),
+]:
+    SCRATCH[_n] = ("sbuf", [128, _w], _d)
+for _t in range(R):
+    for _n, _w, _d in [("tq", 256, X4), ("ts", 256, U8), ("lq", 256, X4), ("ls", 256, U8), ("ol", 6, U16), ("al", 6, U16),
+                       ("of", 16, U16), ("af", 16, U16), ("ulq", 8, X4), ("uls", 8, U8), ("upq", 128, X4), ("ups", 128, U8)]:
+        SCRATCH[_n + str(_t)] = ("sbuf", [128, _w], _d)
+for _t in range(8):
+    SCRATCH["ps%d" % _t] = ("psum", [128, 512], F32)
+
+SEMAPHORES = (["qv", "qs", "qt", "qg", "dx", "du", "dv", "dw", "dz", "dq", "dr", "dy", "loc", "ru", "rt"]
+              + ["%s%d" % (a, t) for a in ("au", "at", "al", "af") for t in range(R)])
+
+
+def A(name, a=None, b=None, s=1):
+    n = SCRATCH[name][1][1]
+    return (name, 0 if a is None else a, n if b is None else b, s)
+
+
+def col(name, j):
+    return (name, j, j + 1, 1)
+
+
+def half(name, h, w=128):
+    return A(name, w * h, w * h + w)
+
+
+def helper(core, T, topo):
+    mine = [c for c in topo.cores_of(core) if T.rank_of(c) is not None]
+    free = [c for c in topo.cores_of(core) if T.rank_of(c) is None and topo.die(c) != topo.die(core)]
+    return free[mine.index(core)]
+
+
+def far_round(rank, T, topo):
+    return [t for t in range(R) if topo.chip(T.cores[rank ^ STEP[t]]) != topo.chip(T.cores[rank])][0]
+
+
+def hand_on(g, core, T, topo):
+    for r, c in enumerate(T.cores):
+        if helper(c, T, topo) != core:
+            continue
+        t = far_round(r, T, topo)
+        dst = T.cores[r ^ STEP[t]]
+        rid, pid, se = topo.addr(dst)
+        m, n = topo.mask(core, dst), len(topo.engines(core, dst))
+        g.wait_ge(T.sem.ru, 8)
+        g.remote_dma(T["ulq%d" % t][:].bitcast(dt.uint8), T.ruq[:].bitcast(dt.uint8), T.sem["au%d" % t], T.sem.loc, pid, rid, m)
+        g.remote_dma(T["uls%d" % t][:], T.rus[:], T.sem["au%d" % t], T.sem.loc, pid, rid, m)
+        g.wait_ge(T.sem.rt, 2 * len(topo.engines(c, core)))
+        g.remote_dma(T["lq%d" % t][:, 0:128].bitcast(dt.uint8), T.rtq[:].bitcast(dt.uint8), T.sem["at%d" % t], T.sem.loc, pid, rid, m)
+        g.remote_dma(T["ls%d" % t][:, 0:128], T.rts[:], T.sem["at%d" % t], T.sem.loc, pid, rid, m)
+        g.wait_ge(T.sem.loc, 4 * n)
+
+
+def rank_program(g, core, T, topo):
+    rank = T.rank_of(core)
+    if rank is None:
+        hand_on(g, core, T, topo)
+        return
+    ALU, ACT = AluOpType, ActivationFunctionType
+    Q = {"v": g.vector, "s": g.scalar, "t": g.tensor, "g": g, "y": g.sync}
+    count = {}
+    known = {q: 0 for q in Q}
+    done = {q: 0 for q in Q}
+    ops = []
+    hist = {}
+
+    def ap(a):
+        return T[a[0]][:, a[1]:a[2]:a[3]] if a[3] != 1 else T[a[0]][:, a[1]:a[2]]
+
+    def bits(a):
+        if a[0].startswith("ps"):
+            return 1
+        m = 0
+        for c in range(a[1], a[2], a[3]):
+            m |= 1 << c
+        return m
+
+    def op(q, fn, reads, writes, sem=None, acc=False):
+        deps = set()
+        touched = [(a, False) for a in reads] + [(a, True) for a in writes]
+        for a, w in touched:
+            m, bank = bits(a), a[0].startswith("ps")
+            for hm, i, hw, hq in hist.get(a[0], []):
+                if hm & m and (w or hw or (bank and hq != q)) and not (acc and bank and hq == q):
+                    deps.add(i)
+        for i in sorted(deps, reverse=True):
+            if not known[q] >> i & 1:
+                Q[q].wait_ge(T.sem[ops[i][0]], ops[i][1])
+                known[q] |= ops[i][2]
+        me = len(ops)
+        if sem == "remote":
+            count["loc"] = count.get("loc", 0) + fn()
+            ops.append(("loc", None, 0))
+            return
+        if sem is None:
+            s = "q" + q
+            fn().then_inc(T.sem[s], 1)
+            count[s] = count.get(s, 0) + 1
+            done[q] |= 1 << me
+            ops.append((s, count[s], known[q] | done[q]))
+        else:
+            for ins in fn():
+                ins.then_inc(T.sem[sem], 16)
+                count[sem] = count.get(sem, 0) + 16
+            ops.append((sem, count[sem], known[q] | 1 << me))
+        for a, w in touched:
+            h = hist.setdefault(a[0], [])
+            m = bits(a)
+            if w:
+                h[:] = [e for e in h if e[0] & ~m]
+            h.append((m, me, w, q))
+
+    def arrive(sem, n, writes):
+        me = len(ops)
+        count[sem] = n
+        ops.append((sem, n, 1 << me))
+        for a in writes:
+            hist.setdefault(a[0], []).append((bits(a), me, True, None))
+
+    V = g.vector
+
+    def isap(x):
+        return isinstance(x, tuple)
+
+    def ts(out, in0, s1, op0, s2=None, op1=None):
+        x1 = ap(s1) if isap(s1) else s1
+        x2 = ap(s2) if isap(s2) else s2
+        rd = [in0] + [s for s in (s1, s2) if isap(s)]
+        if op1 is None:
+            op("v", lambda: V.tensor_scalar(ap(out), ap(in0), x1, None, op0), rd, [out])
+        else:
+            op("v", lambda: V.tensor_scalar(ap(out), ap(in0), x1, x2, op0, op1), rd, [out])
+
+    def tt(out, in0, in1, o, off=None):
+        a0 = ap(in0) if off is None else ap(in0).indirect(ap(off))
+        op("v", lambda: V.tensor_tensor(ap(out), a0, ap(in1), o), [in0, in1] + ([off] if off else []), [out])
+
+    def cp(out, in_):
+        op("v", lambda: V.tensor_copy(ap(out), ap(in_)), [in_], [out])
+
+    def scatter(win, off, in_):
+        op("v", lambda: V.tensor_copy(ap(win).indirect(ap(off)), ap(in_)), [in_, off], [win])
+
+    def pick(oq, os_, q, s, off):
+        op("v", lambda: V.tensor_copy(ap(oq).bitcast(dt.uint32), ap(q).bitcast(dt.uint32).indirect(ap(off))), [q, off], [oq])
+        op("s", lambda: g.scalar.activation(ap(os_), ap(s).indirect(ap(off)), ACT.Copy), [s, off], [os_])
+
+    def scan(out, d0, d1, o0, o1):
+        op("v", lambda: V.tensor_tensor_scan(ap(out), ap(d0), ap(d1), 0.0, o0, o1), [d0, d1], [out])
+
+    def fill(a, c):
+        op("v", lambda: V.memset(ap(a), c), [], [a])
+
+    def quant(q, s, in_):
+        op("v", lambda: V.quantize_mx(ap(q), ap(s), ap(in_)), [in_], [q, s])
+
+    def act(out, in_, f, off=None, acc=None, bias=None, scale=None):
+        a0 = ap(in_) if off is None else ap(in_).indirect(ap(off))
+        kw, rd = {}, [in_] + ([off] if off else [])
+        if acc is not None:
+            kw["accum_out"] = ap(acc)
+        if bias is not None:
+            kw["bias"] = ap(bias) if isap(bias) else bias
+            rd += [bias] if isap(bias) else []
+        if scale is not None:
+            kw["scale"] = scale
+        op("s", lambda: g.scalar.activation(ap(out), a0, f, **kw), rd, [out] + ([acc] if acc else []))
+
+    def mm(out, lq, ls, rq, rs_, start=True, stop=True):
+        op("t", lambda: g.tensor.matmul_mx(ap(out), ap(lq), ap(ls), ap(rq), ap(rs_), start, stop), [lq, ls, rq, rs_], [out], acc=not start)
+
+    def iota(out, pattern, base, cm=0):
+        if SCRATCH[out[0]][2] == I32:
+            op("g", lambda: g.iota(ap(out), pattern, base, cm), [], [out])
+        else:
+            op("g", lambda: g.iota(ap(out), pattern, base, cm, allow_small_or_imprecise_dtypes=True), [], [out])
+
+    def u8(a):
+        return ap(a).bitcast(dt.uint8) if SCRATCH[a[0]][2] == X4 else ap(a)
+
+    def send(dst, out, in_, sem):
+        def fn():
+            rid, pid, se = topo.addr(dst)
+            g.remote_dma(u8(out), u8(in_), T.sem[sem], T.sem.loc, pid, rid, topo.mask(core, dst))
+            return len(topo.engines(core, dst))
+        op("g", fn, [in_], [], sem="remote")
+
+    peer = [T.cores[rank ^ STEP[t]] for t in range(R)]
+    far, aid = far_round(rank, T, topo), helper(core, T, topo)
+
+    def send3(x, in_, shift):
+        def fn():
+            tr = []
+            for t in range(R):
+                dst, out, sem = (aid, "ru" + x, "ru") if t == far else (peer[t], "ul%s%d" % (x, t), "au%d" % t)
+                es = topo.engines(core, dst)[4 * (t + shift):4 * (t + shift) + 4]
+                rid, pid, se = topo.addr(dst)
+                tr.append(RemoteDMATransfer(dst_ids=[DstId(rid=rid, pnc=pid)], dma_engine_mask=sum(1 << e for e in es),
+                                            remote_sem=T.sem[sem], src=u8(in_), dst=u8(A(out))))
+            g.remote_dma_fused(tr, local_sem=T.sem.loc)
+            return 4 * R
+        op("g", fn, [in_], [], sem="remote")
+
+    for t in range(R):
+        ne = len(topo.engines(peer[t], core))
+        nh = len(topo.engines(helper(peer[t], T, topo), core)) if t == far else 0
+        arrive("au%d" % t, 2 * nh if nh else 8, [A("ulq%d" % t), A("uls%d" % t)])
+        arrive("at%d" % t, 2 * ne + 2 * nh, [A("lq%d" % t), A("ls%d" % t)])
+        arrive("al%d" % t, ne, [A("al%d" % t)])
+        arrive("af%d" % t, ne, [A("af%d" % t)])
+
+    op("s", lambda: [g.scalar.dma_start(ap(A("ut")), T.u[:])], [], [A("ut")], sem="du")
+    op("y", lambda: [g.sync.dma_start(ap(A("tt")), T.x[:])], [], [A("tt")], sem="dx")
+    fill(A("zero"), 0.0)
+    blank = [A("et")]
+    for name, tiles, ln, inb in (("c1", TILES1, LEN1, (0, 256)), ("c2", TILES2, LEN2, (48, 272))):
+        at = 0
+        for w, slots in tiles:
+            lo = min(ln[m] for m in slots if m is not None) if len(slots) == 4 else 0
+            if lo < w:
+                blank.append(A(name, 4 * (at + lo), 4 * (at + w)))
+            if None in slots and inb[0] > 0:
+                blank.append(A(name, 4 * at, 4 * (at + inb[0])))
+            at += w
+    op("y", lambda: [g.sync.dma_start(ap(a), ap(A("zero", 0, a[2] - a[1]))) for a in blank], [A("zero")], blank, sem="dz")
+    op("y", lambda: [g.sync.dma_start(u8(A("wq")), T.wc[:]), g.sync.dma_start(ap(A("wp")), T.ws[:])], [], [A("wq"), A("wp")], sem="dw")
+    op("y", lambda: [g.sync.dma_start(ap(A("vt")), T.v[:])], [], [A("vt")], sem="dv")
+
+    iota(col("pcol", 0), [[0, 1]], 0, 1)
+    iota(A("gi"), [[1, 8], [0, 16]], 0)
+    iota(A("rr"), [[0, 23], [1, 16]], 0)
+    iota(A("l32", 0, 8), [[16, 8]], 0)
+    iota(A("l32", 8, 16), [[1, 8]], 0)
+    kc, gc_, pc, fin, fin0, finr, nk, m15 = (col("fcol", j) for j in range(8))
+    ts(col("pcol", 1), col("pcol", 0), 15, ALU.bitwise_and)
+    ts(col("pcol", 2), col("pcol", 0), 4, ALU.arith_shift_right)
+    ts(col("pcol", 3), col("pcol", 0), 7, ALU.bitwise_and)
+    cp(pc, col("pcol", 0))
+    cp(A("fcol", 0, 2), A("pcol", 1, 3))
+    ts(col("l16", 16), col("pcol", 3), 16.0, ALU.mult)
+    ts(nk, kc, -1.0, ALU.mult)
+    for j in (3, 0, 1, 2, 4, 5, 6):
+        ts(A("wt", 512 * (j // 4) + j % 4, 512 * (j // 4 + 1), 4), A("gi"), gc_, ALU.is_equal)
+    fill(A("rsum"), 0.0)
+    fill(A("ss", 96, 112), -1e29)
+    ts(fin, kc, -1.0, ALU.mult, 2 * SMALL, ALU.add)
+    ts(finr, kc, C - 1 - 2 * SMALL, ALU.add)
+    ts(A("oh"), A("rr", 0, 256), kc, ALU.is_equal)
+    cp(A("l16", 0, 16), A("l32", 0, 16))
+    op("g", lambda: g.affine_select(ap(A("wt", 515, 1024, 4)), ap(A("wt", 3, 512, 4)), [[1, 128]], ALU.is_gt, 0.0, 0, -1),
+       [A("wt", 3, 512, 4)], [A("wt", 515, 1024, 4)])
+    iota(A("crow", 0, 16), [[16, 16]], 15)
+    iota(A("cidx"), [[1, 256]], 0)
+    act(A("rs"), A("rr", 0, 256), ACT.Sign)
+    act(A("sg"), A("rr"), ACT.Sign, bias=nk)
+    act(A("sq"), A("sg"), ACT.Square, scale=4.0, bias=-1.0)
+    quant(A("wcq"), A("wcs"), A("wt"))
+    quant(A("uq"), A("us"), A("ut"))
+    pick(A("urq"), A("urs"), A("uq"), A("us"), A("l16", 0, 8))
+    quant(A("tq0"), A("ts0"), A("tt"))
+
+    def count_ranks(src, tiles, ln, inb, cn, cmp, cmp_in, scal, at0, nb, nscan, ps, tail):
+        c, jk, cq, cs = "c" + cn, "j" + cn, "cq" + cn, "cs" + cn
+        later, at = [], 0
+        for ti, (w, slots) in enumerate(tiles):
+            for t, m in enumerate(slots):
+                if m is None:
+                    v = A(c, 4 * (at + inb[0]) + t, 4 * (at + inb[1]), 4)
+                    tt(v, (src, inb[0], inb[1], 1), A("hh", inb[0], inb[1]), cmp_in)
+                    n = inb[1] - inb[0]
+
+                    def inside(v=v, n=n):
+                        scan(A("ir", 0, n), v, A("gm", 0, n), ALU.add, ALU.mult)
+
+                    def inside2(n=n):
+                        b0 = at0 + inb[0] // 16
+                        tt(A("bb", b0, b0 + n // 16), A("cb", b0, b0 + n // 16), A("ir", 15, n, 16), ALU.subtract)
+                    new = [inside, inside2]
+                else:
+                    v = A(c, 4 * at + t, 4 * (at + ln[m]), 4)
+                    ts(v, (src, 0, ln[m], 1), scal(m), cmp)
+                    act((jk,) + v[1:], v, ACT.Copy, acc=col("rsum", at0 + m))
+                    new = []
+                if later:
+                    later.pop(0)()
+                later.extend(new)
+
+            def close(ti=ti, at=at, w=w, k=128 * (None in slots)):
+                quant(A(cq, at, at + w), A(cs, at, at + w), A(c, 4 * at, 4 * (at + w)))
+                mm(A(ps, 0, w), A("wcq", k, k + 128), A("wcs", k, k + 128), A(cq, at, at + w), A(cs, at, at + w), ti == 0, ti == len(tiles) - 1)
+            later.insert(0, close)
+            at += w
+        for f in later:
+            f()
+        tail()
+        tt(A("md", 15, 16 * nb, 16), A("bb", at0, at0 + nb), A("rsum", at0, at0 + nb), ALU.subtract)
+        scan(A("sc", 0, nscan), A(ps, 0, nscan), A("md", 0, nscan), ALU.max, ALU.add)
+
+    for t in range(R):
+        tq, tsc, lq, ls = A("tq%d" % t), A("ts%d" % t), A("lq%d" % t), A("ls%d" % t)
+        ol, al, of, af = A("ol%d" % t), A("al%d" % t), A("of%d" % t), A("af%d" % t)
+        up = (A("upq%d" % t), A("ups%d" % t))
+
+        def partner_u():
+            pick(up[0], up[1], A("ulq%d" % t), A("uls%d" % t), A("l16", 8, 16))
+
+        def lists_of_a():
+            for b in range(4):
+                ts(A("o4", 6 * b, 6 * b + 6), ol, 4.0, ALU.mult, float(b), ALU.add)
+
+        mm(A("ps2", 0, C), A("urq"), A("urs"), tq, tsc)
+        mm(A("ps3", 0, C), A("urq"), A("urs"), tq, tsc)
+        if t == 0:
+            pick(A("ucq"), A("ucs"), A("uq"), A("us"), A("l16", 16, 17))
+            act(A("gm"), A("sg", 0, 256), ACT.Relu)
+            act(A("md", 0, 368), A("sq"), ACT.Identity, scale=-SMALL / 8, bias=9 * SMALL / 8)
+            send3("q", A("ucq", 0, 8), 0)
+            send3("s", A("ucs", 0, 8), 1)
+        else:
+            partner_u()
+        if t == far:
+            send(peer[t], half(lq[0], 1), half(tq[0], 1), "at%d" % t)
+            send(peer[t], half(ls[0], 1), half(tsc[0], 1), "at%d" % t)
+        else:
+            send(peer[t], lq, tq, "at%d" % t)
+            send(peer[t], ls, tsc, "at%d" % t)
+        act(A("ssb"), A("ps3", 0, C), ACT.Copy)
+        tt(A("xm", 0, C), A("ps2", 0, C), A("oh"), ALU.mult)
+        if t == 0:
+            cp(m15, col("md", 15))
+            iota(A("p0", 0, 5), [[0, 5]], K * 128)
+            at, i = 5, K - 1
+            while i >= 0:
+                n = len([r for r in range(K) if ROWS[r] == ROWS[i]])
+                iota(A("p0", at, at + n * ROWS[i]), [[128, n], [1, ROWS[i]]], 128 * (K - 1 - i) + K - ROWS[i])
+                at, i = at + n * ROWS[i], i - n
+        scan(A("hh", 0, C), A("rs"), A("xm", 0, C), ALU.mult, ALU.add)
+        if t == 0:
+            ts(A("cb", 0, 16), A("crow", 0, 16), m15, ALU.add, -3 * SMALL, ALU.add)
+        count_ranks("ps2", TILES1, LEN1, (0, C), "1", ALU.is_lt, ALU.is_le, lambda m: col("hh", 16 * m + 15), 0, 16, C, "ps0",
+                    partner_u if t == 0 else lambda: None)
+        if t == 0:
+            act(A("mst"), A("sq", 0, 256), ACT.Identity, scale=-BIG / 8, bias=9 * BIG / 8)
+            act(A("mst", 15, 256, 16), A("mst", 15, 256, 16), ACT.Identity, bias=-3 * BIG)
+        ts(of, A("sc", 15, C, 16), -1.0, ALU.mult, finr, ALU.add)
+        send(peer[t], af, of, "af%d" % t)
+        mm(A("ps3", 0, C), up[0], up[1], lq, ls)
+        scatter(A("orep"), of, A("cidx"))
+        if t == 0:
+            for m0, m1, step, base in ((0, 3, -16, 47), (3, 18, 16, 63), (18, 20, -16, 319), (20, 23, -16, 367), (23, 29, -16, 463)):
+                iota(A("crow", 16 + m0, 16 + m1), [[step, m1 - m0]], base)
+            scan(A("sc", 0, NV), A("p0", 0, NV), A("mst", 0, NV), ALU.max, ALU.add)
+        scan(A("sc", 368, NP), A("orep", C - K, C), A("mst", 0, K), ALU.max, ALU.add)
+        if t == 0:
+            ts(A("x32", 0, 16), A("sc", 15, NV, 16), 2 * BIG, ALU.add)
+        ts(ol, A("sc", 383, NP, 16), 2 * BIG, ALU.add)
+        send(peer[t], al, ol, "al%d" % t)
+        act(A("spb"), A("ps3", 0, C), ACT.Copy)
+        act(A("ss", 0, K), A("ssb"), ACT.Copy, off=ol)
+        if t == 0:
+            ts(A("x32", 16, 32), A("x32", 0, 16), 7, ALU.arith_shift_right)
+            ts(A("x32", 32, 48), A("x32", 0, 16), 127, ALU.bitwise_and)
+            ts(A("et", 3, 515, 4), A("cidx", 0, 128), pc, ALU.is_equal)
+            cp(A("ijl"), A("x32", 16, 48))
+            ts(fin0, m15, -1.0, ALU.mult, fin, ALU.add)
+            for b in range(4):
+                quant(half("eq", b), half("es", b), A("et", 3 - b, 515 - b))
+            ts(A("cb", 16, 45), A("crow", 16, 45), m15, ALU.add, -3 * SMALL, ALU.add)
+            iota(A("nn"), [[-16384, NP]], 16384 * (NP - 1))
+        act(A("si"), A("ss"), ACT.Copy, off=A("ijl", 0, 16))
+        for b in range(4):
+            mm(A("ps%d" % (4 + b), 0, C), half("eq", b), half("es", b), lq, ls)
+        if t == 1:
+            tt(A("pk"), A("p0"), A("nn"), ALU.add)
+        if t == 2:
+            quant(A("vq"), A("vs"), A("vt"))
+        scatter(A("ee"), af, A("spb"))
+        if t == 0:
+            cp(A("bb", 16, 45), A("cb", 16, 45))
+        tt(A("xm", 368, NP), A("ee", C - K, C), A("oh", 0, K), ALU.mult)
+        at = 368
+        for i in range(1, K):
+            lo = max(at - ROWS[i], NV)
+            if lo < at:
+                act(A("vv", lo, at), A("ee", C - (at - lo), C), ACT.Identity, bias=col("ss", K - 1 - i))
+            at -= ROWS[i]
+        tt(A("vv", 0, NV), A("ee", C - K, C), A("si"), ALU.add, off=A("ijl", 16, 32))
+        scan(A("hh", 368, NP), A("rs", 0, K), A("xm", 368, NP), ALU.mult, ALU.add)
+        tt(A("xm", 48, 272), A("vv", 48, 272), A("oh", 0, 224), ALU.mult)
+        ts(A("dg", 23, 29), A("hh", 383, NP, 16), col("ss", K - 1), ALU.add)
+        for i, m0, m1 in ((1, 20, 23), (2, 18, 20), (3, 17, 18)):
+            act(A("dg", m0, m1), A("hh", NP - 1 - 16 * (m1 - m0 - 1), NP, 16), ACT.Identity, bias=col("ss", K - 1 - i))
+        scan(A("hh", 48, 272), A("rs", 0, 224), A("xm", 48, 272), ALU.mult, ALU.add)
+        act(half("dp", 0, C), A("ps4", 0, C), ACT.Copy, scale=0.5)
+        count_ranks("vv", TILES2, LEN2, (48, 272), "2", ALU.is_le, ALU.is_lt,
+                    lambda m: col("dg", m) if m >= 17 else col("hh", 16 * m + 15), 16, 29, 368, "ps1", lists_of_a)
+        ts(A("off2", 23, 29), A("md", 383, NP, 16), fin0, ALU.add, SMALL, ALU.add)
+        ts(A("off2", 0, 23), A("sc", 15, 368, 16), fin, ALU.add)
+        for b in range(1, 4):
+            act(half("dp", b, C), A("ps%d" % (4 + b), 0, C), ACT.Copy, scale=0.5)
+        act(A("ap"), A("tt"), ACT.Copy, off=A("o4"), scale=0.5)
+        for b in range(4):
+            act(half("ep", b, K), half("dp", b, C), ACT.Copy, off=al)
+        scatter(A("prep"), A("off2", 0, 29), A("pk" if t == R - 1 else "p0"))
+        scan(A("sc", 0, C), A("prep", 0, C), A("mst"), ALU.max, ALU.add)
+        ts(A("x32", 0, 16), A("sc", 15, C, 16), 2 * BIG, ALU.add)
+        ts(A("x32", 16, 32), A("x32", 0, 16), 7, ALU.arith_shift_right, 127, ALU.bitwise_and)
+        ts(A("x32", 32, 48), A("x32", 0, 16), 127, ALU.bitwise_and)
+        cp(A("il"), A("x32", 16, 32))
+        cp(A("jl"), A("x32", 32, 48))
+        nq, ns = ("tq%d" % (t + 1), "ts%d" % (t + 1)) if t < R - 1 else ("fq", "fs")
+
+        def layer(h):
+            quant(half("zq", h), half("zs", h), half("zz", h, 512))
+            for b in range(4):
+                mm(A("ps%d" % (4 * (1 - h) + b), 0, 128), half("wq", b), half("wp", b), half("zq", h), half("zs", h))
+
+        def state(h):
+            quant(half(nq, h), half(ns, h), half("tt", h, 512))
+            if t + 1 == far and h == 0:
+                send(aid, A("rtq"), half(nq, 0), "rt")
+                send(aid, A("rts"), half(ns, 0), "rt")
+            if t == R - 1:
+                mm(A("ps%d" % (4 + h), 0, 128), A("vq"), A("vs"), half(nq, h), half(ns, h))
+                op("y", lambda: [g.sync.dma_start(T.oc[:, 512 * h:512 * h + 512], u8(half(nq, h)))], [half(nq, h)], [], sem="dq" if h else "dr")
+
+        for k in range(8):
+            h, b = k // 4, k % 4
+            act(half("ag", k), half("ap", b, K), ACT.Copy, off=half("il", h, 8))
+            tt(A("zz", 512 * h + b, 512 * h + 512, 4), half("ep", b, K), half("ag", k), ALU.add, off=half("jl", h, 8))
+            if k == 4:
+                layer(0)
+        for k in range(8):
+            h, b = k // 4, k % 4
+            if k == 0:
+                layer(1)
+            act(half("rl", k), A("ps%d" % (4 * (1 - h) + b), 0, 128), ACT.Relu, scale=0.03125)
+            tt(A("tt", 512 * h + b, 512 * h + 512, 4), half("rl", k), A("zz", 512 * h + b, 512 * h + 512, 4), ALU.add)
+            if k == 4:
+                state(0)
+        if t == R - 1:
+            act(half("nb", 0, C), A("prep", 0, C), ACT.Identity, scale=1.0 / 16384, bias=-0.375)
+            act(half("ysb", 0), A("ps4", 0, 128), ACT.Copy)
+            op("s", lambda: [g.scalar.dma_start(T.y[:, 0:128], ap(half("ysb", 0)))], [half("ysb", 0)], [], sem="dy")
+        state(1)
+
+    cp(half("ysb", 1), A("ps5", 0, 128))
+    act(half("nb", 1, C), half("nb", 0, C), ACT.Identity, bias=1.5 * BIG)
+    act(half("nb", 2, C), half("nb", 1, C), ACT.Identity, bias=-1.5 * BIG)
+    op("y", lambda: [g.sync.dma_start(T.osc[4 * k:4 * k + 4, :], T.fs[32 * k:32 * k + 4, :]) for k in range(4)], [A("fs")], [], sem="dq")
+    op("s", lambda: [g.scalar.dma_start(T.y[:, 128:256], ap(half("ysb", 1))), g.scalar.dma_start(T.ol[:], T.nb[0:128:16, 2 * C:3 * C])],
+       [half("ysb", 1), half("nb", 2, C)], [], sem="dy")
+    for s in count:
+        g.wait_ge(T.sem[s], count[s])

@@ -9,13 +9,18 @@ NV = 256
 F32, BF, I32, U16, X4, U8 = "float32", "bfloat16", "int32", "uint16", "float8_e4m3fn_x4", "uint8"
 BIG, SMALL = float(2 ** 23), 4096.0
 
-LEN2 = {m: 16 * m for m in range(3, 18)}
-LEN2.update({18: 288, 19: 288, 20: 320, 21: 320, 22: 320})
+SPARE = NP - sum(ROWS)
+LEN2 = {m: 16 * m for m in range(3, 17)}
+LEN2.update({17: 264, 18: 288, 19: 288, 20: 320, 21: 320, 22: 320})
 LEN2.update({m: 368 for m in range(23, 29)})
-TILES1 = [(256, [15, 14, 13, None]), (192, [12, 11, 10, 9]), (128, [8, 7, 6, 5]), (128, [4, 3, 2, 1])]
-TILES2 = [(368, [28, 27, 26, 25]), (368, [24, 23, 22, 21]), (320, [20, 19, 18, 17]), (272, [16, 15, 14, None]),
-          (208, [13, 12, 11, 10]), (144, [9, 8, 7, 6]), (128, [5, 4, 3])]
+TILES1 = [(128, [1, 2, 3, 4]), (128, [5, 6, 7, 8]), (192, [9, 10, 11, 12]), (256, [13, 14, 15, None])]
+TILES2 = [(128, [3, 4, 5]), (144, [6, 7, 8, 9]), (208, [10, 11, 12, 13]), (272, [14, 15, 16, None]),
+          (320, [17, 18, 19, 20]), (368, [21, 22, 23, 24]), (368, [25, 26, 27, 28])]
 LEN1 = {m: 16 * m for m in range(1, 16)}
+T0, T1, T2, T3, T4, T5, T6 = [("tile", k) for k in range(7)]
+ORDER1 = [-7, -6, 5, 4, 3, "mask", 2, "carry", 1, 15, 14, 13, "in", 12, T3, 11, 10, 9, 8, T0, "row", T2, "base", T1, "partner", "sum"]
+ORDER2 = [-28, "rows", 27, "carry", 26, 25, 24, T6, 23, 22, 21, 20, T5, 19, 18, 17, 16, T4, 15, 14, 13, 12, 11, 10, 9, T2, 8, 7, 6, 5, T1,
+          4, 3, "in", T0, "row", T3, "base", "sum"]
 W1 = sum(w for w, s in TILES1)
 W2 = sum(w for w, s in TILES2)
 
@@ -48,7 +53,7 @@ for _t in range(R):
 for _t in range(8):
     SCRATCH["ps%d" % _t] = ("psum", [128, 512], F32)
 
-SEMAPHORES = (["qv", "qs", "qt", "qg", "dx", "du", "dv", "dw", "dz", "dq", "dr", "dy", "loc", "ru", "rt"]
+SEMAPHORES = (["qv", "qs", "qt", "qg", "dx0", "dx1", "du", "dv", "dw", "dz", "dq", "dr", "dy", "loc", "ru", "rt"]
               + ["%s%d" % (a, t) for a in ("au", "at", "al", "af") for t in range(R)])
 
 
@@ -186,8 +191,8 @@ def rank_program(g, core, T, topo):
         op("v", lambda: V.tensor_copy(ap(oq).bitcast(dt.uint32), ap(q).bitcast(dt.uint32).indirect(ap(off))), [q, off], [oq])
         op("s", lambda: g.scalar.activation(ap(os_), ap(s).indirect(ap(off)), ACT.Copy), [s, off], [os_])
 
-    def scan(out, d0, d1, o0, o1):
-        op("v", lambda: V.tensor_tensor_scan(ap(out), ap(d0), ap(d1), 0.0, o0, o1), [d0, d1], [out])
+    def scan(out, d0, d1, o0, o1, first=0.0):
+        op("v", lambda: V.tensor_tensor_scan(ap(out), ap(d0), ap(d1), first, o0, o1), [d0, d1], [out])
 
     def fill(a, c):
         op("v", lambda: V.memset(ap(a), c), [], [a])
@@ -251,19 +256,23 @@ def rank_program(g, core, T, topo):
         arrive("af%d" % t, ne, [A("af%d" % t)])
 
     op("s", lambda: [g.scalar.dma_start(ap(A("ut")), T.u[:])], [], [A("ut")], sem="du")
-    op("y", lambda: [g.sync.dma_start(ap(A("tt")), T.x[:])], [], [A("tt")], sem="dx")
+    for h in range(2):
+        op("y", lambda: [g.sync.dma_start(ap(half("tt", h, 512)), T.x[:, 512 * h:512 * h + 512])], [], [half("tt", h, 512)], sem="dx%d" % h)
     fill(A("zero"), 0.0)
-    blank = [A("et")]
-    for name, tiles, ln, inb in (("c1", TILES1, LEN1, (0, 256)), ("c2", TILES2, LEN2, (48, 272))):
+    blank = {"c1": [], "c2": [A("et")]}
+    for name, tiles, ln, first, inb in (("c1", TILES1, LEN1, 0, 0), ("c2", TILES2, LEN2, SPARE, 48)):
         at = 0
         for w, slots in tiles:
             lo = min(ln[m] for m in slots if m is not None) if len(slots) == 4 else 0
             if lo < w:
-                blank.append(A(name, 4 * (at + lo), 4 * (at + w)))
-            if None in slots and inb[0] > 0:
-                blank.append(A(name, 4 * at, 4 * (at + inb[0])))
+                blank[name].append(A(name, 4 * (at + lo), 4 * (at + w)))
+            head = inb if None in slots else first
+            if head and lo:
+                blank[name].append(A(name, 4 * at, 4 * (at + head)))
             at += w
-    op("y", lambda: [g.sync.dma_start(ap(a), ap(A("zero", 0, a[2] - a[1]))) for a in blank], [A("zero")], blank, sem="dz")
+    for a in blank["c1"]:
+        act(a, A("zero", 0, a[2] - a[1]), ACT.Copy)
+    op("y", lambda: [g.sync.dma_start(ap(a), ap(A("zero", 0, a[2] - a[1]))) for a in blank["c2"]], [A("zero")], blank["c2"], sem="dz")
     op("y", lambda: [g.sync.dma_start(u8(A("wq")), T.wc[:]), g.sync.dma_start(ap(A("wp")), T.ws[:])], [], [A("wq"), A("wp")], sem="dw")
     op("y", lambda: [g.sync.dma_start(ap(A("vt")), T.v[:])], [], [A("vt")], sem="dv")
 
@@ -284,7 +293,7 @@ def rank_program(g, core, T, topo):
         ts(A("wt", 512 * (j // 4) + j % 4, 512 * (j // 4 + 1), 4), A("gi"), gc_, ALU.is_equal)
     fill(A("rsum"), 0.0)
     fill(A("ss", 96, 112), -1e29)
-    ts(fin, kc, -1.0, ALU.mult, 2 * SMALL, ALU.add)
+    ts(fin, kc, -1.0, ALU.mult, -2 * SMALL, ALU.add)
     ts(finr, kc, C - 1 - 2 * SMALL, ALU.add)
     ts(A("oh"), A("rr", 0, 256), kc, ALU.is_equal)
     cp(A("l16", 0, 16), A("l32", 0, 16))
@@ -295,47 +304,68 @@ def rank_program(g, core, T, topo):
     act(A("rs"), A("rr", 0, 256), ACT.Sign)
     act(A("sg"), A("rr"), ACT.Sign, bias=nk)
     act(A("sq"), A("sg"), ACT.Square, scale=4.0, bias=-1.0)
-    quant(A("wcq"), A("wcs"), A("wt"))
     quant(A("uq"), A("us"), A("ut"))
     pick(A("urq"), A("urs"), A("uq"), A("us"), A("l16", 0, 8))
-    quant(A("tq0"), A("ts0"), A("tt"))
+    pick(A("ucq"), A("ucs"), A("uq"), A("us"), A("l16", 16, 17))
+    send3("q", A("ucq", 0, 8), 0)
+    send3("s", A("ucs", 0, 8), 1)
+    act(A("gm"), A("sg", 0, 256), ACT.Relu)
+    act(A("md", 0, 368), A("sq"), ACT.Identity, scale=-SMALL / 8, bias=9 * SMALL / 8)
 
-    def count_ranks(src, tiles, ln, inb, cn, cmp, cmp_in, scal, at0, nb, nscan, ps, tail):
+    def counting(src, tiles, ln, lo, inb, cn, cmp, cmp_in, sign, scal, at0, nb, ps):
         c, jk, cq, cs = "c" + cn, "j" + cn, "cq" + cn, "cs" + cn
-        later, at = [], 0
-        for ti, (w, slots) in enumerate(tiles):
-            for t, m in enumerate(slots):
-                if m is None:
-                    v = A(c, 4 * (at + inb[0]) + t, 4 * (at + inb[1]), 4)
-                    tt(v, (src, inb[0], inb[1], 1), A("hh", inb[0], inb[1]), cmp_in)
-                    n = inb[1] - inb[0]
+        start = [sum(w for w, s in tiles[:k]) for k in range(len(tiles))]
+        slot = {m: (start[k], i) for k, (w, s) in enumerate(tiles) for i, m in enumerate(s)}
+        closes = [x for x in (ORDER1 if cn == "1" else ORDER2) if isinstance(x, tuple)]
+        n, b0 = inb[1] - inb[0], at0 + inb[0] // 16
+        inside = A(c, 4 * (slot[None][0] + inb[0]) + slot[None][1], 4 * (slot[None][0] + inb[1]), 4)
 
-                    def inside(v=v, n=n):
-                        scan(A("ir", 0, n), v, A("gm", 0, n), ALU.add, ALU.mult)
-
-                    def inside2(n=n):
-                        b0 = at0 + inb[0] // 16
-                        tt(A("bb", b0, b0 + n // 16), A("cb", b0, b0 + n // 16), A("ir", 15, n, 16), ALU.subtract)
-                    new = [inside, inside2]
-                else:
-                    v = A(c, 4 * at + t, 4 * (at + ln[m]), 4)
-                    ts(v, (src, 0, ln[m], 1), scal(m), cmp)
-                    act((jk,) + v[1:], v, ACT.Copy, acc=col("rsum", at0 + m))
-                    new = []
-                if later:
-                    later.pop(0)()
-                later.extend(new)
-
-            def close(ti=ti, at=at, w=w, k=128 * (None in slots)):
+        def step(x):
+            if x == "in":
+                tt(inside, (src("v", None), inb[0], inb[1], 1), A("hh", inb[0], inb[1]), cmp_in)
+            elif x == "row":
+                scan(A("ir", 0, n), inside, A("gm", 0, n), ALU.add, ALU.mult)
+            elif x == "base":
+                tt(A("bb", b0, b0 + n // 16), A("cb", b0, b0 + n // 16), A("ir", 15, n, 16), ALU.subtract)
+            elif x == "sum":
+                tt(A("md", 15, 16 * nb, 16), A("bb", at0, at0 + nb), A("rsum", at0, at0 + nb), ALU.subtract)
+            elif isinstance(x, tuple):
+                k = x[1]
+                at, w, z = start[k], tiles[k][0], 128 * (None in tiles[k][1])
                 quant(A(cq, at, at + w), A(cs, at, at + w), A(c, 4 * at, 4 * (at + w)))
-                mm(A(ps, 0, w), A("wcq", k, k + 128), A("wcs", k, k + 128), A(cq, at, at + w), A(cs, at, at + w), ti == 0, ti == len(tiles) - 1)
-            later.insert(0, close)
-            at += w
-        for f in later:
-            f()
-        tail()
-        tt(A("md", 15, 16 * nb, 16), A("bb", at0, at0 + nb), A("rsum", at0, at0 + nb), ALU.subtract)
-        scan(A("sc", 0, nscan), A(ps, 0, nscan), A("md", 0, nscan), ALU.max, ALU.add)
+                mm(A(ps, 0, w), A("wcq", z, z + 128), A("wcs", z, z + 128), A(cq, at, at + w), A(cs, at, at + w), x == closes[0], x == closes[-1])
+            else:
+                m = abs(x)
+                at, i = slot[m]
+                v = A(c, 4 * (at + lo) + i, 4 * (at + ln[m]), 4)
+                if x < 0:
+                    act((jk,) + v[1:], (src("s", m), lo, ln[m], 1), ACT.Sign, scale=-1.0, bias=scal(m))
+                    act(v, (jk,) + v[1:], ACT.Relu, scale=sign, acc=col("rsum", at0 + m))
+                else:
+                    ts(v, (src("v", m), lo, ln[m], 1), scal(m), cmp)
+                    act((jk,) + v[1:], v, ACT.Copy, acc=col("rsum", at0 + m))
+        return step
+
+    order1 = counting(lambda q, m: ("ps4" if q == "v" else "ps5") if m is not None and m <= 8 else ("ps2" if q == "v" else "ps3"),
+                      TILES1, LEN1, 0, (0, C), "1", ALU.is_lt, ALU.is_le, 1.0, lambda m: col("hh", 16 * m + 15), 0, 16, "ps0")
+    order2 = counting(lambda q, m: "vv", TILES2, LEN2, SPARE, (48, 272), "2", ALU.is_gt, ALU.is_ge, -1.0,
+                      lambda m: col("dg", m) if m >= 17 else col("hh", 16 * m + 15), 16, 29, "ps1")
+
+    def scores(t, h):
+        for b in (4, 5) if h == 0 else (2, 3):
+            mm(A("ps%d" % b, 0, 128 * (h + 1)), A("urq"), A("urs"), A("tq%d" % t, 0, 128 * (h + 1)), A("ts%d" % t, 0, 128 * (h + 1)))
+
+    def own(h, x):
+        if x == 0:
+            tt(half("xm", h), A("ps2", 128, C) if h else A("ps4", 0, 128), A("oh", 0, 128), ALU.mult)
+        else:
+            scan(half("hh", h), A("rs", 0, 128), half("xm", h), ALU.mult, ALU.add)
+
+    quant(half("tq0", 0), half("ts0", 0), half("tt", 0, 512))
+    scores(0, 0)
+    quant(A("wcq"), A("wcs"), A("wt"))
+    own(0, 0)
+    quant(half("tq0", 1), half("ts0", 1), half("tt", 1, 512))
 
     for t in range(R):
         tq, tsc, lq, ls = A("tq%d" % t), A("ts%d" % t), A("lq%d" % t), A("ls%d" % t)
@@ -349,25 +379,27 @@ def rank_program(g, core, T, topo):
             for b in range(4):
                 ts(A("o4", 6 * b, 6 * b + 6), ol, 4.0, ALU.mult, float(b), ALU.add)
 
-        mm(A("ps2", 0, C), A("urq"), A("urs"), tq, tsc)
-        mm(A("ps3", 0, C), A("urq"), A("urs"), tq, tsc)
-        if t == 0:
-            pick(A("ucq"), A("ucs"), A("uq"), A("us"), A("l16", 16, 17))
-            act(A("gm"), A("sg", 0, 256), ACT.Relu)
-            act(A("md", 0, 368), A("sq"), ACT.Identity, scale=-SMALL / 8, bias=9 * SMALL / 8)
-            send3("q", A("ucq", 0, 8), 0)
-            send3("s", A("ucs", 0, 8), 1)
-        else:
-            partner_u()
+        def unpack():
+            for b in range(4):
+                mm(A("ps%d" % (4 + b), 0, C), half("eq", b), half("es", b), lq, ls)
+
+        def halve():
+            for b in range(4):
+                act(half("dp", b, C), A("ps%d" % (4 + b), 0, C), ACT.Copy, scale=0.5)
+
+        def run(steps, one, more):
+            for x in steps:
+                more[x]() if x in more else one(x)
+
+        scores(t, 1)
         if t == far:
             send(peer[t], half(lq[0], 1), half(tq[0], 1), "at%d" % t)
             send(peer[t], half(ls[0], 1), half(tsc[0], 1), "at%d" % t)
         else:
             send(peer[t], lq, tq, "at%d" % t)
             send(peer[t], ls, tsc, "at%d" % t)
-        act(A("ssb"), A("ps3", 0, C), ACT.Copy)
-        tt(A("xm", 0, C), A("ps2", 0, C), A("oh"), ALU.mult)
         if t == 0:
+            own(0, 1)
             cp(m15, col("md", 15))
             iota(A("p0", 0, 5), [[0, 5]], K * 128)
             at, i = 5, K - 1
@@ -375,79 +407,91 @@ def rank_program(g, core, T, topo):
                 n = len([r for r in range(K) if ROWS[r] == ROWS[i]])
                 iota(A("p0", at, at + n * ROWS[i]), [[128, n], [1, ROWS[i]]], 128 * (K - 1 - i) + K - ROWS[i])
                 at, i = at + n * ROWS[i], i - n
-        scan(A("hh", 0, C), A("rs"), A("xm", 0, C), ALU.mult, ALU.add)
-        if t == 0:
             ts(A("cb", 0, 16), A("crow", 0, 16), m15, ALU.add, -3 * SMALL, ALU.add)
-        count_ranks("ps2", TILES1, LEN1, (0, C), "1", ALU.is_lt, ALU.is_le, lambda m: col("hh", 16 * m + 15), 0, 16, C, "ps0",
-                    partner_u if t == 0 else lambda: None)
+        run(ORDER1, order1, {"mask": lambda: own(1, 0), "carry": lambda: own(1, 1), "partner": partner_u})
+        scan(A("sc", 0, C), A("ps0", 0, C), A("md", 0, C), ALU.max, ALU.add)
+        mm(A("ps1", 0, C), up[0], up[1], lq, ls)
+        if t > 0:
+            unpack()
+        act(A("ssb"), A("ps3", 0, C), ACT.Copy)
         if t == 0:
             act(A("mst"), A("sq", 0, 256), ACT.Identity, scale=-BIG / 8, bias=9 * BIG / 8)
             act(A("mst", 15, 256, 16), A("mst", 15, 256, 16), ACT.Identity, bias=-3 * BIG)
         ts(of, A("sc", 15, C, 16), -1.0, ALU.mult, finr, ALU.add)
         send(peer[t], af, of, "af%d" % t)
-        mm(A("ps3", 0, C), up[0], up[1], lq, ls)
+        act(A("spb"), A("ps1", 0, C), ACT.Copy)
+        if t > 0:
+            halve()
         scatter(A("orep"), of, A("cidx"))
         if t == 0:
-            for m0, m1, step, base in ((0, 3, -16, 47), (3, 18, 16, 63), (18, 20, -16, 319), (20, 23, -16, 367), (23, 29, -16, 463)):
-                iota(A("crow", 16 + m0, 16 + m1), [[step, m1 - m0]], base)
+            iota(A("crow", 16, 45), [[16, 29]], 1 - NP)
             scan(A("sc", 0, NV), A("p0", 0, NV), A("mst", 0, NV), ALU.max, ALU.add)
         scan(A("sc", 368, NP), A("orep", C - K, C), A("mst", 0, K), ALU.max, ALU.add)
         if t == 0:
             ts(A("x32", 0, 16), A("sc", 15, NV, 16), 2 * BIG, ALU.add)
         ts(ol, A("sc", 383, NP, 16), 2 * BIG, ALU.add)
         send(peer[t], al, ol, "al%d" % t)
-        act(A("spb"), A("ps3", 0, C), ACT.Copy)
         act(A("ss", 0, K), A("ssb"), ACT.Copy, off=ol)
         if t == 0:
             ts(A("x32", 16, 32), A("x32", 0, 16), 7, ALU.arith_shift_right)
             ts(A("x32", 32, 48), A("x32", 0, 16), 127, ALU.bitwise_and)
             ts(A("et", 3, 515, 4), A("cidx", 0, 128), pc, ALU.is_equal)
             cp(A("ijl"), A("x32", 16, 48))
-            ts(fin0, m15, -1.0, ALU.mult, fin, ALU.add)
+            ts(fin0, m15, -SMALL, ALU.add, fin, ALU.add)
+            ts(A("cb", 16, 45), A("crow", 16, 45), m15, ALU.add, -3 * SMALL, ALU.add)
             for b in range(4):
                 quant(half("eq", b), half("es", b), A("et", 3 - b, 515 - b))
-            ts(A("cb", 16, 45), A("crow", 16, 45), m15, ALU.add, -3 * SMALL, ALU.add)
+            ts(A("cb", 19, 33), A("cb", 19, 33), nk, ALU.add, 15.0, ALU.add)
+            cp(A("bb", 16, 45), A("cb", 16, 45))
+            ts(A("cb", 19, 33), A("cb", 19, 33), nk, ALU.add)
             iota(A("nn"), [[-16384, NP]], 16384 * (NP - 1))
+            unpack()
+        lists_of_a()
         act(A("si"), A("ss"), ACT.Copy, off=A("ijl", 0, 16))
-        for b in range(4):
-            mm(A("ps%d" % (4 + b), 0, C), half("eq", b), half("es", b), lq, ls)
+        act(A("ap"), A("tt"), ACT.Copy, off=A("o4"), scale=0.5)
         if t == 1:
-            tt(A("pk"), A("p0"), A("nn"), ALU.add)
+            scan(A("pk"), A("nn"), A("p0"), ALU.min, ALU.add, 2 * BIG)
         if t == 2:
             quant(A("vq"), A("vs"), A("vt"))
         scatter(A("ee"), af, A("spb"))
-        if t == 0:
-            cp(A("bb", 16, 45), A("cb", 16, 45))
         tt(A("xm", 368, NP), A("ee", C - K, C), A("oh", 0, K), ALU.mult)
         at = 368
+        rows = []
         for i in range(1, K):
             lo = max(at - ROWS[i], NV)
             if lo < at:
-                act(A("vv", lo, at), A("ee", C - (at - lo), C), ACT.Identity, bias=col("ss", K - 1 - i))
+                rows.append((lo, at, i))
             at -= ROWS[i]
+        for lo, at, i in reversed(rows):
+            act(A("vv", lo, at), A("ee", C - (at - lo), C), ACT.Identity, bias=col("ss", K - 1 - i))
         tt(A("vv", 0, NV), A("ee", C - K, C), A("si"), ALU.add, off=A("ijl", 16, 32))
         scan(A("hh", 368, NP), A("rs", 0, K), A("xm", 368, NP), ALU.mult, ALU.add)
         tt(A("xm", 48, 272), A("vv", 48, 272), A("oh", 0, 224), ALU.mult)
-        ts(A("dg", 23, 29), A("hh", 383, NP, 16), col("ss", K - 1), ALU.add)
-        for i, m0, m1 in ((1, 20, 23), (2, 18, 20), (3, 17, 18)):
-            act(A("dg", m0, m1), A("hh", NP - 1 - 16 * (m1 - m0 - 1), NP, 16), ACT.Identity, bias=col("ss", K - 1 - i))
-        scan(A("hh", 48, 272), A("rs", 0, 224), A("xm", 48, 272), ALU.mult, ALU.add)
-        act(half("dp", 0, C), A("ps4", 0, C), ACT.Copy, scale=0.5)
-        count_ranks("vv", TILES2, LEN2, (48, 272), "2", ALU.is_le, ALU.is_lt,
-                    lambda m: col("dg", m) if m >= 17 else col("hh", 16 * m + 15), 16, 29, 368, "ps1", lists_of_a)
-        ts(A("off2", 23, 29), A("md", 383, NP, 16), fin0, ALU.add, SMALL, ALU.add)
-        ts(A("off2", 0, 23), A("sc", 15, 368, 16), fin, ALU.add)
-        for b in range(1, 4):
-            act(half("dp", b, C), A("ps%d" % (4 + b), 0, C), ACT.Copy, scale=0.5)
-        act(A("ap"), A("tt"), ACT.Copy, off=A("o4"), scale=0.5)
+
+        def rows_own(which):
+            for i, m0, m1 in which:
+                act(A("dg", m0, m1), A("hh", NP - 1 - 16 * (m1 - m0 - 1), NP, 16), ACT.Identity, bias=col("ss", K - 1 - i))
+
+        rows_own([(0, 23, 29)])
+        run(ORDER2, order2, {"rows": lambda: rows_own([(1, 20, 23), (2, 18, 20), (3, 17, 18)]),
+                             "carry": lambda: scan(A("hh", 48, 272), A("rs", 0, 224), A("xm", 48, 272), ALU.mult, ALU.add)})
+        ts(A("off2", 23, 29), A("md", 383, NP, 16), -1.0, ALU.mult, fin0, ALU.add)
+        scan(A("sc", 0, 368), A("ps1", 0, 368), A("md", 0, 368), ALU.max, ALU.add)
+        ts(A("off2", 0, 23), A("sc", 15, 368, 16), -1.0, ALU.mult, fin, ALU.add)
+        if t == 0:
+            halve()
         for b in range(4):
             act(half("ep", b, K), half("dp", b, C), ACT.Copy, off=al)
         scatter(A("prep"), A("off2", 0, 29), A("pk" if t == R - 1 else "p0"))
         scan(A("sc", 0, C), A("prep", 0, C), A("mst"), ALU.max, ALU.add)
         ts(A("x32", 0, 16), A("sc", 15, C, 16), 2 * BIG, ALU.add)
-        ts(A("x32", 16, 32), A("x32", 0, 16), 7, ALU.arith_shift_right, 127, ALU.bitwise_and)
+        if t < R - 1:
+            ts(A("il"), A("sc", 15, C, 16), 2 * BIG - 48, ALU.add, 1.0 / 128, ALU.mult)
+        else:
+            ts(A("x32", 16, 32), A("x32", 0, 16), 7, ALU.arith_shift_right, 127, ALU.bitwise_and)
         ts(A("x32", 32, 48), A("x32", 0, 16), 127, ALU.bitwise_and)
-        cp(A("il"), A("x32", 16, 32))
+        if t == R - 1:
+            cp(A("il"), A("x32", 16, 32))
         cp(A("jl"), A("x32", 32, 48))
         nq, ns = ("tq%d" % (t + 1), "ts%d" % (t + 1)) if t < R - 1 else ("fq", "fs")
 
@@ -461,6 +505,8 @@ def rank_program(g, core, T, topo):
             if t + 1 == far and h == 0:
                 send(aid, A("rtq"), half(nq, 0), "rt")
                 send(aid, A("rts"), half(ns, 0), "rt")
+            if t < R - 1 and h == 0:
+                scores(t + 1, 0)
             if t == R - 1:
                 mm(A("ps%d" % (4 + h), 0, 128), A("vq"), A("vs"), half(nq, h), half(ns, h))
                 op("y", lambda: [g.sync.dma_start(T.oc[:, 512 * h:512 * h + 512], u8(half(nq, h)))], [half(nq, h)], [], sem="dq" if h else "dr")
@@ -479,10 +525,14 @@ def rank_program(g, core, T, topo):
             tt(A("tt", 512 * h + b, 512 * h + 512, 4), half("rl", k), A("zz", 512 * h + b, 512 * h + 512, 4), ALU.add)
             if k == 4:
                 state(0)
+            if k == 6 and t < R - 1:
+                own(0, 0)
         if t == R - 1:
             act(half("nb", 0, C), A("prep", 0, C), ACT.Identity, scale=1.0 / 16384, bias=-0.375)
             act(half("ysb", 0), A("ps4", 0, 128), ACT.Copy)
             op("s", lambda: [g.scalar.dma_start(T.y[:, 0:128], ap(half("ysb", 0)))], [half("ysb", 0)], [], sem="dy")
+        else:
+            own(0, 1)
         state(1)
 
     cp(half("ysb", 1), A("ps5", 0, 128))

@@ -5,7 +5,8 @@ C, K, R = 256, 96, 3
 STEP = [1, 2, 4]
 ROWS = [K // (i + 1) for i in range(K)]
 NP = 464
-NV = 256
+NV0, NV = 48, 256
+UP, UP0 = 272, 192
 F32, BF, I32, U16, X4, U8 = "float32", "bfloat16", "int32", "uint16", "float8_e4m3fn_x4", "uint8"
 BIG, SMALL = float(2 ** 23), 4096.0
 
@@ -18,9 +19,10 @@ TILES2 = [(128, [3, 4, 5]), (144, [6, 7, 8, 9]), (208, [10, 11, 12, 13]), (272, 
           (320, [17, 18, 19, 20]), (368, [21, 22, 23, 24]), (368, [25, 26, 27, 28])]
 LEN1 = {m: 16 * m for m in range(1, 16)}
 T0, T1, T2, T3, T4, T5, T6 = [("tile", k) for k in range(7)]
-ORDER1 = [-7, -6, 5, 4, 3, "mask", 2, "carry", 1, 15, 14, 13, "in", 12, T3, 11, 10, 9, 8, T0, "row", T2, "base", T1, "partner", "sum"]
-ORDER2 = [-28, "rows", 27, "carry", 26, 25, 24, T6, 23, 22, 21, 20, T5, 19, 18, 17, 16, T4, 15, 14, 13, 12, 11, 10, 9, T2, 8, 7, 6, 5, T1,
-          4, 3, "in", T0, "row", T3, "base", "sum"]
+ORDER1 = [-7, -6, 107, 106, 5, 4, 3, 2, "mask", 1, "carry", -8, 15, 108, 14, 13, "in", 12, T3, 11, 10, 9, "masks", T0, "row", T2, "base", T1,
+          "partner", "sum"]
+ORDER2 = [-28, 27, 128, "carry", -24, 26, 124, 25, 23, T6, "spare", 22, 21, 20, T5, "spare", 19, 18, 17, -16, T4, "in", 15, 116, 14, 13,
+          "up0", 12, "up1", "up2", "up3", 11, 10, 9, 8, 7, 6, 5, 4, 3, "up4", T3, T2, T1, "row", T0, "base", "spare", "sum"]
 W1 = sum(w for w, s in TILES1)
 W2 = sum(w for w, s in TILES2)
 
@@ -37,7 +39,7 @@ for _n, _w, _d in [
     ("et", 520, BF), ("eq", 512, X4), ("es", 512, U8), ("zero", 520, BF),
     ("cidx", 256, F32), ("crow", 48, F32), ("cb", 48, F32), ("bb", 48, F32), ("rsum", 48, F32), ("dg", 32, F32),
     ("p0", NP, F32), ("nn", NP, F32), ("pk", NP, F32), ("ijl", 32, U16),
-    ("c1", 4 * W1, BF), ("c2", 4 * W2, BF), ("j1", 4 * W1, BF), ("j2", 4 * W2, BF),
+    ("c1", 4 * W1, BF), ("c2", 4 * W2, BF), ("jk", 4 * W2, BF), ("pm", K, BF),
     ("cq1", W1, X4), ("cs1", W1, U8), ("cq2", W2, X4), ("cs2", W2, U8),
     ("ssb", 256, F32), ("spb", 256, F32), ("xm", NP, F32), ("hh", NP, F32), ("ir", 256, BF), ("sc", NP, F32),
     ("off2", 30, U16), ("orep", 256, F32), ("prep", NP, F32), ("o4", 24, U16),
@@ -53,7 +55,7 @@ for _t in range(R):
 for _t in range(8):
     SCRATCH["ps%d" % _t] = ("psum", [128, 512], F32)
 
-SEMAPHORES = (["qv", "qs", "qt", "qg", "dx0", "dx1", "du", "dv", "dw", "dz", "dq", "dr", "dy", "loc", "ru", "rt"]
+SEMAPHORES = (["qv", "qs", "qt", "qg", "dx0", "dx1", "du", "dv", "dw", "dz", "dq", "dr", "dy", "do", "loc", "ru", "rt"]
               + ["%s%d" % (a, t) for a in ("au", "at", "al", "af") for t in range(R)])
 
 
@@ -292,7 +294,6 @@ def rank_program(g, core, T, topo):
     for j in (3, 0, 1, 2, 4, 5, 6):
         ts(A("wt", 512 * (j // 4) + j % 4, 512 * (j // 4 + 1), 4), A("gi"), gc_, ALU.is_equal)
     fill(A("rsum"), 0.0)
-    fill(A("ss", 96, 112), -1e29)
     ts(fin, kc, -1.0, ALU.mult, -2 * SMALL, ALU.add)
     ts(finr, kc, C - 1 - 2 * SMALL, ALU.add)
     ts(A("oh"), A("rr", 0, 256), kc, ALU.is_equal)
@@ -301,19 +302,21 @@ def rank_program(g, core, T, topo):
        [A("wt", 3, 512, 4)], [A("wt", 515, 1024, 4)])
     iota(A("crow", 0, 16), [[16, 16]], 15)
     iota(A("cidx"), [[1, 256]], 0)
-    act(A("rs"), A("rr", 0, 256), ACT.Sign)
+    act(A("rs", 0, 224), A("rr", 0, 224), ACT.Sign)
     act(A("sg"), A("rr"), ACT.Sign, bias=nk)
-    act(A("sq"), A("sg"), ACT.Square, scale=4.0, bias=-1.0)
+    ts(m15, kc, 15.0, ALU.is_equal, SMALL, ALU.mult)
     quant(A("uq"), A("us"), A("ut"))
+    ts(A("cb", 0, 16), A("crow", 0, 16), m15, ALU.add, -3 * SMALL, ALU.add)
     pick(A("urq"), A("urs"), A("uq"), A("us"), A("l16", 0, 8))
     pick(A("ucq"), A("ucs"), A("uq"), A("us"), A("l16", 16, 17))
     send3("q", A("ucq", 0, 8), 0)
     send3("s", A("ucs", 0, 8), 1)
+    act(A("sq"), A("sg"), ACT.Square, scale=4.0, bias=-1.0)
     act(A("gm"), A("sg", 0, 256), ACT.Relu)
     act(A("md", 0, 368), A("sq"), ACT.Identity, scale=-SMALL / 8, bias=9 * SMALL / 8)
 
     def counting(src, tiles, ln, lo, inb, cn, cmp, cmp_in, sign, scal, at0, nb, ps):
-        c, jk, cq, cs = "c" + cn, "j" + cn, "cq" + cn, "cs" + cn
+        c, jk, cq, cs = "c" + cn, "jk", "cq" + cn, "cs" + cn
         start = [sum(w for w, s in tiles[:k]) for k in range(len(tiles))]
         slot = {m: (start[k], i) for k, (w, s) in enumerate(tiles) for i, m in enumerate(s)}
         closes = [x for x in (ORDER1 if cn == "1" else ORDER2) if isinstance(x, tuple)]
@@ -333,13 +336,19 @@ def rank_program(g, core, T, topo):
                 k = x[1]
                 at, w, z = start[k], tiles[k][0], 128 * (None in tiles[k][1])
                 quant(A(cq, at, at + w), A(cs, at, at + w), A(c, 4 * at, 4 * (at + w)))
+                if w > 16 * nb:
+                    wide = [y for y in closes if tiles[y[1]][0] > 16 * nb]
+                    mm(A("ps0", 0, w - UP0), A("wcq", 0, 128), A("wcs", 0, 128), A(cq, at + UP0, at + w), A(cs, at + UP0, at + w),
+                       x == wide[0], x == wide[-1])
+                    w = 16 * nb
                 mm(A(ps, 0, w), A("wcq", z, z + 128), A("wcs", z, z + 128), A(cq, at, at + w), A(cs, at, at + w), x == closes[0], x == closes[-1])
             else:
-                m = abs(x)
+                m = abs(x) % 100
                 at, i = slot[m]
                 v = A(c, 4 * (at + lo) + i, 4 * (at + ln[m]), 4)
                 if x < 0:
                     act((jk,) + v[1:], (src("s", m), lo, ln[m], 1), ACT.Sign, scale=-1.0, bias=scal(m))
+                elif x > 100:
                     act(v, (jk,) + v[1:], ACT.Relu, scale=sign, acc=col("rsum", at0 + m))
                 else:
                     ts(v, (src("v", m), lo, ln[m], 1), scal(m), cmp)
@@ -349,15 +358,17 @@ def rank_program(g, core, T, topo):
     order1 = counting(lambda q, m: ("ps4" if q == "v" else "ps5") if m is not None and m <= 8 else ("ps2" if q == "v" else "ps3"),
                       TILES1, LEN1, 0, (0, C), "1", ALU.is_lt, ALU.is_le, 1.0, lambda m: col("hh", 16 * m + 15), 0, 16, "ps0")
     order2 = counting(lambda q, m: "vv", TILES2, LEN2, SPARE, (48, 272), "2", ALU.is_gt, ALU.is_ge, -1.0,
-                      lambda m: col("dg", m) if m >= 17 else col("hh", 16 * m + 15), 16, 29, "ps1")
+                      lambda m: col("dg", m) if m >= 17 else col("hh", 16 * m + 15), 16, UP // 16, "ps1")
 
     def scores(t, h):
+        if h:
+            mm(A("ps6", 0, 128), A("urq"), A("urs"), half("tq%d" % t, 1), half("ts%d" % t, 1))
         for b in (4, 5) if h == 0 else (2, 3):
             mm(A("ps%d" % b, 0, 128 * (h + 1)), A("urq"), A("urs"), A("tq%d" % t, 0, 128 * (h + 1)), A("ts%d" % t, 0, 128 * (h + 1)))
 
     def own(h, x):
         if x == 0:
-            tt(half("xm", h), A("ps2", 128, C) if h else A("ps4", 0, 128), A("oh", 0, 128), ALU.mult)
+            tt(half("xm", h), A("ps6" if h else "ps4", 0, 128), A("oh", 0, 128), ALU.mult)
         else:
             scan(half("hh", h), A("rs", 0, 128), half("xm", h), ALU.mult, ALU.add)
 
@@ -400,61 +411,70 @@ def rank_program(g, core, T, topo):
             send(peer[t], ls, tsc, "at%d" % t)
         if t == 0:
             own(0, 1)
-            cp(m15, col("md", 15))
             iota(A("p0", 0, 5), [[0, 5]], K * 128)
             at, i = 5, K - 1
             while i >= 0:
                 n = len([r for r in range(K) if ROWS[r] == ROWS[i]])
                 iota(A("p0", at, at + n * ROWS[i]), [[128, n], [1, ROWS[i]]], 128 * (K - 1 - i) + K - ROWS[i])
                 at, i = at + n * ROWS[i], i - n
-            ts(A("cb", 0, 16), A("crow", 0, 16), m15, ALU.add, -3 * SMALL, ALU.add)
-        run(ORDER1, order1, {"mask": lambda: own(1, 0), "carry": lambda: own(1, 1), "partner": partner_u})
+        nv = (NV - NV0) // 16
+        aside = [] if t else [
+            lambda: ts(A("et", 3, 515, 4), A("cidx", 0, 128), pc, ALU.is_equal),
+            lambda: ts(fin0, m15, -SMALL, ALU.add, fin, ALU.add),
+            lambda: ts(A("cb", 16, 45), A("crow", 16, 45), m15, ALU.add, -3 * SMALL, ALU.add),
+            lambda: scan(A("xm", NV0, NV), A("p0", NV0, NV), A("mst", 0, NV - NV0), ALU.max, ALU.add),
+            partner_u,
+            lambda: ts(A("ijl", 0, nv), A("xm", NV0 + 15, NV, 16), 2 * BIG - 48, ALU.add, 1.0 / 128, ALU.mult),
+            lambda: ts(A("x32", 0, nv), A("xm", NV0 + 15, NV, 16), 2 * BIG, ALU.add),
+            lambda: ts(A("x32", 16, 16 + nv), A("x32", 0, nv), 127, ALU.bitwise_and),
+            lambda: cp(A("ijl", 16, 16 + nv), A("x32", 16, 16 + nv)),
+            lambda: cp(A("bb", 16, 45), A("cb", 16, 45)),
+            lambda: ts(A("cb", 19, 33), A("cb", 19, 33), nk, ALU.add, 15.0, ALU.add),
+            lambda: ts(A("cb", 19, 33), A("cb", 19, 33), nk, ALU.add),
+        ] + [lambda b=b: quant(half("eq", b), half("es", b), A("et", 3 - b, 515 - b)) for b in range(4)]
+
+        def spare(n=1):
+            for f in aside[:n]:
+                f()
+            del aside[:n]
+
+        def masks():
+            if t == 0:
+                act(A("mst"), A("sq", 0, 256), ACT.Identity, scale=-BIG / 8, bias=9 * BIG / 8)
+                act(A("mst", 15, 256, 16), A("mst", 15, 256, 16), ACT.Identity, bias=-3 * BIG)
+                act(A("pm"), A("oh", 0, K), ACT.Identity, scale=2e29, bias=-1e29)
+                iota(A("crow", 16, 45), [[16, 29]], 1 - NP)
+
+        steps = ORDER1 if t else [abs(x) if isinstance(x, int) else x for x in ORDER1 if not (isinstance(x, int) and x > 100)]
+        run(steps, order1, {"mask": lambda: own(1, 0), "carry": lambda: own(1, 1), "partner": partner_u if t else spare, "masks": masks})
+        spare()
         scan(A("sc", 0, C), A("ps0", 0, C), A("md", 0, C), ALU.max, ALU.add)
-        mm(A("ps1", 0, C), up[0], up[1], lq, ls)
-        if t > 0:
-            unpack()
+        spare()
         act(A("ssb"), A("ps3", 0, C), ACT.Copy)
-        if t == 0:
-            act(A("mst"), A("sq", 0, 256), ACT.Identity, scale=-BIG / 8, bias=9 * BIG / 8)
-            act(A("mst", 15, 256, 16), A("mst", 15, 256, 16), ACT.Identity, bias=-3 * BIG)
         ts(of, A("sc", 15, C, 16), -1.0, ALU.mult, finr, ALU.add)
         send(peer[t], af, of, "af%d" % t)
+        spare(2)
+        mm(A("ps1", 0, C), up[0], up[1], lq, ls)
         act(A("spb"), A("ps1", 0, C), ACT.Copy)
         if t > 0:
+            unpack()
             halve()
         scatter(A("orep"), of, A("cidx"))
-        if t == 0:
-            iota(A("crow", 16, 45), [[16, 29]], 1 - NP)
-            scan(A("sc", 0, NV), A("p0", 0, NV), A("mst", 0, NV), ALU.max, ALU.add)
+        spare()
         scan(A("sc", 368, NP), A("orep", C - K, C), A("mst", 0, K), ALU.max, ALU.add)
-        if t == 0:
-            ts(A("x32", 0, 16), A("sc", 15, NV, 16), 2 * BIG, ALU.add)
+        spare()
         ts(ol, A("sc", 383, NP, 16), 2 * BIG, ALU.add)
         send(peer[t], al, ol, "al%d" % t)
         act(A("ss", 0, K), A("ssb"), ACT.Copy, off=ol)
+        spare()
         if t == 0:
-            ts(A("x32", 16, 32), A("x32", 0, 16), 7, ALU.arith_shift_right)
-            ts(A("x32", 32, 48), A("x32", 0, 16), 127, ALU.bitwise_and)
-            ts(A("et", 3, 515, 4), A("cidx", 0, 128), pc, ALU.is_equal)
-            cp(A("ijl"), A("x32", 16, 48))
-            ts(fin0, m15, -SMALL, ALU.add, fin, ALU.add)
-            ts(A("cb", 16, 45), A("crow", 16, 45), m15, ALU.add, -3 * SMALL, ALU.add)
-            for b in range(4):
-                quant(half("eq", b), half("es", b), A("et", 3 - b, 515 - b))
-            ts(A("cb", 19, 33), A("cb", 19, 33), nk, ALU.add, 15.0, ALU.add)
-            cp(A("bb", 16, 45), A("cb", 16, 45))
-            ts(A("cb", 19, 33), A("cb", 19, 33), nk, ALU.add)
             iota(A("nn"), [[-16384, NP]], 16384 * (NP - 1))
-            unpack()
         lists_of_a()
-        act(A("si"), A("ss"), ACT.Copy, off=A("ijl", 0, 16))
+        act(A("si", NV0, NV), A("ss", 0, K), ACT.Copy, off=A("ijl", 0, nv))
         act(A("ap"), A("tt"), ACT.Copy, off=A("o4"), scale=0.5)
-        if t == 1:
-            scan(A("pk"), A("nn"), A("p0"), ALU.min, ALU.add, 2 * BIG)
-        if t == 2:
-            quant(A("vq"), A("vs"), A("vt"))
         scatter(A("ee"), af, A("spb"))
-        tt(A("xm", 368, NP), A("ee", C - K, C), A("oh", 0, K), ALU.mult)
+        spare()
+        scan(A("hh", 368, NP), A("pm"), A("ee", C - K, C), ALU.max, ALU.min)
         at = 368
         rows = []
         for i in range(1, K):
@@ -462,32 +482,54 @@ def rank_program(g, core, T, topo):
             if lo < at:
                 rows.append((lo, at, i))
             at -= ROWS[i]
+        act(A("vv", SPARE, NV0), A("ss", 0, NV0 - SPARE), ACT.Identity, bias=col("ee", C - 1))
         for lo, at, i in reversed(rows):
             act(A("vv", lo, at), A("ee", C - (at - lo), C), ACT.Identity, bias=col("ss", K - 1 - i))
-        tt(A("vv", 0, NV), A("ee", C - K, C), A("si"), ALU.add, off=A("ijl", 16, 32))
-        scan(A("hh", 368, NP), A("rs", 0, K), A("xm", 368, NP), ALU.mult, ALU.add)
-        tt(A("xm", 48, 272), A("vv", 48, 272), A("oh", 0, 224), ALU.mult)
+        tt(A("vv", NV0, NV), A("ee", C - K, C), A("si", NV0, NV), ALU.add, off=A("ijl", 16, 16 + nv))
 
         def rows_own(which):
             for i, m0, m1 in which:
                 act(A("dg", m0, m1), A("hh", NP - 1 - 16 * (m1 - m0 - 1), NP, 16), ACT.Identity, bias=col("ss", K - 1 - i))
 
-        rows_own([(0, 23, 29)])
-        run(ORDER2, order2, {"rows": lambda: rows_own([(1, 20, 23), (2, 18, 20), (3, 17, 18)]),
-                             "carry": lambda: scan(A("hh", 48, 272), A("rs", 0, 224), A("xm", 48, 272), ALU.mult, ALU.add)})
-        ts(A("off2", 23, 29), A("md", 383, NP, 16), -1.0, ALU.mult, fin0, ALU.add)
-        scan(A("sc", 0, 368), A("ps1", 0, 368), A("md", 0, 368), ALU.max, ALU.add)
-        ts(A("off2", 0, 23), A("sc", 15, 368, 16), -1.0, ALU.mult, fin, ALU.add)
+        rows_own([(0, 23, 29), (1, 20, 23), (2, 18, 20), (3, 17, 18)])
+        spare()
+        tt(A("xm", 48, 272), A("vv", 48, 272), A("oh", 0, 224), ALU.mult)
+        src = "pk" if t == R - 1 else "p0"
+        run(ORDER2, order2, {
+            "carry": lambda: scan(A("hh", 48, 272), A("rs", 0, 224), A("xm", 48, 272), ALU.mult, ALU.add),
+            "spare": spare,
+            "up0": lambda: tt(A("md", UP + 15, NP, 16), A("bb", 33, 45), A("rsum", 33, 45), ALU.subtract),
+            "up1": lambda: scan(A("sc", UP, 368), A("ps0", UP - UP0, 368 - UP0), A("md", UP, 368), ALU.max, ALU.add),
+            "up2": lambda: ts(A("off2", 24, 30), A("md", 383, NP, 16), -1.0, ALU.mult, fin0, ALU.add),
+            "up3": lambda: ts(A("off2", 18, 24), A("sc", UP + 15, 368, 16), -1.0, ALU.mult, fin, ALU.add),
+            "up4": lambda: scatter(A("prep"), A("off2", 18, 30), A(src, UP, NP))})
+        spare()
+        scan(A("sc", 0, UP), A("ps1", 0, UP), A("md", 0, UP), ALU.max, ALU.add)
+        spare()
+        ts(A("off2", 0, 17), A("sc", 15, UP, 16), -1.0, ALU.mult, fin, ALU.add)
+        spare(len(aside))
         if t == 0:
+            unpack()
             halve()
         for b in range(4):
             act(half("ep", b, K), half("dp", b, C), ACT.Copy, off=al)
-        scatter(A("prep"), A("off2", 0, 29), A("pk" if t == R - 1 else "p0"))
+        scatter(A("prep"), A("off2", 0, 17), A(src, 0, UP))
+        if t == R - 1:
+            act(half("nb", 0, C), A("prep", 0, C), ACT.Identity, scale=1.0 / 16384, bias=-0.375)
+        if t < R - 1:
+            aside.extend([lambda b=b: scan(half("pk", b, 116), half("nn", b, 116), half("p0", b, 116), ALU.min, ALU.add, 2 * BIG)
+                          for b in (2 * t, 2 * t + 1)])
+        if t == 1:
+            aside.append(lambda: quant(A("vq"), A("vs"), A("vt")))
+        spare()
         scan(A("sc", 0, C), A("prep", 0, C), A("mst"), ALU.max, ALU.add)
-        ts(A("x32", 0, 16), A("sc", 15, C, 16), 2 * BIG, ALU.add)
+        spare()
         if t < R - 1:
             ts(A("il"), A("sc", 15, C, 16), 2 * BIG - 48, ALU.add, 1.0 / 128, ALU.mult)
-        else:
+        ts(A("x32", 0, 16), A("sc", 15, C, 16), 2 * BIG, ALU.add)
+        spare()
+        if t == R - 1:
+            act(half("nb", 1, C), half("nb", 0, C), ACT.Identity, bias=1.5 * BIG)
             ts(A("x32", 16, 32), A("x32", 0, 16), 7, ALU.arith_shift_right, 127, ALU.bitwise_and)
         ts(A("x32", 32, 48), A("x32", 0, 16), 127, ALU.bitwise_and)
         if t == R - 1:
@@ -525,21 +567,17 @@ def rank_program(g, core, T, topo):
             tt(A("tt", 512 * h + b, 512 * h + 512, 4), half("rl", k), A("zz", 512 * h + b, 512 * h + 512, 4), ALU.add)
             if k == 4:
                 state(0)
-            if k == 6 and t < R - 1:
-                own(0, 0)
+            if k in (6, 7) and t < R - 1:
+                own(0, k - 6)
         if t == R - 1:
-            act(half("nb", 0, C), A("prep", 0, C), ACT.Identity, scale=1.0 / 16384, bias=-0.375)
+            act(half("nb", 2, C), half("nb", 1, C), ACT.Identity, bias=-1.5 * BIG)
+            op("y", lambda: [g.sync.dma_start(T.ol[:], T.nb[0:128:16, 2 * C:3 * C])], [half("nb", 2, C)], [], sem="do")
             act(half("ysb", 0), A("ps4", 0, 128), ACT.Copy)
             op("s", lambda: [g.scalar.dma_start(T.y[:, 0:128], ap(half("ysb", 0)))], [half("ysb", 0)], [], sem="dy")
-        else:
-            own(0, 1)
         state(1)
 
     cp(half("ysb", 1), A("ps5", 0, 128))
-    act(half("nb", 1, C), half("nb", 0, C), ACT.Identity, bias=1.5 * BIG)
-    act(half("nb", 2, C), half("nb", 1, C), ACT.Identity, bias=-1.5 * BIG)
     op("y", lambda: [g.sync.dma_start(T.osc[4 * k:4 * k + 4, :], T.fs[32 * k:32 * k + 4, :]) for k in range(4)], [A("fs")], [], sem="dq")
-    op("s", lambda: [g.scalar.dma_start(T.y[:, 128:256], ap(half("ysb", 1))), g.scalar.dma_start(T.ol[:], T.nb[0:128:16, 2 * C:3 * C])],
-       [half("ysb", 1), half("nb", 2, C)], [], sem="dy")
+    op("s", lambda: [g.scalar.dma_start(T.y[:, 128:256], ap(half("ysb", 1)))], [half("ysb", 1)], [], sem="dy")
     for s in count:
         g.wait_ge(T.sem[s], count[s])

@@ -1,5 +1,5 @@
 from concourse.bass import DstId, RemoteDMATransfer
-from concourse.mybir import dt, AluOpType, ActivationFunctionType
+from concourse.mybir import dt, AluOpType, ActivationFunctionType, AxisListType
 
 C, K, R = 256, 96, 3
 STEP = [1, 2, 4]
@@ -9,20 +9,22 @@ NV0, NV = 48, 256
 UP, UP0 = 272, 192
 F32, BF, I32, U16, X4, U8 = "float32", "bfloat16", "int32", "uint16", "float8_e4m3fn_x4", "uint8"
 BIG, SMALL = float(2 ** 23), 4096.0
+GAP = 128.0 * (K - 1) + K
+OFF = GAP + 160
 
 SPARE = NP - sum(ROWS)
 LEN2 = {m: 16 * m for m in range(3, 17)}
 LEN2.update({17: 264, 18: 288, 19: 288, 20: 320, 21: 320, 22: 320})
 LEN2.update({m: 368 for m in range(23, 29)})
-TILES1 = [(128, [1, 2, 3, 4]), (128, [5, 6, 7, 8]), (192, [9, 10, 11, 12]), (256, [13, 14, 15, None])]
-TILES2 = [(128, [3, 4, 5]), (144, [6, 7, 8, 9]), (208, [10, 11, 12, 13]), (272, [14, 15, 16, None]),
-          (320, [17, 18, 19, 20]), (368, [21, 22, 23, 24]), (368, [25, 26, 27, 28])]
+TILES1 = [(256, [13, 14, 15, None]), (128, [5, 6, 7, 8]), (192, [9, 10, 11, 12]), (128, [1, 2, 3, 4])]
+TILES2 = [(368, [25, 26, 27, 28]), (368, [21, 22, 23, 24]), (320, [17, 18, 19, 20]), (272, [14, 15, 16, None]),
+          (208, [10, 11, 12, 13]), (144, [6, 7, 8, 9]), (128, [3, 4, 5])]
 LEN1 = {m: 16 * m for m in range(1, 16)}
-T0, T1, T2, T3, T4, T5, T6 = [("tile", k) for k in range(7)]
-ORDER1 = [-7, -6, 107, 106, 5, 4, 3, 2, "mask", 1, "carry", -8, 15, 108, 14, 13, "in", 12, T3, 11, 10, 9, "masks", T0, "row", T2, "base", T1,
-          "partner", "sum"]
-ORDER2 = [-28, 27, 128, "carry", -24, 26, 124, 25, 23, T6, "spare", 22, 21, 20, T5, "spare", 19, 18, 17, -16, T4, "in", 15, 116, 14, 13,
-          "up0", 12, "up1", "up2", "up3", 11, 10, 9, 8, 7, 6, 5, 4, 3, "up4", T3, T2, T1, "row", T0, "base", "spare", "sum"]
+ORDER1 = [-7, 107, 6, 5, 4, 3, 2, "mask", 201, "carry", 301, -12, 15, 112, 14, 13, "in", 11, (0,), 10, 9, 8, "masks", (2, 3), (1,), "row",
+          "partner", "base", "sum"]
+ORDER2 = ["rows", -22, -21, 122, 121, -20, -19, 120, 119, 228, "carry", 227, 226, 225, -18, -17, 118, 117, 224, (0,), "spare", 223, -16, "in", (1,),
+          116, "spare", 15, 14, 13, (2,), 12, 11, "up0", 10, 9, "up1", (3,), "up2", 8, 7, 6, 5, 4, 3, (4,), "row", (5, 6), "base", "up3",
+          "spare", "sum"]
 W1 = sum(w for w, s in TILES1)
 W2 = sum(w for w, s in TILES2)
 
@@ -33,19 +35,19 @@ for _n, _w, _d in [
     ("urq", 128, X4), ("urs", 128, U8), ("ucq", 16, X4), ("ucs", 16, U8),
     ("ruq", 8, X4), ("rus", 8, U8), ("rtq", 128, X4), ("rts", 128, U8),
     ("zq", 256, X4), ("zs", 256, U8), ("fq", 256, X4), ("fs", 256, U8),
-    ("pcol", 8, I32), ("fcol", 8, F32), ("l32", 18, I32), ("l16", 18, U16),
-    ("rr", 368, BF), ("oh", 256, BF), ("sg", 368, BF), ("sq", 368, BF), ("gm", 256, BF), ("rs", 256, BF), ("mst", 256, BF), ("md", NP, F32),
+    ("pcol", 8, I32), ("fcol", 10, F32), ("l32", 18, I32), ("l16", 18, U16),
+    ("rr", 368, BF), ("oh", 256, BF), ("sg", 368, BF), ("sq", 368, BF), ("gm", 256, BF), ("rs", 256, BF), ("mst", 256, F32), ("md", NP, F32), ("fl", 1024, BF),
     ("gi", 128, BF), ("wt", 1024, BF), ("wcq", 256, X4), ("wcs", 256, U8),
     ("et", 520, BF), ("eq", 512, X4), ("es", 512, U8), ("zero", 520, BF),
     ("cidx", 256, F32), ("crow", 48, F32), ("cb", 48, F32), ("bb", 48, F32), ("rsum", 48, F32), ("dg", 32, F32),
-    ("p0", NP, F32), ("nn", NP, F32), ("pk", NP, F32), ("ijl", 32, U16),
+    ("p0", NP, F32), ("nn", NP, F32), ("ijl", 32, U16),
     ("c1", 4 * W1, BF), ("c2", 4 * W2, BF), ("jk", 4 * W2, BF), ("pm", K, BF),
     ("cq1", W1, X4), ("cs1", W1, U8), ("cq2", W2, X4), ("cs2", W2, U8),
     ("ssb", 256, F32), ("spb", 256, F32), ("xm", NP, F32), ("hh", NP, F32), ("ir", 256, BF), ("sc", NP, F32),
     ("off2", 30, U16), ("orep", 256, F32), ("prep", NP, F32), ("o4", 24, U16),
     ("ss", 112, F32), ("ee", 256, F32), ("si", NV, F32), ("vv", 368, F32),
     ("ap", 384, BF), ("ep", 384, BF), ("dp", 1024, BF), ("ag", 1024, BF), ("rl", 1024, F32),
-    ("x32", 48, I32), ("il", 16, U16), ("jl", 16, U16), ("nb", 768, F32), ("ysb", 256, F32),
+    ("x32", 64, I32), ("il", 16, U16), ("jl", 16, U16), ("nb", 80, F32), ("ysb", 256, F32),
 ]:
     SCRATCH[_n] = ("sbuf", [128, _w], _d)
 for _t in range(R):
@@ -55,7 +57,7 @@ for _t in range(R):
 for _t in range(8):
     SCRATCH["ps%d" % _t] = ("psum", [128, 512], F32)
 
-SEMAPHORES = (["qv", "qs", "qt", "qg", "dx0", "dx1", "du", "dv", "dw", "dz", "dq", "dr", "dy", "do", "loc", "ru", "rt"]
+SEMAPHORES = (["qv", "qs", "qt", "qg", "dx0", "dx1", "du", "dv", "dw", "dz", "dq", "dr", "dy", "do", "dn", "loc", "ru", "rt"]
               + ["%s%d" % (a, t) for a in ("au", "at", "al", "af") for t in range(R)])
 
 
@@ -194,7 +196,8 @@ def rank_program(g, core, T, topo):
         op("s", lambda: g.scalar.activation(ap(os_), ap(s).indirect(ap(off)), ACT.Copy), [s, off], [os_])
 
     def scan(out, d0, d1, o0, o1, first=0.0):
-        op("v", lambda: V.tensor_tensor_scan(ap(out), ap(d0), ap(d1), first, o0, o1), [d0, d1], [out])
+        op("v", lambda: V.tensor_tensor_scan(ap(out), ap(d0), ap(d1), ap(first) if isap(first) else first, o0, o1),
+           [d0, d1] + ([first] if isap(first) else []), [out])
 
     def fill(a, c):
         op("v", lambda: V.memset(ap(a), c), [], [a])
@@ -281,8 +284,6 @@ def rank_program(g, core, T, topo):
     iota(col("pcol", 0), [[0, 1]], 0, 1)
     iota(A("gi"), [[1, 8], [0, 16]], 0)
     iota(A("rr"), [[0, 23], [1, 16]], 0)
-    iota(A("l32", 0, 8), [[16, 8]], 0)
-    iota(A("l32", 8, 16), [[1, 8]], 0)
     kc, gc_, pc, fin, fin0, finr, nk, m15 = (col("fcol", j) for j in range(8))
     ts(col("pcol", 1), col("pcol", 0), 15, ALU.bitwise_and)
     ts(col("pcol", 2), col("pcol", 0), 4, ALU.arith_shift_right)
@@ -297,18 +298,20 @@ def rank_program(g, core, T, topo):
     ts(fin, kc, -1.0, ALU.mult, -2 * SMALL, ALU.add)
     ts(finr, kc, C - 1 - 2 * SMALL, ALU.add)
     ts(A("oh"), A("rr", 0, 256), kc, ALU.is_equal)
-    cp(A("l16", 0, 16), A("l32", 0, 16))
     op("g", lambda: g.affine_select(ap(A("wt", 515, 1024, 4)), ap(A("wt", 3, 512, 4)), [[1, 128]], ALU.is_gt, 0.0, 0, -1),
        [A("wt", 3, 512, 4)], [A("wt", 515, 1024, 4)])
+    iota(A("l32", 0, 8), [[16, 8]], 0)
+    iota(A("l32", 8, 16), [[1, 8]], 0)
     iota(A("crow", 0, 16), [[16, 16]], 15)
     iota(A("cidx"), [[1, 256]], 0)
     act(A("rs", 0, 224), A("rr", 0, 224), ACT.Sign)
     act(A("sg"), A("rr"), ACT.Sign, bias=nk)
     ts(m15, kc, 15.0, ALU.is_equal, SMALL, ALU.mult)
+    quant(A("wcq"), A("wcs"), A("wt"))
     quant(A("uq"), A("us"), A("ut"))
-    ts(A("cb", 0, 16), A("crow", 0, 16), m15, ALU.add, -3 * SMALL, ALU.add)
-    pick(A("urq"), A("urs"), A("uq"), A("us"), A("l16", 0, 8))
+    cp(A("l16", 0, 16), A("l32", 0, 16))
     pick(A("ucq"), A("ucs"), A("uq"), A("us"), A("l16", 16, 17))
+    pick(A("urq"), A("urs"), A("uq"), A("us"), A("l16", 0, 8))
     send3("q", A("ucq", 0, 8), 0)
     send3("s", A("ucs", 0, 8), 1)
     act(A("sq"), A("sg"), ACT.Square, scale=4.0, bias=-1.0)
@@ -319,11 +322,11 @@ def rank_program(g, core, T, topo):
         c, jk, cq, cs = "c" + cn, "jk", "cq" + cn, "cs" + cn
         start = [sum(w for w, s in tiles[:k]) for k in range(len(tiles))]
         slot = {m: (start[k], i) for k, (w, s) in enumerate(tiles) for i, m in enumerate(s)}
-        closes = [x for x in (ORDER1 if cn == "1" else ORDER2) if isinstance(x, tuple)]
+        closes = [k for x in (ORDER1 if cn == "1" else ORDER2) if isinstance(x, tuple) for k in x]
         n, b0 = inb[1] - inb[0], at0 + inb[0] // 16
         inside = A(c, 4 * (slot[None][0] + inb[0]) + slot[None][1], 4 * (slot[None][0] + inb[1]), 4)
 
-        def step(x):
+        def step(x, again):
             if x == "in":
                 tt(inside, (src("v", None), inb[0], inb[1], 1), A("hh", inb[0], inb[1]), cmp_in)
             elif x == "row":
@@ -333,26 +336,33 @@ def rank_program(g, core, T, topo):
             elif x == "sum":
                 tt(A("md", 15, 16 * nb, 16), A("bb", at0, at0 + nb), A("rsum", at0, at0 + nb), ALU.subtract)
             elif isinstance(x, tuple):
-                k = x[1]
-                at, w, z = start[k], tiles[k][0], 128 * (None in tiles[k][1])
-                quant(A(cq, at, at + w), A(cs, at, at + w), A(c, 4 * at, 4 * (at + w)))
-                if w > 16 * nb:
-                    wide = [y for y in closes if tiles[y[1]][0] > 16 * nb]
-                    mm(A("ps0", 0, w - UP0), A("wcq", 0, 128), A("wcs", 0, 128), A(cq, at + UP0, at + w), A(cs, at + UP0, at + w),
-                       x == wide[0], x == wide[-1])
-                    w = 16 * nb
-                mm(A(ps, 0, w), A("wcq", z, z + 128), A("wcs", z, z + 128), A(cq, at, at + w), A(cs, at, at + w), x == closes[0], x == closes[-1])
+                at, last = start[x[0]], tiles[x[-1]]
+                end = start[x[-1]] + (max(ln[m] for m in last[1]) if again and x[-1] == len(tiles) - 1 else last[0])
+                quant(A(cq, at, end), A(cs, at, end), A(c, 4 * at, 4 * end))
+                for k in x:
+                    at, w, z = start[k], tiles[k][0], 128 * (None in tiles[k][1])
+                    if w > 16 * nb:
+                        wide = [y for y in closes if tiles[y][0] > 16 * nb]
+                        mm(A("ps0", 0, w - UP0), A("wcq", 0, 128), A("wcs", 0, 128), A(cq, at + UP0, at + w), A(cs, at + UP0, at + w),
+                           k == wide[0], k == wide[-1])
+                        w = 16 * nb
+                    mm(A(ps, 0, w), A("wcq", z, z + 128), A("wcs", z, z + 128), A(cq, at, at + w), A(cs, at, at + w),
+                       k == closes[0], k == closes[-1])
             else:
                 m = abs(x) % 100
                 at, i = slot[m]
                 v = A(c, 4 * (at + lo) + i, 4 * (at + ln[m]), 4)
                 if x < 0:
                     act((jk,) + v[1:], (src("s", m), lo, ln[m], 1), ACT.Sign, scale=-1.0, bias=scal(m))
-                elif x > 100:
+                elif x > 300:
+                    r = col("rsum", at0 + m)
+                    op("v", lambda: V.tensor_reduce(ap(r), ap(v), AxisListType.X, ALU.add), [v], [r])
+                elif 100 < x < 200:
                     act(v, (jk,) + v[1:], ACT.Relu, scale=sign, acc=col("rsum", at0 + m))
                 else:
                     ts(v, (src("v", m), lo, ln[m], 1), scal(m), cmp)
-                    act((jk,) + v[1:], v, ACT.Copy, acc=col("rsum", at0 + m))
+                    if x < 100:
+                        act((jk,) + v[1:], v, ACT.Copy, acc=col("rsum", at0 + m))
         return step
 
     order1 = counting(lambda q, m: ("ps4" if q == "v" else "ps5") if m is not None and m <= 8 else ("ps2" if q == "v" else "ps3"),
@@ -374,9 +384,9 @@ def rank_program(g, core, T, topo):
 
     quant(half("tq0", 0), half("ts0", 0), half("tt", 0, 512))
     scores(0, 0)
-    quant(A("wcq"), A("wcs"), A("wt"))
-    own(0, 0)
     quant(half("tq0", 1), half("ts0", 1), half("tt", 1, 512))
+    own(0, 0)
+    ts(A("cb", 0, 16), A("crow", 0, 16), m15, ALU.add, -3 * SMALL, ALU.add)
 
     for t in range(R):
         tq, tsc, lq, ls = A("tq%d" % t), A("ts%d" % t), A("lq%d" % t), A("ls%d" % t)
@@ -386,21 +396,21 @@ def rank_program(g, core, T, topo):
         def partner_u():
             pick(up[0], up[1], A("ulq%d" % t), A("uls%d" % t), A("l16", 8, 16))
 
-        def lists_of_a():
-            for b in range(4):
-                ts(A("o4", 6 * b, 6 * b + 6), ol, 4.0, ALU.mult, float(b), ALU.add)
-
-        def unpack():
-            for b in range(4):
+        def unpack(which):
+            for b in which:
                 mm(A("ps%d" % (4 + b), 0, C), half("eq", b), half("es", b), lq, ls)
 
-        def halve():
-            for b in range(4):
+        def halve(which):
+            for b in which:
                 act(half("dp", b, C), A("ps%d" % (4 + b), 0, C), ACT.Copy, scale=0.5)
+
+        def arrived(which):
+            for b in which:
+                act(half("ep", b, K), half("dp", b, C), ACT.Copy, off=al)
 
         def run(steps, one, more):
             for x in steps:
-                more[x]() if x in more else one(x)
+                more[x]() if x in more else one(x, t > 0)
 
         scores(t, 1)
         if t == far:
@@ -411,24 +421,25 @@ def rank_program(g, core, T, topo):
             send(peer[t], ls, tsc, "at%d" % t)
         if t == 0:
             own(0, 1)
-            iota(A("p0", 0, 5), [[0, 5]], K * 128)
-            at, i = 5, K - 1
+            runs, at, i = [], SPARE, K - 1
             while i >= 0:
                 n = len([r for r in range(K) if ROWS[r] == ROWS[i]])
-                iota(A("p0", at, at + n * ROWS[i]), [[128, n], [1, ROWS[i]]], 128 * (K - 1 - i) + K - ROWS[i])
+                runs.append((A("p0", at, at + n * ROWS[i]), [[128, n], [1, ROWS[i]]], 128 * (K - 1 - i) + K - ROWS[i]))
                 at, i = at + n * ROWS[i], i - n
+            iota(A("crow", 16, 45), [[16, 29]], 1 - NP)
+            for r in runs:
+                if r[0][1] < NV:
+                    iota(*r)
         nv = (NV - NV0) // 16
         aside = [] if t else [
             lambda: ts(A("et", 3, 515, 4), A("cidx", 0, 128), pc, ALU.is_equal),
-            lambda: ts(fin0, m15, -SMALL, ALU.add, fin, ALU.add),
             lambda: ts(A("cb", 16, 45), A("crow", 16, 45), m15, ALU.add, -3 * SMALL, ALU.add),
+            lambda: cp(A("bb", 16, 45), A("cb", 16, 45)),
             lambda: scan(A("xm", NV0, NV), A("p0", NV0, NV), A("mst", 0, NV - NV0), ALU.max, ALU.add),
-            partner_u,
-            lambda: ts(A("ijl", 0, nv), A("xm", NV0 + 15, NV, 16), 2 * BIG - 48, ALU.add, 1.0 / 128, ALU.mult),
-            lambda: ts(A("x32", 0, nv), A("xm", NV0 + 15, NV, 16), 2 * BIG, ALU.add),
+            lambda: ts(A("ijl", 0, nv), A("xm", NV0 + 15, NV, 16), OFF - 48, ALU.add, 1.0 / 128, ALU.mult),
+            lambda: ts(A("x32", 0, nv), A("xm", NV0 + 15, NV, 16), OFF, ALU.add),
             lambda: ts(A("x32", 16, 16 + nv), A("x32", 0, nv), 127, ALU.bitwise_and),
             lambda: cp(A("ijl", 16, 16 + nv), A("x32", 16, 16 + nv)),
-            lambda: cp(A("bb", 16, 45), A("cb", 16, 45)),
             lambda: ts(A("cb", 19, 33), A("cb", 19, 33), nk, ALU.add, 15.0, ALU.add),
             lambda: ts(A("cb", 19, 33), A("cb", 19, 33), nk, ALU.add),
         ] + [lambda b=b: quant(half("eq", b), half("es", b), A("et", 3 - b, 515 - b)) for b in range(4)]
@@ -440,12 +451,11 @@ def rank_program(g, core, T, topo):
 
         def masks():
             if t == 0:
-                act(A("mst"), A("sq", 0, 256), ACT.Identity, scale=-BIG / 8, bias=9 * BIG / 8)
-                act(A("mst", 15, 256, 16), A("mst", 15, 256, 16), ACT.Identity, bias=-3 * BIG)
+                act(A("mst", 0, C), A("sq", 0, C), ACT.Identity, scale=-BIG / 8, bias=9 * BIG / 8)
                 act(A("pm"), A("oh", 0, K), ACT.Identity, scale=2e29, bias=-1e29)
-                iota(A("crow", 16, 45), [[16, 29]], 1 - NP)
+                act(A("mst", 15, C, 16), A("mst", 15, C, 16), ACT.Identity, bias=-BIG - OFF)
 
-        steps = ORDER1 if t else [abs(x) if isinstance(x, int) else x for x in ORDER1 if not (isinstance(x, int) and x > 100)]
+        steps = ORDER1 if t else [-ORDER1[0]] + ORDER1[2:]
         run(steps, order1, {"mask": lambda: own(1, 0), "carry": lambda: own(1, 1), "partner": partner_u if t else spare, "masks": masks})
         spare()
         scan(A("sc", 0, C), A("ps0", 0, C), A("md", 0, C), ALU.max, ALU.add)
@@ -453,25 +463,47 @@ def rank_program(g, core, T, topo):
         act(A("ssb"), A("ps3", 0, C), ACT.Copy)
         ts(of, A("sc", 15, C, 16), -1.0, ALU.mult, finr, ALU.add)
         send(peer[t], af, of, "af%d" % t)
-        spare(2)
+        spare()
+        if t == 0:
+            partner_u()
         mm(A("ps1", 0, C), up[0], up[1], lq, ls)
-        act(A("spb"), A("ps1", 0, C), ACT.Copy)
         if t > 0:
-            unpack()
-            halve()
+            unpack(range(4))
+        else:
+            act(half("fl", 6), A("sq", 0, 128), ACT.Identity, scale=-16.0, bias=144.0)
+        act(A("prep", 0, C), A("cidx"), ACT.Identity, scale=0.0, bias=GAP if t < R - 1 else 0.0)
+        if t == 0:
+            act(A("fl", 3 * C + 15, 896, 16), A("fl", 3 * C + 15, 896, 16), ACT.Identity, bias=GAP - OFF - 128)
+        act(A("spb"), A("ps1", 0, C), ACT.Copy)
+        early, mid, late = ((), (), range(4)) if t == 0 else ((), (0,), (1, 2, 3)) if t == far else ((0, 1), (2,), (3,))
+        halve(early)
         scatter(A("orep"), of, A("cidx"))
         spare()
         scan(A("sc", 368, NP), A("orep", C - K, C), A("mst", 0, K), ALU.max, ALU.add)
         spare()
-        ts(ol, A("sc", 383, NP, 16), 2 * BIG, ALU.add)
+        ts(ol, A("sc", 383, NP, 16), OFF, ALU.add)
         send(peer[t], al, ol, "al%d" % t)
         act(A("ss", 0, K), A("ssb"), ACT.Copy, off=ol)
         spare()
         if t == 0:
+            for r in runs:
+                if r[0][1] >= NV:
+                    iota(*r)
+            iota(A("p0", 0, SPARE), [[0, SPARE]], 0)
             iota(A("nn"), [[-16384, NP]], 16384 * (NP - 1))
-        lists_of_a()
+        aside.extend([lambda b=b: ts(A("o4", 6 * b, 6 * b + 6), ol, 4.0, ALU.mult, float(b), ALU.add) for b in range(4)])
         act(A("si", NV0, NV), A("ss", 0, K), ACT.Copy, off=A("ijl", 0, nv))
-        act(A("ap"), A("tt"), ACT.Copy, off=A("o4"), scale=0.5)
+        if t == 0:
+            for b in range(4):
+                aside.pop()()
+            act(A("ap"), A("tt"), ACT.Copy, off=A("o4"), scale=0.5)
+        halve(mid)
+        if t == 1:
+            quant(A("vq"), A("vs"), A("vt"))
+        if t == R - 1:
+            act(A("mst", 15, C, 16), A("mst", 15, C, 16), ACT.Identity, bias=OFF - 2 * BIG)
+            ts(col("pcol", 4), col("pcol", 2), 1, ALU.bitwise_and)
+            aside[:0] = [lambda e=e: ts(col("fcol", 8 + e), col("pcol", 4), float(e), ALU.is_equal) for e in range(2)]
         scatter(A("ee"), af, A("spb"))
         spare()
         scan(A("hh", 368, NP), A("pm"), A("ee", C - K, C), ALU.max, ALU.min)
@@ -491,50 +523,64 @@ def rank_program(g, core, T, topo):
             for i, m0, m1 in which:
                 act(A("dg", m0, m1), A("hh", NP - 1 - 16 * (m1 - m0 - 1), NP, 16), ACT.Identity, bias=col("ss", K - 1 - i))
 
-        rows_own([(0, 23, 29), (1, 20, 23), (2, 18, 20), (3, 17, 18)])
+        rows_own([(0, 23, 29)])
         spare()
         tt(A("xm", 48, 272), A("vv", 48, 272), A("oh", 0, 224), ALU.mult)
-        src = "pk" if t == R - 1 else "p0"
         run(ORDER2, order2, {
             "carry": lambda: scan(A("hh", 48, 272), A("rs", 0, 224), A("xm", 48, 272), ALU.mult, ALU.add),
-            "spare": spare,
-            "up0": lambda: tt(A("md", UP + 15, NP, 16), A("bb", 33, 45), A("rsum", 33, 45), ALU.subtract),
+            "spare": lambda: spare(t == 0),
+            "rows": lambda: rows_own([(1, 20, 23), (2, 18, 20), (3, 17, 18)]),
+            "up0": lambda: tt(A("md", UP + 15, 368, 16), A("bb", 33, 39), A("rsum", 33, 39), ALU.subtract),
             "up1": lambda: scan(A("sc", UP, 368), A("ps0", UP - UP0, 368 - UP0), A("md", UP, 368), ALU.max, ALU.add),
-            "up2": lambda: ts(A("off2", 24, 30), A("md", 383, NP, 16), -1.0, ALU.mult, fin0, ALU.add),
-            "up3": lambda: ts(A("off2", 18, 24), A("sc", UP + 15, 368, 16), -1.0, ALU.mult, fin, ALU.add),
-            "up4": lambda: scatter(A("prep"), A("off2", 18, 30), A(src, UP, NP))})
+            "up2": lambda: ts(A("off2", 18, 24), A("sc", UP + 15, 368, 16), -1.0, ALU.mult, fin, ALU.add),
+            "up3": lambda: scatter(A("prep"), A("off2", 18, 24), A("p0", UP, 368))})
         spare()
         scan(A("sc", 0, UP), A("ps1", 0, UP), A("md", 0, UP), ALU.max, ALU.add)
         spare()
         ts(A("off2", 0, 17), A("sc", 15, UP, 16), -1.0, ALU.mult, fin, ALU.add)
         spare(len(aside))
         if t == 0:
-            unpack()
-            halve()
-        for b in range(4):
-            act(half("ep", b, K), half("dp", b, C), ACT.Copy, off=al)
-        scatter(A("prep"), A("off2", 0, 17), A(src, 0, UP))
-        if t == R - 1:
-            act(half("nb", 0, C), A("prep", 0, C), ACT.Identity, scale=1.0 / 16384, bias=-0.375)
-        if t < R - 1:
-            aside.extend([lambda b=b: scan(half("pk", b, 116), half("nn", b, 116), half("p0", b, 116), ALU.min, ALU.add, 2 * BIG)
-                          for b in (2 * t, 2 * t + 1)])
-        if t == 1:
-            aside.append(lambda: quant(A("vq"), A("vs"), A("vt")))
-        spare()
-        scan(A("sc", 0, C), A("prep", 0, C), A("mst"), ALU.max, ALU.add)
-        spare()
-        if t < R - 1:
-            ts(A("il"), A("sc", 15, C, 16), 2 * BIG - 48, ALU.add, 1.0 / 128, ALU.mult)
-        ts(A("x32", 0, 16), A("sc", 15, C, 16), 2 * BIG, ALU.add)
-        spare()
-        if t == R - 1:
-            act(half("nb", 1, C), half("nb", 0, C), ACT.Identity, bias=1.5 * BIG)
-            ts(A("x32", 16, 32), A("x32", 0, 16), 7, ALU.arith_shift_right, 127, ALU.bitwise_and)
-        ts(A("x32", 32, 48), A("x32", 0, 16), 127, ALU.bitwise_and)
-        if t == R - 1:
-            cp(A("il"), A("x32", 16, 32))
-        cp(A("jl"), A("x32", 32, 48))
+            unpack(range(4))
+        halve(late)
+        if t > 0:
+            arrived((0,))
+            act(A("ap"), A("tt"), ACT.Copy, off=A("o4"), scale=0.5)
+            arrived((1,))
+        scatter(A("prep"), A("off2", 0, 17), A("p0", 0, UP))
+        if t == R - 2:
+            op("g", lambda: [g.dma_start(ap(A("p0")), ap(A("nn")), accum_op=ALU.add)], [A("nn")], [A("p0")], sem="dn")
+        last = t == R - 1
+        arrived((2, 3) if t else range(4))
+
+        def every(name, a):
+            return A(name, a + 15, a + 128, 16)
+
+        chain = [
+            lambda h: ts(half("fl", h), half("prep", h), 0.0 if last else GAP, ALU.is_equal),
+            lambda h: scan(half("sc", h), half("prep", h), half("mst", h), ALU.max, ALU.add),
+            lambda h: scan(half("fl", 2 + h), A("zero", 0, 128), half("fl", h), ALU.add, ALU.subtract, col("fl", C + 127) if h else 0.0),
+            lambda h: scan(half("fl", 4 + h), half("fl", 2 + h), half("fl", 6), ALU.max, ALU.add, GAP - OFF),
+        ]
+        if last:
+            chain += [
+                lambda h: ts(half("xm", h, 8), every("fl", 512 + 128 * h), -16383.0, ALU.mult, GAP - 16384 - 16383 * (OFF - GAP) - 2 * BIG, ALU.add),
+                lambda h: tt(half("x32", h, 8), every("sc", 128 * h), half("xm", h, 8), ALU.max),
+                lambda h: ts(half("x32", 2 + h, 8), half("x32", h, 8), 7, ALU.arith_shift_right, 127, ALU.bitwise_and),
+                lambda h: cp(half("il", h, 8), half("x32", 2 + h, 8))]
+        else:
+            chain += [
+                lambda h: tt(half("x32", h, 8), every("sc", 128 * h), every("fl", 512 + 128 * h), ALU.min),
+                lambda h: ts(half("il", h, 8), half("x32", h, 8), OFF - 48, ALU.add, 1.0 / 128, ALU.mult)]
+        chain += [lambda h: ts(half("x32", 4 + h, 8), half("x32", h, 8), 127, ALU.bitwise_and),
+                  lambda h: cp(half("jl", h, 8), half("x32", 4 + h, 8))]
+        chain[0](0)
+        chain[1](0)
+        for i in range(2, len(chain)):
+            chain[i](0)
+            chain[i - 2](1)
+        chain[-2](1)
+        if last:
+            ts(A("x32", 48, 64), A("x32", 0, 16), 14, ALU.arith_shift_right)
         nq, ns = ("tq%d" % (t + 1), "ts%d" % (t + 1)) if t < R - 1 else ("fq", "fs")
 
         def layer(h):
@@ -559,6 +605,15 @@ def rank_program(g, core, T, topo):
             tt(A("zz", 512 * h + b, 512 * h + 512, 4), half("ep", b, K), half("ag", k), ALU.add, off=half("jl", h, 8))
             if k == 4:
                 layer(0)
+            if k == 0:
+                chain[-1](1)
+            if last and k < 2:
+                ts(half("nb", k, 16), A("x32", 48, 64), 2 * BIG / 16384, ALU.add, col("fcol", 8 + k), ALU.mult)
+            if last and k == 2:
+                op("v", lambda: V.transpose(ap(A("nb", 32, 64)), ap(A("nb", 0, 32))), [A("nb", 0, 32)], [A("nb", 32, 64)])
+            if last and k == 3:
+                tt(A("nb", 64, 80), A("nb", 32, 48), A("nb", 48, 64), ALU.add)
+                op("y", lambda: [g.sync.dma_start(T.ol[:], ap(A("nb", 64, 80)))], [A("nb", 64, 80)], [], sem="do")
         for k in range(8):
             h, b = k // 4, k % 4
             if k == 0:
@@ -570,13 +625,11 @@ def rank_program(g, core, T, topo):
             if k in (6, 7) and t < R - 1:
                 own(0, k - 6)
         if t == R - 1:
-            act(half("nb", 2, C), half("nb", 1, C), ACT.Identity, bias=-1.5 * BIG)
-            op("y", lambda: [g.sync.dma_start(T.ol[:], T.nb[0:128:16, 2 * C:3 * C])], [half("nb", 2, C)], [], sem="do")
             act(half("ysb", 0), A("ps4", 0, 128), ACT.Copy)
             op("s", lambda: [g.scalar.dma_start(T.y[:, 0:128], ap(half("ysb", 0)))], [half("ysb", 0)], [], sem="dy")
         state(1)
 
-    cp(half("ysb", 1), A("ps5", 0, 128))
+    act(half("ysb", 1), A("ps5", 0, 128), ACT.Copy)
     op("y", lambda: [g.sync.dma_start(T.osc[4 * k:4 * k + 4, :], T.fs[32 * k:32 * k + 4, :]) for k in range(4)], [A("fs")], [], sem="dq")
     op("s", lambda: [g.scalar.dma_start(T.y[:, 128:256], ap(half("ysb", 1)))], [half("ysb", 1)], [], sem="dy")
     for s in count:

@@ -6,7 +6,7 @@ STEP = [1, 2, 4]
 ROWS = [K // (i + 1) for i in range(K)]
 NP = 464
 NV0, NV = 48, 256
-UP, UP0 = 272, 192
+PARTS = [("ps0", 240, 272, 368), ("ps1", 0, 0, 272)]
 F32, BF, I32, U16, X4, U8 = "float32", "bfloat16", "int32", "uint16", "float8_e4m3fn_x4", "uint8"
 BIG, SMALL = float(2 ** 23), 4096.0
 GAP = 128.0 * (K - 1) + K
@@ -15,16 +15,17 @@ OFF = GAP + 160
 SPARE = NP - sum(ROWS)
 LEN2 = {m: 16 * m for m in range(3, 17)}
 LEN2.update({17: 264, 18: 288, 19: 288, 20: 320, 21: 320, 22: 320})
-LEN2.update({m: 368 for m in range(23, 29)})
-TILES1 = [(256, [13, 14, 15, None]), (128, [5, 6, 7, 8]), (192, [9, 10, 11, 12]), (128, [1, 2, 3, 4])]
-TILES2 = [(368, [25, 26, 27, 28]), (368, [21, 22, 23, 24]), (320, [17, 18, 19, 20]), (272, [14, 15, 16, None]),
+COARSE, FINE, RUN = 23, 24, 16
+LEN2.update({COARSE: 368, FINE: 368})
+TILES1 = [(256, [13, 14, 15, None]), (192, [9, 10, 11, 12]), (128, [5, 6, 7, 8]), (128, [1, 2, 3, 4])]
+TILES2 = [(368, [20, 21, 22, COARSE]), (368, [17, 18, 19, FINE]), (272, [14, 15, 16, None]),
           (208, [10, 11, 12, 13]), (144, [6, 7, 8, 9]), (128, [3, 4, 5])]
 LEN1 = {m: 16 * m for m in range(1, 16)}
-ORDER1 = [-7, 107, 6, 5, 4, 3, 2, "mask", 201, "carry", 301, -12, 15, 112, 14, 13, "in", 11, (0,), 10, 9, 8, "masks", (2, 3), (1,), "row",
-          "partner", "base", "sum"]
-ORDER2 = ["rows", -22, -21, 122, 121, -20, -19, 120, 119, 228, "carry", 227, 226, 225, -18, -17, 118, 117, 224, (0,), "spare", 223, -16, "in", (1,),
-          116, "spare", 15, 14, 13, (2,), 12, 11, "up0", 10, 9, "up1", (3,), "up2", 8, 7, 6, 5, 4, 3, (4,), "row", (5, 6), "base", "up3",
-          "spare", "sum"]
+ORDER1 = [-5, 105, 4, 3, 2, 201, "mask", 7, "carry", 6, 301, -12, 15, 112, 14, 13, "in", 8, (0,), 11, (2, 3), 10, 9, "row", (1,), "masks",
+          "base", "partner", "sum"]
+ORDER2 = [-22, "ends", -21, 122, 121, "rows", 20, "carry", COARSE, -19, -18, 119, 118, -17, -16, 117, 116, "spare", 15, 14, (0,), 13, 12, 11, 10, "in",
+          "runs", 9, "list", 8, "fine", (3,), 7, (1,), 6, 5, "up0", 4, (2,), 203, "up1", "row", "up2", 303, (4, 5), "base", "up3",
+          "spare", "spare", "sum"]
 W1 = sum(w for w, s in TILES1)
 W2 = sum(w for w, s in TILES2)
 
@@ -35,19 +36,19 @@ for _n, _w, _d in [
     ("urq", 128, X4), ("urs", 128, U8), ("ucq", 16, X4), ("ucs", 16, U8),
     ("ruq", 8, X4), ("rus", 8, U8), ("rtq", 128, X4), ("rts", 128, U8),
     ("zq", 256, X4), ("zs", 256, U8), ("fq", 256, X4), ("fs", 256, U8),
-    ("pcol", 8, I32), ("fcol", 10, F32), ("l32", 18, I32), ("l16", 18, U16),
-    ("rr", 368, BF), ("oh", 256, BF), ("sg", 368, BF), ("sq", 368, BF), ("gm", 256, BF), ("rs", 256, BF), ("mst", 256, F32), ("md", NP, F32), ("fl", 1024, BF),
-    ("gi", 128, BF), ("wt", 1024, BF), ("wcq", 256, X4), ("wcs", 256, U8),
+    ("pcol", 8, I32), ("fcol", 11, F32), ("l32", 18, I32), ("l16", 18, U16),
+    ("rr", 368, BF), ("oh", 256, BF), ("sg", 368, BF), ("sq", 368, BF), ("gm", 256, BF), ("rs", 256, BF), ("mst", 256, F32), ("md", NP, F32), ("fl", 768 + 368, BF),
+    ("gi", 128, BF), ("wt", 1536, BF), ("wcq", 384, X4), ("wcs", 384, U8),
     ("et", 520, BF), ("eq", 512, X4), ("es", 512, U8), ("zero", 520, BF),
-    ("cidx", 256, F32), ("crow", 48, F32), ("cb", 48, F32), ("bb", 48, F32), ("rsum", 48, F32), ("dg", 32, F32),
-    ("p0", NP, F32), ("nn", NP, F32), ("ijl", 32, U16),
-    ("c1", 4 * W1, BF), ("c2", 4 * W2, BF), ("jk", 4 * W2, BF), ("pm", K, BF),
+    ("cidx", 256, F32), ("crow", 48, F32), ("cb", 48, F32), ("bb", 48, F32), ("rsum", 48, F32), ("dg", 49, F32),
+    ("p0", 368, F32), ("nn", K, F32), ("ijl", 32, U16),
+    ("c1", 4 * W1, BF), ("c2", 4 * W2, BF), ("jk", 4 * W2, BF), ("pm", 2 * K, BF),
     ("cq1", W1, X4), ("cs1", W1, U8), ("cq2", W2, X4), ("cs2", W2, U8),
     ("ssb", 256, F32), ("spb", 256, F32), ("xm", NP, F32), ("hh", NP, F32), ("ir", 256, BF), ("sc", NP, F32),
-    ("off2", 30, U16), ("orep", 256, F32), ("prep", NP, F32), ("o4", 24, U16),
+    ("off2", 56, U16), ("orep", 256, F32), ("prep", NP, F32), ("o4", 24, U16),
     ("ss", 112, F32), ("ee", 256, F32), ("si", NV, F32), ("vv", 368, F32),
     ("ap", 384, BF), ("ep", 384, BF), ("dp", 1024, BF), ("ag", 1024, BF), ("rl", 1024, F32),
-    ("x32", 64, I32), ("il", 16, U16), ("jl", 16, U16), ("nb", 80, F32), ("ysb", 256, F32),
+    ("x32", 64, I32), ("il", 16, U16), ("jl", 16, U16), ("nb", 768, F32), ("ysb", 256, F32),
 ]:
     SCRATCH[_n] = ("sbuf", [128, _w], _d)
 for _t in range(R):
@@ -57,7 +58,7 @@ for _t in range(R):
 for _t in range(8):
     SCRATCH["ps%d" % _t] = ("psum", [128, 512], F32)
 
-SEMAPHORES = (["qv", "qs", "qt", "qg", "dx0", "dx1", "du", "dv", "dw", "dz", "dq", "dr", "dy", "do", "dn", "loc", "ru", "rt"]
+SEMAPHORES = (["qv", "qs", "qt", "qg", "dx0", "dx1", "du", "dv", "dw", "dz", "dq", "dr", "dy", "do", "loc", "ru", "rt"]
               + ["%s%d" % (a, t) for a in ("au", "at", "al", "af") for t in range(R)])
 
 
@@ -264,8 +265,8 @@ def rank_program(g, core, T, topo):
     for h in range(2):
         op("y", lambda: [g.sync.dma_start(ap(half("tt", h, 512)), T.x[:, 512 * h:512 * h + 512])], [], [half("tt", h, 512)], sem="dx%d" % h)
     fill(A("zero"), 0.0)
-    blank = {"c1": [], "c2": [A("et")]}
-    for name, tiles, ln, first, inb in (("c1", TILES1, LEN1, 0, 0), ("c2", TILES2, LEN2, SPARE, 48)):
+    blank = {"c1": [], "c2": []}
+    for name, tiles, ln, first, inb in (("c1", TILES1, LEN1, 0, 0), ("c2", TILES2, LEN2, 0, 48)):
         at = 0
         for w, slots in tiles:
             lo = min(ln[m] for m in slots if m is not None) if len(slots) == 4 else 0
@@ -278,47 +279,47 @@ def rank_program(g, core, T, topo):
     for a in blank["c1"]:
         act(a, A("zero", 0, a[2] - a[1]), ACT.Copy)
     op("y", lambda: [g.sync.dma_start(ap(a), ap(A("zero", 0, a[2] - a[1]))) for a in blank["c2"]], [A("zero")], blank["c2"], sem="dz")
-    op("y", lambda: [g.sync.dma_start(u8(A("wq")), T.wc[:]), g.sync.dma_start(ap(A("wp")), T.ws[:])], [], [A("wq"), A("wp")], sem="dw")
-    op("y", lambda: [g.sync.dma_start(ap(A("vt")), T.v[:])], [], [A("vt")], sem="dv")
 
     iota(col("pcol", 0), [[0, 1]], 0, 1)
+    iota(A("l32", 0, 8), [[16, 8]], 0)
     iota(A("gi"), [[1, 8], [0, 16]], 0)
     iota(A("rr"), [[0, 23], [1, 16]], 0)
-    kc, gc_, pc, fin, fin0, finr, nk, m15 = (col("fcol", j) for j in range(8))
+    kc, gc_, pc, fin, ends, finr, nk, m15 = (col("fcol", j) for j in range(8))
+    few, turn, none = col("fcol", 8), col("fcol", 9), col("fcol", 10)
     ts(col("pcol", 1), col("pcol", 0), 15, ALU.bitwise_and)
     ts(col("pcol", 2), col("pcol", 0), 4, ALU.arith_shift_right)
     ts(col("pcol", 3), col("pcol", 0), 7, ALU.bitwise_and)
     cp(pc, col("pcol", 0))
     cp(A("fcol", 0, 2), A("pcol", 1, 3))
     ts(col("l16", 16), col("pcol", 3), 16.0, ALU.mult)
-    ts(nk, kc, -1.0, ALU.mult)
+    cp(A("l16", 0, 8), A("l32", 0, 8))
+    ts(m15, kc, 15.0, ALU.is_equal, SMALL, ALU.mult)
+    for a, scale, bias in ((nk, -1.0, 0.0), (finr, 1.0, C - 1 - 2 * SMALL), (ends, float(RUN), RUN - 1.0)):
+        ts(a, kc, scale, ALU.mult, bias, ALU.add)
+    fill(A("rsum"), 0.0)
+    ts(m15, m15, -3 * SMALL, ALU.add)
     for j in (3, 0, 1, 2, 4, 5, 6):
         ts(A("wt", 512 * (j // 4) + j % 4, 512 * (j // 4 + 1), 4), A("gi"), gc_, ALU.is_equal)
-    fill(A("rsum"), 0.0)
-    ts(fin, kc, -1.0, ALU.mult, -2 * SMALL, ALU.add)
-    ts(finr, kc, C - 1 - 2 * SMALL, ALU.add)
-    ts(A("oh"), A("rr", 0, 256), kc, ALU.is_equal)
     op("g", lambda: g.affine_select(ap(A("wt", 515, 1024, 4)), ap(A("wt", 3, 512, 4)), [[1, 128]], ALU.is_gt, 0.0, 0, -1),
        [A("wt", 3, 512, 4)], [A("wt", 515, 1024, 4)])
-    iota(A("l32", 0, 8), [[16, 8]], 0)
     iota(A("l32", 8, 16), [[1, 8]], 0)
     iota(A("crow", 0, 16), [[16, 16]], 15)
     iota(A("cidx"), [[1, 256]], 0)
     act(A("rs", 0, 224), A("rr", 0, 224), ACT.Sign)
-    act(A("sg"), A("rr"), ACT.Sign, bias=nk)
-    ts(m15, kc, 15.0, ALU.is_equal, SMALL, ALU.mult)
-    quant(A("wcq"), A("wcs"), A("wt"))
+    ts(A("oh"), A("rr", 0, 256), kc, ALU.is_equal)
     quant(A("uq"), A("us"), A("ut"))
-    cp(A("l16", 0, 16), A("l32", 0, 16))
-    pick(A("ucq"), A("ucs"), A("uq"), A("us"), A("l16", 16, 17))
+    ts(few, kc, RUN - 1.0, ALU.is_ge, 1e29, ALU.mult)
+    ts(none, kc, float(K // RUN), ALU.is_ge, 1e29, ALU.mult)
     pick(A("urq"), A("urs"), A("uq"), A("us"), A("l16", 0, 8))
+    pick(A("ucq"), A("ucs"), A("uq"), A("us"), A("l16", 16, 17))
     send3("q", A("ucq", 0, 8), 0)
     send3("s", A("ucs", 0, 8), 1)
+    act(A("sg"), A("rr"), ACT.Sign, bias=nk)
     act(A("sq"), A("sg"), ACT.Square, scale=4.0, bias=-1.0)
     act(A("gm"), A("sg", 0, 256), ACT.Relu)
     act(A("md", 0, 368), A("sq"), ACT.Identity, scale=-SMALL / 8, bias=9 * SMALL / 8)
 
-    def counting(src, tiles, ln, lo, inb, cn, cmp, cmp_in, sign, scal, at0, nb, ps):
+    def counting(src, tiles, ln, skip, inb, cn, cmp, cmp_in, sign, scal, at0, nb, parts):
         c, jk, cq, cs = "c" + cn, "jk", "cq" + cn, "cs" + cn
         start = [sum(w for w, s in tiles[:k]) for k in range(len(tiles))]
         slot = {m: (start[k], i) for k, (w, s) in enumerate(tiles) for i, m in enumerate(s)}
@@ -329,6 +330,9 @@ def rank_program(g, core, T, topo):
         def step(x, again):
             if x == "in":
                 tt(inside, (src("v", None), inb[0], inb[1], 1), A("hh", inb[0], inb[1]), cmp_in)
+            elif x == "fine":
+                at, i = slot[FINE]
+                tt(A(c, 4 * at + i, 4 * (at + 368), 4), A("dg", 32, 39), A("vv"), ALU.is_lt, off=A("off2", 32, 55))
             elif x == "row":
                 scan(A("ir", 0, n), inside, A("gm", 0, n), ALU.add, ALU.mult)
             elif x == "base":
@@ -337,28 +341,32 @@ def rank_program(g, core, T, topo):
                 tt(A("md", 15, 16 * nb, 16), A("bb", at0, at0 + nb), A("rsum", at0, at0 + nb), ALU.subtract)
             elif isinstance(x, tuple):
                 at, last = start[x[0]], tiles[x[-1]]
-                end = start[x[-1]] + (max(ln[m] for m in last[1]) if again and x[-1] == len(tiles) - 1 else last[0])
+                end = start[x[-1]] + (max(ln[m] for m in last[1]) if again and len(x) > 1 else last[0])
                 quant(A(cq, at, end), A(cs, at, end), A(c, 4 * at, 4 * end))
                 for k in x:
-                    at, w, z = start[k], tiles[k][0], 128 * (None in tiles[k][1])
-                    if w > 16 * nb:
-                        wide = [y for y in closes if tiles[y][0] > 16 * nb]
-                        mm(A("ps0", 0, w - UP0), A("wcq", 0, 128), A("wcs", 0, 128), A(cq, at + UP0, at + w), A(cs, at + UP0, at + w),
-                           k == wide[0], k == wide[-1])
-                        w = 16 * nb
-                    mm(A(ps, 0, w), A("wcq", z, z + 128), A("wcs", z, z + 128), A(cq, at, at + w), A(cs, at, at + w),
-                       k == closes[0], k == closes[-1])
+                    at, z = start[k], 128 * (None in tiles[k][1])
+                    if COARSE in tiles[k][1]:
+                        mm(A("ps2", 0, 368), half("wcq", 2), half("wcs", 2), A(cq, at, at + 368), A(cs, at, at + 368))
+                    for bank, first, bottom, top in parts:
+                        wide, w = [y for y in closes if tiles[y][0] > bottom], min(tiles[k][0], top)
+                        if k in wide:
+                            mm(A(bank, 0, w - first), A("wcq", z, z + 128), A("wcs", z, z + 128), A(cq, at + first, at + w),
+                               A(cs, at + first, at + w), k == wide[0], k == wide[-1])
             else:
-                m = abs(x) % 100
+                m, lo = abs(x) % 100, skip if again else 0
                 at, i = slot[m]
                 v = A(c, 4 * (at + lo) + i, 4 * (at + ln[m]), 4)
                 if x < 0:
                     act((jk,) + v[1:], (src("s", m), lo, ln[m], 1), ACT.Sign, scale=-1.0, bias=scal(m))
+                elif x > 400:
+                    act((jk,) + v[1:], v, ACT.Copy, acc=col("rsum", at0 + m))
                 elif x > 300:
                     r = col("rsum", at0 + m)
                     op("v", lambda: V.tensor_reduce(ap(r), ap(v), AxisListType.X, ALU.add), [v], [r])
                 elif 100 < x < 200:
                     act(v, (jk,) + v[1:], ACT.Relu, scale=sign, acc=col("rsum", at0 + m))
+                elif m == COARSE:
+                    ts(v, (src("v", m), lo, ln[m], 1), scal(m), cmp, float(RUN), ALU.mult)
                 else:
                     ts(v, (src("v", m), lo, ln[m], 1), scal(m), cmp)
                     if x < 100:
@@ -366,9 +374,9 @@ def rank_program(g, core, T, topo):
         return step
 
     order1 = counting(lambda q, m: ("ps4" if q == "v" else "ps5") if m is not None and m <= 8 else ("ps2" if q == "v" else "ps3"),
-                      TILES1, LEN1, 0, (0, C), "1", ALU.is_lt, ALU.is_le, 1.0, lambda m: col("hh", 16 * m + 15), 0, 16, "ps0")
+                      TILES1, LEN1, 0, (0, C), "1", ALU.is_lt, ALU.is_le, 1.0, lambda m: col("hh", 16 * m + 15), 0, 16, [("ps0", 0, 0, C)])
     order2 = counting(lambda q, m: "vv", TILES2, LEN2, SPARE, (48, 272), "2", ALU.is_gt, ALU.is_ge, -1.0,
-                      lambda m: col("dg", m) if m >= 17 else col("hh", 16 * m + 15), 16, UP // 16, "ps1")
+                      lambda m: col("dg", m) if m >= 17 else col("hh", 16 * m + 15), 16, PARTS[-1][3] // 16, PARTS)
 
     def scores(t, h):
         if h:
@@ -385,8 +393,9 @@ def rank_program(g, core, T, topo):
     quant(half("tq0", 0), half("ts0", 0), half("tt", 0, 512))
     scores(0, 0)
     quant(half("tq0", 1), half("ts0", 1), half("tt", 1, 512))
+    quant(A("wcq", 0, 256), A("wcs", 0, 256), A("wt", 0, 1024))
     own(0, 0)
-    ts(A("cb", 0, 16), A("crow", 0, 16), m15, ALU.add, -3 * SMALL, ALU.add)
+    ts(A("cb", 0, 16), A("crow", 0, 16), m15, ALU.add)
 
     for t in range(R):
         tq, tsc, lq, ls = A("tq%d" % t), A("ts%d" % t), A("lq%d" % t), A("ls%d" % t)
@@ -421,28 +430,27 @@ def rank_program(g, core, T, topo):
             send(peer[t], ls, tsc, "at%d" % t)
         if t == 0:
             own(0, 1)
+            cp(A("l16", 8, 16), A("l32", 8, 16))
             runs, at, i = [], SPARE, K - 1
-            while i >= 0:
+            while i > 0:
                 n = len([r for r in range(K) if ROWS[r] == ROWS[i]])
                 runs.append((A("p0", at, at + n * ROWS[i]), [[128, n], [1, ROWS[i]]], 128 * (K - 1 - i) + K - ROWS[i]))
                 at, i = at + n * ROWS[i], i - n
-            iota(A("crow", 16, 45), [[16, 29]], 1 - NP)
             for r in runs:
                 if r[0][1] < NV:
                     iota(*r)
         nv = (NV - NV0) // 16
         aside = [] if t else [
-            lambda: ts(A("et", 3, 515, 4), A("cidx", 0, 128), pc, ALU.is_equal),
-            lambda: ts(A("cb", 16, 45), A("crow", 16, 45), m15, ALU.add, -3 * SMALL, ALU.add),
-            lambda: cp(A("bb", 16, 45), A("cb", 16, 45)),
+            lambda: ts(half("pm", 1, K), A("cidx", 0, K), ends, ALU.is_equal),
+            lambda: None,
             lambda: scan(A("xm", NV0, NV), A("p0", NV0, NV), A("mst", 0, NV - NV0), ALU.max, ALU.add),
-            lambda: ts(A("ijl", 0, nv), A("xm", NV0 + 15, NV, 16), OFF - 48, ALU.add, 1.0 / 128, ALU.mult),
             lambda: ts(A("x32", 0, nv), A("xm", NV0 + 15, NV, 16), OFF, ALU.add),
             lambda: ts(A("x32", 16, 16 + nv), A("x32", 0, nv), 127, ALU.bitwise_and),
+            lambda: ts(A("ijl", 0, nv), A("xm", NV0 + 15, NV, 16), OFF - 48, ALU.add, 1.0 / 128, ALU.mult),
             lambda: cp(A("ijl", 16, 16 + nv), A("x32", 16, 16 + nv)),
-            lambda: ts(A("cb", 19, 33), A("cb", 19, 33), nk, ALU.add, 15.0, ALU.add),
-            lambda: ts(A("cb", 19, 33), A("cb", 19, 33), nk, ALU.add),
-        ] + [lambda b=b: quant(half("eq", b), half("es", b), A("et", 3 - b, 515 - b)) for b in range(4)]
+            lambda: lists[3](),
+            lambda: quant(half("wcq", 2), half("wcs", 2), half("wt", 2, 512)),
+        ] + [lambda b=b: (quant(half("eq", b), half("es", b), A("et", 3 - b, 515 - b)), unpack((b,))) for b in range(4)]
 
         def spare(n=1):
             for f in aside[:n]:
@@ -452,7 +460,7 @@ def rank_program(g, core, T, topo):
         def masks():
             if t == 0:
                 act(A("mst", 0, C), A("sq", 0, C), ACT.Identity, scale=-BIG / 8, bias=9 * BIG / 8)
-                act(A("pm"), A("oh", 0, K), ACT.Identity, scale=2e29, bias=-1e29)
+                act(A("pm", 0, K), A("oh", 0, K), ACT.Identity, scale=2e29, bias=-1e29)
                 act(A("mst", 15, C, 16), A("mst", 15, C, 16), ACT.Identity, bias=-BIG - OFF)
 
         steps = ORDER1 if t else [-ORDER1[0]] + ORDER1[2:]
@@ -466,15 +474,20 @@ def rank_program(g, core, T, topo):
         spare()
         if t == 0:
             partner_u()
+            iota(A("crow", 16, 45), [[16, 29]], 1 - NP)
         mm(A("ps1", 0, C), up[0], up[1], lq, ls)
         if t > 0:
             unpack(range(4))
         else:
-            act(half("fl", 6), A("sq", 0, 128), ACT.Identity, scale=-16.0, bias=144.0)
-        act(A("prep", 0, C), A("cidx"), ACT.Identity, scale=0.0, bias=GAP if t < R - 1 else 0.0)
-        if t == 0:
-            act(A("fl", 3 * C + 15, 896, 16), A("fl", 3 * C + 15, 896, 16), ACT.Identity, bias=GAP - OFF - 128)
+            act(A("fl", 768), A("sq"), ACT.Identity, scale=-16.0, bias=144.0)
+        act(A("prep", 0, C), A("cidx"), ACT.Identity, scale=0.0, bias=GAP)
         act(A("spb"), A("ps1", 0, C), ACT.Copy)
+        if t == 0:
+            act(A("fl", 768 + 15, None, 16), A("fl", 768 + 15, None, 16), ACT.Identity, bias=GAP - OFF - 128)
+            for a, scale, bias in ((fin, -1.0, -2 * SMALL), (turn, -2.0, 15.0)):
+                act(a, kc, ACT.Identity, scale=scale, bias=bias)
+            for a, bias in ((A("vv", 0, SPARE), -1e29), (col("dg", 38), 1e29)):
+                act(a, A("zero", 0, a[2] - a[1]), ACT.Identity, bias=bias)
         early, mid, late = ((), (), range(4)) if t == 0 else ((), (0,), (1, 2, 3)) if t == far else ((0, 1), (2,), (3,))
         halve(early)
         scatter(A("orep"), of, A("cidx"))
@@ -486,27 +499,35 @@ def rank_program(g, core, T, topo):
         act(A("ss", 0, K), A("ssb"), ACT.Copy, off=ol)
         spare()
         if t == 0:
+            op("g", lambda: g.affine_select(ap(half("wt", 2, 512)), ap(half("wt", 0, 512)), [[0, 128], [1, 4]], ALU.is_equal, 0.0, -3, 0),
+               [half("wt", 0, 512)], [half("wt", 2, 512)])
+            op("g", lambda: g.affine_select(ap(A("et")), ap(A("wt", 0, 520)), [[1, 520]], ALU.is_equal, 0.0, -3, -4), [A("wt", 0, 520)], [A("et")])
             for r in runs:
                 if r[0][1] >= NV:
                     iota(*r)
             iota(A("p0", 0, SPARE), [[0, SPARE]], 0)
-            iota(A("nn"), [[-16384, NP]], 16384 * (NP - 1))
-        aside.extend([lambda b=b: ts(A("o4", 6 * b, 6 * b + 6), ol, 4.0, ALU.mult, float(b), ALU.add) for b in range(4)])
+        lists = [lambda b=b: ts(A("o4", 6 * b, 6 * b + 6), ol, 4.0, ALU.mult, float(b), ALU.add) for b in range(4)]
+        aside.extend(lists if t else [])
         act(A("si", NV0, NV), A("ss", 0, K), ACT.Copy, off=A("ijl", 0, nv))
         if t == 0:
-            for b in range(4):
-                aside.pop()()
-            act(A("ap"), A("tt"), ACT.Copy, off=A("o4"), scale=0.5)
+            for f in lists[:3]:
+                f()
+            act(A("pm", K), A("pm", K), ACT.Identity, scale=2e29, bias=-1e29)
+            act(A("bb", 16, 45), A("crow", 16, 45), ACT.Identity, bias=m15)
         halve(mid)
         if t == 1:
-            quant(A("vq"), A("vs"), A("vt"))
-        if t == R - 1:
-            act(A("mst", 15, C, 16), A("mst", 15, C, 16), ACT.Identity, bias=OFF - 2 * BIG)
-            ts(col("pcol", 4), col("pcol", 2), 1, ALU.bitwise_and)
-            aside[:0] = [lambda e=e: ts(col("fcol", 8 + e), col("pcol", 4), float(e), ALU.is_equal) for e in range(2)]
+            i = K - 1
+            while i >= 0:
+                n = len([r for r in range(K) if ROWS[r] == ROWS[i]])
+                iota(A("nn", K - 1 - i, K - 1 - i + n), [[-ROWS[i], n]], sum(ROWS[:i]) + K - 1)
+                i -= n
+        if t == 0:
+            act(A("cb", 19, 33), A("bb", 19, 33), ACT.Identity, bias=turn)
+        act(col("ss", K), col("ss", K - 1), ACT.Identity, bias=few)
+        act(col("ss", K + 1), col("ss", K - 1), ACT.Identity, bias=none)
         scatter(A("ee"), af, A("spb"))
         spare()
-        scan(A("hh", 368, NP), A("pm"), A("ee", C - K, C), ALU.max, ALU.min)
+        scan(A("hh", 368, NP), half("pm", 0, K), A("ee", C - K, C), ALU.max, ALU.min)
         at = 368
         rows = []
         for i in range(1, K):
@@ -523,64 +544,66 @@ def rank_program(g, core, T, topo):
             for i, m0, m1 in which:
                 act(A("dg", m0, m1), A("hh", NP - 1 - 16 * (m1 - m0 - 1), NP, 16), ACT.Identity, bias=col("ss", K - 1 - i))
 
-        rows_own([(0, 23, 29)])
-        spare()
+        def place(k, i):
+            bank, first, a, b = PARTS[k]
+            off = A("off2", a // 16 + (a > 0), b // 16 + (a > 0))
+            if i == 0:
+                tt(A("md", a + 15, b, 16), A("bb", 16 + a // 16, 16 + b // 16), A("rsum", 16 + a // 16, 16 + b // 16), ALU.subtract)
+            elif i == 1:
+                scan(A("sc", a, b), A(bank, a - first, b - first), A("md", a, b), ALU.max, ALU.add)
+            elif i == 2:
+                ts(off, A("sc", a + 15, b, 16), -1.0, ALU.mult, fin, ALU.add)
+            else:
+                scatter(A("prep"), off, A("p0", a, b))
+
+        def rows():
+            rows_own([(2, 18, 20), (3, 17, 18)])
+            act(A("dg", 32, 38), A("hh", 368 + RUN - 1, NP, RUN), ACT.Identity, bias=col("ss", K))
+
+        rows_own([(1, 20, 23)])
+        scan(A("sc", 368, NP), half("pm", 1, K), A("ee", C - K, C), ALU.max, ALU.min)
+        if t == 0:
+            op("y", lambda: [g.sync.dma_start(u8(A("wq")), T.wc[:]), g.sync.dma_start(ap(A("wp")), T.ws[:])], [A("ee")], [A("wq"), A("wp")], sem="dw")
+            op("y", lambda: [g.sync.dma_start(ap(A("vt")), T.v[:])], [], [A("vt")], sem="dv")
         tt(A("xm", 48, 272), A("vv", 48, 272), A("oh", 0, 224), ALU.mult)
         run(ORDER2, order2, {
             "carry": lambda: scan(A("hh", 48, 272), A("rs", 0, 224), A("xm", 48, 272), ALU.mult, ALU.add),
             "spare": lambda: spare(t == 0),
-            "rows": lambda: rows_own([(1, 20, 23), (2, 18, 20), (3, 17, 18)]),
-            "up0": lambda: tt(A("md", UP + 15, 368, 16), A("bb", 33, 39), A("rsum", 33, 39), ALU.subtract),
-            "up1": lambda: scan(A("sc", UP, 368), A("ps0", UP - UP0, 368 - UP0), A("md", UP, 368), ALU.max, ALU.add),
-            "up2": lambda: ts(A("off2", 18, 24), A("sc", UP + 15, 368, 16), -1.0, ALU.mult, fin, ALU.add),
-            "up3": lambda: scatter(A("prep"), A("off2", 18, 24), A("p0", UP, 368))})
+            "rows": rows,
+            "ends": lambda: act(col("dg", COARSE), col("sc", NP - 1), ACT.Identity, bias=col("ss", K + 1)),
+            "runs": lambda: scan(A("sc", 0, 368), A("ps2", 0, 368), A("fl", 768), ALU.max, ALU.add),
+            "list": lambda: ts(A("off2", 32, 55), A("sc", 15, 368, 16), OFF - GAP, ALU.add, 1.0 / RUN, ALU.mult),
+            **{"up%d" % i: lambda i=i: place(0, i) for i in range(4)}})
         spare()
-        scan(A("sc", 0, UP), A("ps1", 0, UP), A("md", 0, UP), ALU.max, ALU.add)
+        place(1, 1)
         spare()
-        ts(A("off2", 0, 17), A("sc", 15, UP, 16), -1.0, ALU.mult, fin, ALU.add)
+        place(1, 2)
         spare(len(aside))
         if t == 0:
-            unpack(range(4))
+            act(A("ap"), A("tt"), ACT.Copy, off=A("o4"), scale=0.5)
         halve(late)
         if t > 0:
             arrived((0,))
             act(A("ap"), A("tt"), ACT.Copy, off=A("o4"), scale=0.5)
             arrived((1,))
-        scatter(A("prep"), A("off2", 0, 17), A("p0", 0, UP))
-        if t == R - 2:
-            op("g", lambda: [g.dma_start(ap(A("p0")), ap(A("nn")), accum_op=ALU.add)], [A("nn")], [A("p0")], sem="dn")
-        last = t == R - 1
+        place(1, 3)
+        act(half("fl", 1), half("prep", 1), ACT.Relu, bias=1.0 - GAP)
         arrived((2, 3) if t else range(4))
+        ts(half("fl", 0), half("prep", 0), GAP, ALU.is_equal)
 
         def every(name, a):
             return A(name, a + 15, a + 128, 16)
 
         chain = [
-            lambda h: ts(half("fl", h), half("prep", h), 0.0 if last else GAP, ALU.is_equal),
             lambda h: scan(half("sc", h), half("prep", h), half("mst", h), ALU.max, ALU.add),
             lambda h: scan(half("fl", 2 + h), A("zero", 0, 128), half("fl", h), ALU.add, ALU.subtract, col("fl", C + 127) if h else 0.0),
             lambda h: scan(half("fl", 4 + h), half("fl", 2 + h), half("fl", 6), ALU.max, ALU.add, GAP - OFF),
-        ]
-        if last:
-            chain += [
-                lambda h: ts(half("xm", h, 8), every("fl", 512 + 128 * h), -16383.0, ALU.mult, GAP - 16384 - 16383 * (OFF - GAP) - 2 * BIG, ALU.add),
-                lambda h: tt(half("x32", h, 8), every("sc", 128 * h), half("xm", h, 8), ALU.max),
-                lambda h: ts(half("x32", 2 + h, 8), half("x32", h, 8), 7, ALU.arith_shift_right, 127, ALU.bitwise_and),
-                lambda h: cp(half("il", h, 8), half("x32", 2 + h, 8))]
-        else:
-            chain += [
-                lambda h: tt(half("x32", h, 8), every("sc", 128 * h), every("fl", 512 + 128 * h), ALU.min),
-                lambda h: ts(half("il", h, 8), half("x32", h, 8), OFF - 48, ALU.add, 1.0 / 128, ALU.mult)]
-        chain += [lambda h: ts(half("x32", 4 + h, 8), half("x32", h, 8), 127, ALU.bitwise_and),
-                  lambda h: cp(half("jl", h, 8), half("x32", 4 + h, 8))]
-        chain[0](0)
-        chain[1](0)
-        for i in range(2, len(chain)):
-            chain[i](0)
-            chain[i - 2](1)
-        chain[-2](1)
-        if last:
-            ts(A("x32", 48, 64), A("x32", 0, 16), 14, ALU.arith_shift_right)
+            lambda h: tt(half("x32", h, 8), every("sc", 128 * h), every("fl", 512 + 128 * h), ALU.min),
+            lambda h: ts(half("il", h, 8), half("x32", h, 8), OFF - 48, ALU.add, 1.0 / 128, ALU.mult),
+            lambda h: ts(half("x32", 4 + h, 8), half("x32", h, 8), 127, ALU.bitwise_and),
+            lambda h: cp(half("jl", h, 8), half("x32", 4 + h, 8))]
+        for i, h in ((0, 0), (1, 0), (0, 1), (2, 0), (1, 1), (3, 0), (2, 1), (4, 0), (5, 0), (3, 1), (6, 0), (5, 1), (4, 1), (6, 1)):
+            chain[i](h)
         nq, ns = ("tq%d" % (t + 1), "ts%d" % (t + 1)) if t < R - 1 else ("fq", "fs")
 
         def layer(h):
@@ -605,15 +628,8 @@ def rank_program(g, core, T, topo):
             tt(A("zz", 512 * h + b, 512 * h + 512, 4), half("ep", b, K), half("ag", k), ALU.add, off=half("jl", h, 8))
             if k == 4:
                 layer(0)
-            if k == 0:
-                chain[-1](1)
-            if last and k < 2:
-                ts(half("nb", k, 16), A("x32", 48, 64), 2 * BIG / 16384, ALU.add, col("fcol", 8 + k), ALU.mult)
-            if last and k == 2:
-                op("v", lambda: V.transpose(ap(A("nb", 32, 64)), ap(A("nb", 0, 32))), [A("nb", 0, 32)], [A("nb", 32, 64)])
-            if last and k == 3:
-                tt(A("nb", 64, 80), A("nb", 32, 48), A("nb", 48, 64), ALU.add)
-                op("y", lambda: [g.sync.dma_start(T.ol[:], ap(A("nb", 64, 80)))], [A("nb", 64, 80)], [], sem="do")
+            if k == 7 and t == 1:
+                quant(A("vq"), A("vs"), A("vt"))
         for k in range(8):
             h, b = k // 4, k % 4
             if k == 0:
@@ -622,15 +638,22 @@ def rank_program(g, core, T, topo):
             tt(A("tt", 512 * h + b, 512 * h + 512, 4), half("rl", k), A("zz", 512 * h + b, 512 * h + 512, 4), ALU.add)
             if k == 4:
                 state(0)
-            if k in (6, 7) and t < R - 1:
-                own(0, k - 6)
+            if k == 7 and t < R - 1:
+                own(0, 0)
         if t == R - 1:
+            act(half("nb", 0, C), A("nn"), ACT.Copy, off=A("il"))
+            act(half("nb", 1, C), A("cidx", 0, K), ACT.Copy, off=A("jl"))
             act(half("ysb", 0), A("ps4", 0, 128), ACT.Copy)
-            op("s", lambda: [g.scalar.dma_start(T.y[:, 0:128], ap(half("ysb", 0)))], [half("ysb", 0)], [], sem="dy")
+            op("y", lambda: [g.sync.dma_start(T.y[:, 0:128], ap(half("ysb", 0)))], [half("ysb", 0)], [], sem="dr")
         state(1)
+        if t < R - 1:
+            own(0, 1)
 
+    tt(half("nb", 2, C), half("nb", 0, C), half("nb", 1, C), ALU.subtract)
+    op("s", lambda: [g.scalar.dma_start(T.osc[4 * k:4 * k + 4, :], T.fs[32 * k:32 * k + 4, :]) for k in (2, 3)], [A("fs")], [], sem="dy")
     act(half("ysb", 1), A("ps5", 0, 128), ACT.Copy)
-    op("y", lambda: [g.sync.dma_start(T.osc[4 * k:4 * k + 4, :], T.fs[32 * k:32 * k + 4, :]) for k in range(4)], [A("fs")], [], sem="dq")
+    op("y", lambda: [g.sync.dma_start(T.osc[4 * k:4 * k + 4, :], T.fs[32 * k:32 * k + 4, :]) for k in (0, 1)], [A("fs")], [], sem="dq")
+    op("y", lambda: [g.sync.dma_start(T.ol[:], T.nb[0:128:16, 2 * C:3 * C])], [half("nb", 2, C)], [], sem="do")
     op("s", lambda: [g.scalar.dma_start(T.y[:, 128:256], ap(half("ysb", 1)))], [half("ysb", 1)], [], sem="dy")
     for s in count:
         g.wait_ge(T.sem[s], count[s])

from concourse.bass import DstId, RemoteDMATransfer
from concourse.mybir import dt, AluOpType, ActivationFunctionType, AxisListType

C, K, R = 256, 96, 3
STEP = [1, 2, 4]
ROWS = [K // (i + 1) for i in range(K)]
NP = 464
NV0, NV = 48, 256
PARTS = [("ps0", 240, 272, 368), ("ps1", 0, 0, 272)]
F32, BF, I32, U16, X4, U8 = "float32", "bfloat16", "int32", "uint16", "float8_e4m3fn_x4", "uint8"
BIG, SMALL = float(2 ** 23), 4096.0
GAP = 128.0 * (K - 1) + K
OFF = GAP + 160

SPARE = NP - sum(ROWS)
LEN2 = {m: 16 * m for m in range(3, 17)}
LEN2.update({17: 264, 18: 288, 19: 288, 20: 320, 21: 320, 22: 320})
COARSE, FINE, RUN = 23, 24, 16
LEN2.update({COARSE: 368, FINE: 368})
TILES1 = [(256, [13, 14, 15, None]), (192, [9, 10, 11, 12]), (128, [5, 6, 7, 8]), (128, [1, 2, 3, 4])]
TILES2 = [(368, [20, 21, 22, COARSE]), (368, [17, 18, 19, FINE]), (272, [14, 15, 16, None]),
          (208, [10, 11, 12, 13]), (144, [6, 7, 8, 9]), (128, [3, 4, 5])]
LEN1 = {m: 16 * m for m in range(1, 16)}
ORDER1 = [-5, 105, 4, 3, 2, 201, "mask", 7, "carry", 6, 301, -12, 15, 112, 14, 13, "in", 8, (0,), 11, (2, 3), 10, 9, "row", (1,), "masks",
          "base", "partner", "sum"]
ORDER2 = [-22, "ends", -21, 122, 121, "rows", 20, "carry", COARSE, -19, -18, 119, 118, -17, -16, 117, 116, "spare", 15, 14, (0,), 13, 12, 11, 10, "in",
          "runs", 9, "list", 8, "fine", (3,), 7, (1,), 6, 5, "up0", 4, (2,), 203, "up1", "row", "up2", 303, (4, 5), "base", "up3",
          "spare", "spare", "sum"]
W1 = sum(w for w, s in TILES1)
W2 = sum(w for w, s in TILES2)

SCRATCH = {}
for _n, _w, _d in [
    ("tt", 1024, BF), ("zz", 1024, BF), ("ut", 512, BF), ("vt", 512, BF),
    ("uq", 128, X4), ("us", 128, U8), ("vq", 128, X4), ("vs", 128, U8), ("wq", 512, X4), ("wp", 512, U8),
    ("urq", 128, X4), ("urs", 128, U8), ("ucq", 16, X4), ("ucs", 16, U8),
    ("ruq", 8, X4), ("rus", 8, U8), ("rtq", 128, X4), ("rts", 128, U8),
    ("zq", 256, X4), ("zs", 256, U8), ("fq", 256, X4), ("fs", 256, U8),
    ("pcol", 8, I32), ("fcol", 11, F32), ("l32", 18, I32), ("l16", 18, U16),
    ("rr", 368, BF), ("oh", 256, BF), ("sg", 368, BF), ("sq", 368, BF), ("gm", 256, BF), ("rs", 256, BF), ("mst", 256, F32), ("md", NP, F32), ("fl", 768 + 368, BF),
    ("gi", 128, BF), ("wt", 1536, BF), ("wcq", 384, X4), ("wcs", 384, U8),
    ("et", 520, BF), ("eq", 512, X4), ("es", 512, U8), ("zero", 520, BF),
    ("cidx", 256, F32), ("crow", 48, F32), ("cb", 48, F32), ("bb", 48, F32), ("rsum", 48, F32), ("dg", 49, F32),
    ("p0", 368, F32), ("nn", K, F32), ("ijl", 32, U16),
    ("c1", 4 * W1, BF), ("c2", 4 * W2, BF), ("jk", 4 * W2, BF), ("pm", 2 * K, BF),
    ("cq1", W1, X4), ("cs1", W1, U8), ("cq2", W2, X4), ("cs2", W2, U8),
    ("ssb", 256, F32), ("spb", 256, F32), ("xm", NP, F32), ("hh", NP, F32), ("ir", 256, BF), ("sc", NP, F32),
    ("off2", 56, U16), ("orep", 256, F32), ("prep", NP, F32), ("o4", 24, U16),
    ("ss", 112, F32), ("ee", 256, F32), ("si", NV, F32), ("vv", 368, F32),
    ("ap", 384, BF), ("ep", 384, BF), ("dp", 1024, BF), ("ag", 1024, BF), ("rl", 1024, F32),
    ("x32", 64, I32), ("il", 16, U16), ("jl", 16, U16), ("nb", 768, F32), ("ysb", 256, F32),
]:
    SCRATCH[_n] = ("sbuf", [128, _w], _d)
for _t in range(R):
    for _n, _w, _d in [("tq", 256, X4), ("ts", 256, U8), ("lq", 256, X4), ("ls", 256, U8), ("ol", 6, U16), ("al", 6, U16),
                       ("of", 16, U16), ("af", 16, U16), ("ulq", 8, X4), ("uls", 8, U8), ("upq", 128, X4), ("ups", 128, U8)]:
        SCRATCH[_n + str(_t)] = ("sbuf", [128, _w], _d)
for _t in range(8):
    SCRATCH["ps%d" % _t] = ("psum", [128, 512], F32)

SEMAPHORES = (["qv", "qs", "qt", "qg", "dx0", "dx1", "du", "dv", "dw", "dz", "dq", "dr", "dy", "do", "loc", "ru", "rt"]
              + ["%s%d" % (a, t) for a in ("au", "at", "al", "af") for t in range(R)])


def A(name, a=None, b=None, s=1):
    n = SCRATCH[name][1][1]
    return (name, 0 if a is None else a, n if b is None else b, s)


def col(name, j):
    return (name, j, j + 1, 1)


def half(name, h, w=128):
    return A(name, w * h, w * h + w)


def helper(core, T, topo):
    mine = [c for c in topo.cores_of(core) if T.rank_of(c) is not None]
    free = [c for c in topo.cores_of(core) if T.rank_of(c) is None and topo.die(c) != topo.die(core)]
    return free[mine.index(core)]


def far_round(rank, T, topo):
    return [t for t in range(R) if topo.chip(T.cores[rank ^ STEP[t]]) != topo.chip(T.cores[rank])][0]


def hand_on(g, core, T, topo):
    for r, c in enumerate(T.cores):
        if helper(c, T, topo) != core:
            continue
        t = far_round(r, T, topo)
        dst = T.cores[r ^ STEP[t]]
        rid, pid, se = topo.addr(dst)
        m, n = topo.mask(core, dst), len(topo.engines(core, dst))
        g.wait_ge(T.sem.ru, 8)
        g.remote_dma(T["ulq%d" % t][:].bitcast(dt.uint8), T.ruq[:].bitcast(dt.uint8), T.sem["au%d" % t], T.sem.loc, pid, rid, m)
        g.remote_dma(T["uls%d" % t][:], T.rus[:], T.sem["au%d" % t], T.sem.loc, pid, rid, m)
        g.wait_ge(T.sem.rt, 2 * len(topo.engines(c, core)))
        g.remote_dma(T["lq%d" % t][:, 0:128].bitcast(dt.uint8), T.rtq[:].bitcast(dt.uint8), T.sem["at%d" % t], T.sem.loc, pid, rid, m)
        g.remote_dma(T["ls%d" % t][:, 0:128], T.rts[:], T.sem["at%d" % t], T.sem.loc, pid, rid, m)
        g.wait_ge(T.sem.loc, 4 * n)


def rank_program(g, core, T, topo):
    rank = T.rank_of(core)
    if rank is None:
        hand_on(g, core, T, topo)
        return
    ALU, ACT = AluOpType, ActivationFunctionType
    Q = {"v": g.vector, "s": g.scalar, "t": g.tensor, "g": g, "y": g.sync}
    count = {}
    known = {q: 0 for q in Q}
    done = {q: 0 for q in Q}
    ops = []
    hist = {}

    def ap(a):
        return T[a[0]][:, a[1]:a[2]:a[3]] if a[3] != 1 else T[a[0]][:, a[1]:a[2]]

    def bits(a):
        if a[0].startswith("ps"):
            return 1
        m = 0
        for c in range(a[1], a[2], a[3]):
            m |= 1 << c
        return m

    def op(q, fn, reads, writes, sem=None, acc=False):
        deps = set()
        touched = [(a, False) for a in reads] + [(a, True) for a in writes]
        for a, w in touched:
            m, bank = bits(a), a[0].startswith("ps")
            for hm, i, hw, hq in hist.get(a[0], []):
                if hm & m and (w or hw or (bank and hq != q)) and not (acc and bank and hq == q):
                    deps.add(i)
        for i in sorted(deps, reverse=True):
            if not known[q] >> i & 1:
                Q[q].wait_ge(T.sem[ops[i][0]], ops[i][1])
                known[q] |= ops[i][2]
        me = len(ops)
        if sem == "remote":
            count["loc"] = count.get("loc", 0) + fn()
            ops.append(("loc", None, 0))
            return
        if sem is None:
            s = "q" + q
            fn().then_inc(T.sem[s], 1)
            count[s] = count.get(s, 0) + 1
            done[q] |= 1 << me
            ops.append((s, count[s], known[q] | done[q]))
        else:
            for ins in fn():
                ins.then_inc(T.sem[sem], 16)
                count[sem] = count.get(sem, 0) + 16
            ops.append((sem, count[sem], known[q] | 1 << me))
        for a, w in touched:
            h = hist.setdefault(a[0], [])
            m = bits(a)
            if w:
                h[:] = [e for e in h if e[0] & ~m]
            h.append((m, me, w, q))

    def arrive(sem, n, writes):
        me = len(ops)
        count[sem] = n
        ops.append((sem, n, 1 << me))
        for a in writes:
            hist.setdefault(a[0], []).append((bits(a), me, True, None))

    V = g.vector

    def isap(x):
        return isinstance(x, tuple)

    def ts(out, in0, s1, op0, s2=None, op1=None):
        x1 = ap(s1) if isap(s1) else s1
        x2 = ap(s2) if isap(s2) else s2
        rd = [in0] + [s for s in (s1, s2) if isap(s)]
        if op1 is None:
            op("v", lambda: V.tensor_scalar(ap(out), ap(in0), x1, None, op0), rd, [out])
        else:
            op("v", lambda: V.tensor_scalar(ap(out), ap(in0), x1, x2, op0, op1), rd, [out])

    def tt(out, in0, in1, o, off=None):
        a0 = ap(in0) if off is None else ap(in0).indirect(ap(off))
        op("v", lambda: V.tensor_tensor(ap(out), a0, ap(in1), o), [in0, in1] + ([off] if off else []), [out])

    def cp(out, in_):
        op("v", lambda: V.tensor_copy(ap(out), ap(in_)), [in_], [out])

    def scatter(win, off, in_):
        op("v", lambda: V.tensor_copy(ap(win).indirect(ap(off)), ap(in_)), [in_, off], [win])

    def pick(oq, os_, q, s, off):
        op("v", lambda: V.tensor_copy(ap(oq).bitcast(dt.uint32), ap(q).bitcast(dt.uint32).indirect(ap(off))), [q, off], [oq])
        op("s", lambda: g.scalar.activation(ap(os_), ap(s).indirect(ap(off)), ACT.Copy), [s, off], [os_])

    def scan(out, d0, d1, o0, o1, first=0.0):
        op("v", lambda: V.tensor_tensor_scan(ap(out), ap(d0), ap(d1), ap(first) if isap(first) else first, o0, o1),
           [d0, d1] + ([first] if isap(first) else []), [out])

    def fill(a, c):
        op("v", lambda: V.memset(ap(a), c), [], [a])

    def quant(q, s, in_):
        op("v", lambda: V.quantize_mx(ap(q), ap(s), ap(in_)), [in_], [q, s])

    def act(out, in_, f, off=None, acc=None, bias=None, scale=None):
        a0 = ap(in_) if off is None else ap(in_).indirect(ap(off))
        kw, rd = {}, [in_] + ([off] if off else [])
        if acc is not None:
            kw["accum_out"] = ap(acc)
        if bias is not None:
            kw["bias"] = ap(bias) if isap(bias) else bias
            rd += [bias] if isap(bias) else []
        if scale is not None:
            kw["scale"] = scale
        op("s", lambda: g.scalar.activation(ap(out), a0, f, **kw), rd, [out] + ([acc] if acc else []))

    def mm(out, lq, ls, rq, rs_, start=True, stop=True):
        op("t", lambda: g.tensor.matmul_mx(ap(out), ap(lq), ap(ls), ap(rq), ap(rs_), start, stop), [lq, ls, rq, rs_], [out], acc=not start)

    def iota(out, pattern, base, cm=0):
        if SCRATCH[out[0]][2] == I32:
            op("g", lambda: g.iota(ap(out), pattern, base, cm), [], [out])
        else:
            op("g", lambda: g.iota(ap(out), pattern, base, cm, allow_small_or_imprecise_dtypes=True), [], [out])

    def u8(a):
        return ap(a).bitcast(dt.uint8) if SCRATCH[a[0]][2] == X4 else ap(a)

    def send(dst, out, in_, sem):
        def fn():
            rid, pid, se = topo.addr(dst)
            g.remote_dma(u8(out), u8(in_), T.sem[sem], T.sem.loc, pid, rid, topo.mask(core, dst))
            return len(topo.engines(core, dst))
        op("g", fn, [in_], [], sem="remote")

    peer = [T.cores[rank ^ STEP[t]] for t in range(R)]
    far, aid = far_round(rank, T, topo), helper(core, T, topo)

    def send3(x, in_, shift):
        def fn():
            tr = []
            for t in range(R):
                dst, out, sem = (aid, "ru" + x, "ru") if t == far else (peer[t], "ul%s%d" % (x, t), "au%d" % t)
                es = topo.engines(core, dst)[4 * (t + shift):4 * (t + shift) + 4]
                rid, pid, se = topo.addr(dst)
                tr.append(RemoteDMATransfer(dst_ids=[DstId(rid=rid, pnc=pid)], dma_engine_mask=sum(1 << e for e in es),
                                            remote_sem=T.sem[sem], src=u8(in_), dst=u8(A(out))))
            g.remote_dma_fused(tr, local_sem=T.sem.loc)
            return 4 * R
        op("g", fn, [in_], [], sem="remote")

    for t in range(R):
        ne = len(topo.engines(peer[t], core))
        nh = len(topo.engines(helper(peer[t], T, topo), core)) if t == far else 0
        arrive("au%d" % t, 2 * nh if nh else 8, [A("ulq%d" % t), A("uls%d" % t)])
        arrive("at%d" % t, 2 * ne + 2 * nh, [A("lq%d" % t), A("ls%d" % t)])
        arrive("al%d" % t, ne, [A("al%d" % t)])
        arrive("af%d" % t, ne, [A("af%d" % t)])

    op("s", lambda: [g.scalar.dma_start(ap(A("ut")), T.u[:])], [], [A("ut")], sem="du")
    for h in range(2):
        op("y", lambda: [g.sync.dma_start(ap(half("tt", h, 512)), T.x[:, 512 * h:512 * h + 512])], [], [half("tt", h, 512)], sem="dx%d" % h)
    fill(A("zero"), 0.0)
    blank = {"c1": [], "c2": []}
    for name, tiles, ln, first, inb in (("c1", TILES1, LEN1, 0, 0), ("c2", TILES2, LEN2, 0, 48)):
        at = 0
        for w, slots in tiles:
            lo = min(ln[m] for m in slots if m is not None) if len(slots) == 4 else 0
            if lo < w:
                blank[name].append(A(name, 4 * (at + lo), 4 * (at + w)))
            head = inb if None in slots else first
            if head and lo:
                blank[name].append(A(name, 4 * at, 4 * (at + head)))
            at += w
    for a in blank["c1"]:
        act(a, A("zero", 0, a[2] - a[1]), ACT.Copy)
    op("y", lambda: [g.sync.dma_start(ap(a), ap(A("zero", 0, a[2] - a[1]))) for a in blank["c2"]], [A("zero")], blank["c2"], sem="dz")

    iota(col("pcol", 0), [[0, 1]], 0, 1)
    iota(A("l32", 0, 8), [[16, 8]], 0)
    iota(A("gi"), [[1, 8], [0, 16]], 0)
    iota(A("rr"), [[0, 23], [1, 16]], 0)
    kc, gc_, pc, fin, ends, finr, nk, m15 = (col("fcol", j) for j in range(8))
    few, turn, none = col("fcol", 8), col("fcol", 9), col("fcol", 10)
    ts(col("pcol", 1), col("pcol", 0), 15, ALU.bitwise_and)
    ts(col("pcol", 2), col("pcol", 0), 4, ALU.arith_shift_right)
    ts(col("pcol", 3), col("pcol", 0), 7, ALU.bitwise_and)
    cp(pc, col("pcol", 0))
    cp(A("fcol", 0, 2), A("pcol", 1, 3))
    ts(col("l16", 16), col("pcol", 3), 16.0, ALU.mult)
    cp(A("l16", 0, 8), A("l32", 0, 8))
    ts(m15, kc, 15.0, ALU.is_equal, SMALL, ALU.mult)
    for a, scale, bias in ((nk, -1.0, 0.0), (finr, 1.0, C - 1 - 2 * SMALL), (ends, float(RUN), RUN - 1.0)):
        ts(a, kc, scale, ALU.mult, bias, ALU.add)
    fill(A("rsum"), 0.0)
    ts(m15, m15, -3 * SMALL, ALU.add)
    for j in (3, 0, 1, 2, 4, 5, 6):
        ts(A("wt", 512 * (j // 4) + j % 4, 512 * (j // 4 + 1), 4), A("gi"), gc_, ALU.is_equal)
    op("g", lambda: g.affine_select(ap(A("wt", 515, 1024, 4)), ap(A("wt", 3, 512, 4)), [[1, 128]], ALU.is_gt, 0.0, 0, -1),
       [A("wt", 3, 512, 4)], [A("wt", 515, 1024, 4)])
    iota(A("l32", 8, 16), [[1, 8]], 0)
    iota(A("crow", 0, 16), [[16, 16]], 15)
    iota(A("cidx"), [[1, 256]], 0)
    act(A("rs", 0, 224), A("rr", 0, 224), ACT.Sign)
    ts(A("oh"), A("rr", 0, 256), kc, ALU.is_equal)
    quant(A("uq"), A("us"), A("ut"))
    ts(few, kc, RUN - 1.0, ALU.is_ge, 1e29, ALU.mult)
    ts(none, kc, float(K // RUN), ALU.is_ge, 1e29, ALU.mult)
    pick(A("urq"), A("urs"), A("uq"), A("us"), A("l16", 0, 8))
    pick(A("ucq"), A("ucs"), A("uq"), A("us"), A("l16", 16, 17))
    send3("q", A("ucq", 0, 8), 0)
    send3("s", A("ucs", 0, 8), 1)
    act(A("sg"), A("rr"), ACT.Sign, bias=nk)
    act(A("sq"), A("sg"), ACT.Square, scale=4.0, bias=-1.0)
    act(A("gm"), A("sg", 0, 256), ACT.Relu)
    act(A("md", 0, 368), A("sq"), ACT.Identity, scale=-SMALL / 8, bias=9 * SMALL / 8)

    def counting(src, tiles, ln, skip, inb, cn, cmp, cmp_in, sign, scal, at0, nb, parts):
        c, jk, cq, cs = "c" + cn, "jk", "cq" + cn, "cs" + cn
        start = [sum(w for w, s in tiles[:k]) for k in range(len(tiles))]
        slot = {m: (start[k], i) for k, (w, s) in enumerate(tiles) for i, m in enumerate(s)}
        closes = [k for x in (ORDER1 if cn == "1" else ORDER2) if isinstance(x, tuple) for k in x]
        n, b0 = inb[1] - inb[0], at0 + inb[0] // 16
        inside = A(c, 4 * (slot[None][0] + inb[0]) + slot[None][1], 4 * (slot[None][0] + inb[1]), 4)

        def step(x, again):
            if x == "in":
                tt(inside, (src("v", None), inb[0], inb[1], 1), A("hh", inb[0], inb[1]), cmp_in)
            elif x == "fine":
                at, i = slot[FINE]
                tt(A(c, 4 * at + i, 4 * (at + 368), 4), A("dg", 32, 39), A("vv"), ALU.is_lt, off=A("off2", 32, 55))
            elif x == "row":
                scan(A("ir", 0, n), inside, A("gm", 0, n), ALU.add, ALU.mult)
            elif x == "base":
                tt(A("bb", b0, b0 + n // 16), A("cb", b0, b0 + n // 16), A("ir", 15, n, 16), ALU.subtract)
            elif x == "sum":
                tt(A("md", 15, 16 * nb, 16), A("bb", at0, at0 + nb), A("rsum", at0, at0 + nb), ALU.subtract)
            elif isinstance(x, tuple):
                at, last = start[x[0]], tiles[x[-1]]
                end = start[x[-1]] + (max(ln[m] for m in last[1]) if again and len(x) > 1 else last[0])
                quant(A(cq, at, end), A(cs, at, end), A(c, 4 * at, 4 * end))
                for k in x:
                    at, z = start[k], 128 * (None in tiles[k][1])
                    if COARSE in tiles[k][1]:
                        mm(A("ps2", 0, 368), half("wcq", 2), half("wcs", 2), A(cq, at, at + 368), A(cs, at, at + 368))
                    for bank, first, bottom, top in parts:
                        wide, w = [y for y in closes if tiles[y][0] > bottom], min(tiles[k][0], top)
                        if k in wide:
                            mm(A(bank, 0, w - first), A("wcq", z, z + 128), A("wcs", z, z + 128), A(cq, at + first, at + w),
                               A(cs, at + first, at + w), k == wide[0], k == wide[-1])
            else:
                m, lo = abs(x) % 100, skip if again else 0
                at, i = slot[m]
                v = A(c, 4 * (at + lo) + i, 4 * (at + ln[m]), 4)
                if x < 0:
                    act((jk,) + v[1:], (src("s", m), lo, ln[m], 1), ACT.Sign, scale=-1.0, bias=scal(m))
                elif x > 400:
                    act((jk,) + v[1:], v, ACT.Copy, acc=col("rsum", at0 + m))
                elif x > 300:
                    r = col("rsum", at0 + m)
                    op("v", lambda: V.tensor_reduce(ap(r), ap(v), AxisListType.X, ALU.add), [v], [r])
                elif 100 < x < 200:
                    act(v, (jk,) + v[1:], ACT.Relu, scale=sign, acc=col("rsum", at0 + m))
                elif m == COARSE:
                    ts(v, (src("v", m), lo, ln[m], 1), scal(m), cmp, float(RUN), ALU.mult)
                else:
                    ts(v, (src("v", m), lo, ln[m], 1), scal(m), cmp)
                    if x < 100:
                        act((jk,) + v[1:], v, ACT.Copy, acc=col("rsum", at0 + m))
        return step

    order1 = counting(lambda q, m: ("ps4" if q == "v" else "ps5") if m is not None and m <= 8 else ("ps2" if q == "v" else "ps3"),
                      TILES1, LEN1, 0, (0, C), "1", ALU.is_lt, ALU.is_le, 1.0, lambda m: col("hh", 16 * m + 15), 0, 16, [("ps0", 0, 0, C)])
    order2 = counting(lambda q, m: "vv", TILES2, LEN2, SPARE, (48, 272), "2", ALU.is_gt, ALU.is_ge, -1.0,
                      lambda m: col("dg", m) if m >= 17 else col("hh", 16 * m + 15), 16, PARTS[-1][3] // 16, PARTS)

    def scores(t, h):
        if h:
            mm(A("ps6", 0, 128), A("urq"), A("urs"), half("tq%d" % t, 1), half("ts%d" % t, 1))
        for b in (4, 5) if h == 0 else (2, 3):
            mm(A("ps%d" % b, 0, 128 * (h + 1)), A("urq"), A("urs"), A("tq%d" % t, 0, 128 * (h + 1)), A("ts%d" % t, 0, 128 * (h + 1)))

    def own(h, x):
        if x == 0:
            tt(half("xm", h), A("ps6" if h else "ps4", 0, 128), A("oh", 0, 128), ALU.mult)
        else:
            scan(half("hh", h), A("rs", 0, 128), half("xm", h), ALU.mult, ALU.add)

    quant(half("tq0", 0), half("ts0", 0), half("tt", 0, 512))
    scores(0, 0)
    quant(half("tq0", 1), half("ts0", 1), half("tt", 1, 512))
    quant(A("wcq", 0, 256), A("wcs", 0, 256), A("wt", 0, 1024))
    own(0, 0)
    ts(A("cb", 0, 16), A("crow", 0, 16), m15, ALU.add)

    for t in range(R):
        tq, tsc, lq, ls = A("tq%d" % t), A("ts%d" % t), A("lq%d" % t), A("ls%d" % t)
        ol, al, of, af = A("ol%d" % t), A("al%d" % t), A("of%d" % t), A("af%d" % t)
        up = (A("upq%d" % t), A("ups%d" % t))

        def partner_u():
            pick(up[0], up[1], A("ulq%d" % t), A("uls%d" % t), A("l16", 8, 16))

        def unpack(which):
            for b in which:
                mm(A("ps%d" % (4 + b), 0, C), half("eq", b), half("es", b), lq, ls)

        def halve(which):
            for b in which:
                act(half("dp", b, C), A("ps%d" % (4 + b), 0, C), ACT.Copy, scale=0.5)

        def arrived(which):
            for b in which:
                act(half("ep", b, K), half("dp", b, C), ACT.Copy, off=al)

        def run(steps, one, more):
            for x in steps:
                more[x]() if x in more else one(x, t > 0)

        scores(t, 1)
        if t == far:
            send(peer[t], half(lq[0], 1), half(tq[0], 1), "at%d" % t)
            send(peer[t], half(ls[0], 1), half(tsc[0], 1), "at%d" % t)
        else:
            send(peer[t], lq, tq, "at%d" % t)
            send(peer[t], ls, tsc, "at%d" % t)
        if t == 0:
            own(0, 1)
            cp(A("l16", 8, 16), A("l32", 8, 16))
            runs, at, i = [], SPARE, K - 1
            while i > 0:
                n = len([r for r in range(K) if ROWS[r] == ROWS[i]])
                runs.append((A("p0", at, at + n * ROWS[i]), [[128, n], [1, ROWS[i]]], 128 * (K - 1 - i) + K - ROWS[i]))
                at, i = at + n * ROWS[i], i - n
            for r in runs:
                if r[0][1] < NV:
                    iota(*r)
        nv = (NV - NV0) // 16
        aside = [] if t else [
            lambda: ts(half("pm", 1, K), A("cidx", 0, K), ends, ALU.is_equal),
            lambda: None,
            lambda: scan(A("xm", NV0, NV), A("p0", NV0, NV), A("mst", 0, NV - NV0), ALU.max, ALU.add),
            lambda: ts(A("x32", 0, nv), A("xm", NV0 + 15, NV, 16), OFF, ALU.add),
            lambda: ts(A("x32", 16, 16 + nv), A("x32", 0, nv), 127, ALU.bitwise_and),
            lambda: ts(A("ijl", 0, nv), A("xm", NV0 + 15, NV, 16), OFF - 48, ALU.add, 1.0 / 128, ALU.mult),
            lambda: cp(A("ijl", 16, 16 + nv), A("x32", 16, 16 + nv)),
            lambda: lists[3](),
            lambda: quant(half("wcq", 2), half("wcs", 2), half("wt", 2, 512)),
        ] + [lambda b=b: (quant(half("eq", b), half("es", b), A("et", 3 - b, 515 - b)), unpack((b,))) for b in range(4)]

        def spare(n=1):
            for f in aside[:n]:
                f()
            del aside[:n]

        def masks():
            if t == 0:
                act(A("mst", 0, C), A("sq", 0, C), ACT.Identity, scale=-BIG / 8, bias=9 * BIG / 8)
                act(A("pm", 0, K), A("oh", 0, K), ACT.Identity, scale=2e29, bias=-1e29)
                act(A("mst", 15, C, 16), A("mst", 15, C, 16), ACT.Identity, bias=-BIG - OFF)

        steps = ORDER1 if t else [-ORDER1[0]] + ORDER1[2:]
        run(steps, order1, {"mask": lambda: own(1, 0), "carry": lambda: own(1, 1), "partner": partner_u if t else spare, "masks": masks})
        spare()
        scan(A("sc", 0, C), A("ps0", 0, C), A("md", 0, C), ALU.max, ALU.add)
        spare()
        act(A("ssb"), A("ps3", 0, C), ACT.Copy)
        ts(of, A("sc", 15, C, 16), -1.0, ALU.mult, finr, ALU.add)
        send(peer[t], af, of, "af%d" % t)
        spare()
        if t == 0:
            partner_u()
            iota(A("crow", 16, 45), [[16, 29]], 1 - NP)
        mm(A("ps1", 0, C), up[0], up[1], lq, ls)
        if t > 0:
            unpack(range(4))
        else:
            act(A("fl", 768), A("sq"), ACT.Identity, scale=-16.0, bias=144.0)
        act(A("prep", 0, C), A("cidx"), ACT.Identity, scale=0.0, bias=GAP)
        act(A("spb"), A("ps1", 0, C), ACT.Copy)
        if t == 0:
            act(A("fl", 768 + 15, None, 16), A("fl", 768 + 15, None, 16), ACT.Identity, bias=GAP - OFF - 128)
            for a, scale, bias in ((fin, -1.0, -2 * SMALL), (turn, -2.0, 15.0)):
                act(a, kc, ACT.Identity, scale=scale, bias=bias)
            for a, bias in ((A("vv", 0, SPARE), -1e29), (col("dg", 38), 1e29)):
                act(a, A("zero", 0, a[2] - a[1]), ACT.Identity, bias=bias)
        early, mid, late = ((), (), range(4)) if t == 0 else ((), (0,), (1, 2, 3)) if t == far else ((0, 1), (2,), (3,))
        halve(early)
        scatter(A("orep"), of, A("cidx"))
        spare()
        scan(A("sc", 368, NP), A("orep", C - K, C), A("mst", 0, K), ALU.max, ALU.add)
        spare()
        ts(ol, A("sc", 383, NP, 16), OFF, ALU.add)
        send(peer[t], al, ol, "al%d" % t)
        act(A("ss", 0, K), A("ssb"), ACT.Copy, off=ol)
        spare()
        if t == 0:
            op("g", lambda: g.affine_select(ap(half("wt", 2, 512)), ap(half("wt", 0, 512)), [[0, 128], [1, 4]], ALU.is_equal, 0.0, -3, 0),
               [half("wt", 0, 512)], [half("wt", 2, 512)])
            op("g", lambda: g.affine_select(ap(A("et")), ap(A("wt", 0, 520)), [[1, 520]], ALU.is_equal, 0.0, -3, -4), [A("wt", 0, 520)], [A("et")])
            for r in runs:
                if r[0][1] >= NV:
                    iota(*r)
            iota(A("p0", 0, SPARE), [[0, SPARE]], 0)
        lists = [lambda b=b: ts(A("o4", 6 * b, 6 * b + 6), ol, 4.0, ALU.mult, float(b), ALU.add) for b in range(4)]
        aside.extend(lists if t else [])
        act(A("si", NV0, NV), A("ss", 0, K), ACT.Copy, off=A("ijl", 0, nv))
        if t == 0:
            for f in lists[:3]:
                f()
            act(A("pm", K), A("pm", K), ACT.Identity, scale=2e29, bias=-1e29)
            act(A("bb", 16, 45), A("crow", 16, 45), ACT.Identity, bias=m15)
        halve(mid)
        if t == 1:
            i = K - 1
            while i >= 0:
                n = len([r for r in range(K) if ROWS[r] == ROWS[i]])
                iota(A("nn", K - 1 - i, K - 1 - i + n), [[-ROWS[i], n]], sum(ROWS[:i]) + K - 1)
                i -= n
        if t == 0:
            act(A("cb", 19, 33), A("bb", 19, 33), ACT.Identity, bias=turn)
        act(col("ss", K), col("ss", K - 1), ACT.Identity, bias=few)
        act(col("ss", K + 1), col("ss", K - 1), ACT.Identity, bias=none)
        scatter(A("ee"), af, A("spb"))
        spare()
        scan(A("hh", 368, NP), half("pm", 0, K), A("ee", C - K, C), ALU.max, ALU.min)
        at = 368
        rows = []
        for i in range(1, K):
            lo = max(at - ROWS[i], NV)
            if lo < at:
                rows.append((lo, at, i))
            at -= ROWS[i]
        act(A("vv", SPARE, NV0), A("ss", 0, NV0 - SPARE), ACT.Identity, bias=col("ee", C - 1))
        for lo, at, i in reversed(rows):
            act(A("vv", lo, at), A("ee", C - (at - lo), C), ACT.Identity, bias=col("ss", K - 1 - i))
        tt(A("vv", NV0, NV), A("ee", C - K, C), A("si", NV0, NV), ALU.add, off=A("ijl", 16, 16 + nv))

        def rows_own(which):
            for i, m0, m1 in which:
                act(A("dg", m0, m1), A("hh", NP - 1 - 16 * (m1 - m0 - 1), NP, 16), ACT.Identity, bias=col("ss", K - 1 - i))

        def place(k, i):
            bank, first, a, b = PARTS[k]
            off = A("off2", a // 16 + (a > 0), b // 16 + (a > 0))
            if i == 0:
                tt(A("md", a + 15, b, 16), A("bb", 16 + a // 16, 16 + b // 16), A("rsum", 16 + a // 16, 16 + b // 16), ALU.subtract)
            elif i == 1:
                scan(A("sc", a, b), A(bank, a - first, b - first), A("md", a, b), ALU.max, ALU.add)
            elif i == 2:
                ts(off, A("sc", a + 15, b, 16), -1.0, ALU.mult, fin, ALU.add)
            else:
                scatter(A("prep"), off, A("p0", a, b))

        def rows():
            rows_own([(2, 18, 20), (3, 17, 18)])
            act(A("dg", 32, 38), A("hh", 368 + RUN - 1, NP, RUN), ACT.Identity, bias=col("ss", K))

        rows_own([(1, 20, 23)])
        scan(A("sc", 368, NP), half("pm", 1, K), A("ee", C - K, C), ALU.max, ALU.min)
        if t == 0:
            op("y", lambda: [g.sync.dma_start(u8(A("wq")), T.wc[:]), g.sync.dma_start(ap(A("wp")), T.ws[:])], [A("ee")], [A("wq"), A("wp")], sem="dw")
            op("y", lambda: [g.sync.dma_start(ap(A("vt")), T.v[:])], [], [A("vt")], sem="dv")
        tt(A("xm", 48, 272), A("vv", 48, 272), A("oh", 0, 224), ALU.mult)
        run(ORDER2, order2, {
            "carry": lambda: scan(A("hh", 48, 272), A("rs", 0, 224), A("xm", 48, 272), ALU.mult, ALU.add),
            "spare": lambda: spare(t == 0),
            "rows": rows,
            "ends": lambda: act(col("dg", COARSE), col("sc", NP - 1), ACT.Identity, bias=col("ss", K + 1)),
            "runs": lambda: scan(A("sc", 0, 368), A("ps2", 0, 368), A("fl", 768), ALU.max, ALU.add),
            "list": lambda: ts(A("off2", 32, 55), A("sc", 15, 368, 16), OFF - GAP, ALU.add, 1.0 / RUN, ALU.mult),
            **{"up%d" % i: lambda i=i: place(0, i) for i in range(4)}})
        spare()
        place(1, 1)
        spare()
        place(1, 2)
        spare(len(aside))
        if t == 0:
            act(A("ap"), A("tt"), ACT.Copy, off=A("o4"), scale=0.5)
        halve(late)
        if t > 0:
            arrived((0,))
            act(A("ap"), A("tt"), ACT.Copy, off=A("o4"), scale=0.5)
            arrived((1,))
        place(1, 3)
        act(half("fl", 1), half("prep", 1), ACT.Relu, bias=1.0 - GAP)
        arrived((2, 3) if t else range(4))
        ts(half("fl", 0), half("prep", 0), GAP, ALU.is_equal)

        def every(name, a):
            return A(name, a + 15, a + 128, 16)

        chain = [
            lambda h: scan(half("sc", h), half("prep", h), half("mst", h), ALU.max, ALU.add),
            lambda h: scan(half("fl", 2 + h), A("zero", 0, 128), half("fl", h), ALU.add, ALU.subtract, col("fl", C + 127) if h else 0.0),
            lambda h: scan(half("fl", 4 + h), half("fl", 2 + h), half("fl", 6), ALU.max, ALU.add, GAP - OFF),
            lambda h: tt(half("x32", h, 8), every("sc", 128 * h), every("fl", 512 + 128 * h), ALU.min),
            lambda h: ts(half("il", h, 8), half("x32", h, 8), OFF - 48, ALU.add, 1.0 / 128, ALU.mult),
            lambda h: ts(half("x32", 4 + h, 8), half("x32", h, 8), 127, ALU.bitwise_and),
            lambda h: cp(half("jl", h, 8), half("x32", 4 + h, 8))]
        for i, h in ((0, 0), (1, 0), (0, 1), (2, 0), (1, 1), (3, 0), (2, 1), (4, 0), (5, 0), (3, 1), (6, 0), (5, 1), (4, 1), (6, 1)):
            chain[i](h)
        nq, ns = ("tq%d" % (t + 1), "ts%d" % (t + 1)) if t < R - 1 else ("fq", "fs")

        def layer(h):
            quant(half("zq", h), half("zs", h), half("zz", h, 512))
            for b in range(4):
                mm(A("ps%d" % (4 * (1 - h) + b), 0, 128), half("wq", b), half("wp", b), half("zq", h), half("zs", h))

        def state(h):
            quant(half(nq, h), half(ns, h), half("tt", h, 512))
            if t + 1 == far and h == 0:
                send(aid, A("rtq"), half(nq, 0), "rt")
                send(aid, A("rts"), half(ns, 0), "rt")
            if t < R - 1 and h == 0:
                scores(t + 1, 0)
            if t == R - 1:
                mm(A("ps%d" % (4 + h), 0, 128), A("vq"), A("vs"), half(nq, h), half(ns, h))
                op("y", lambda: [g.sync.dma_start(T.oc[:, 512 * h:512 * h + 512], u8(half(nq, h)))], [half(nq, h)], [], sem="dq" if h else "dr")

        for k in range(8):
            h, b = k // 4, k % 4
            act(half("ag", k), half("ap", b, K), ACT.Copy, off=half("il", h, 8))
            tt(A("zz", 512 * h + b, 512 * h + 512, 4), half("ep", b, K), half("ag", k), ALU.add, off=half("jl", h, 8))
            if k == 4:
                layer(0)
            if k == 7 and t == 1:
                quant(A("vq"), A("vs"), A("vt"))
        for k in range(8):
            h, b = k // 4, k % 4
            if k == 0:
                layer(1)
            act(half("rl", k), A("ps%d" % (4 * (1 - h) + b), 0, 128), ACT.Relu, scale=0.03125)
            tt(A("tt", 512 * h + b, 512 * h + 512, 4), half("rl", k), A("zz", 512 * h + b, 512 * h + 512, 4), ALU.add)
            if k == 4:
                state(0)
            if k == 7 and t < R - 1:
                own(0, 0)
        if t == R - 1:
            act(half("nb", 0, C), A("nn"), ACT.Copy, off=A("il"))
            act(half("nb", 1, C), A("cidx", 0, K), ACT.Copy, off=A("jl"))
            act(half("ysb", 0), A("ps4", 0, 128), ACT.Copy)
            op("y", lambda: [g.sync.dma_start(T.y[:, 0:128], ap(half("ysb", 0)))], [half("ysb", 0)], [], sem="dr")
        state(1)
        if t < R - 1:
            own(0, 1)

    tt(half("nb", 2, C), half("nb", 0, C), half("nb", 1, C), ALU.subtract)
    op("s", lambda: [g.scalar.dma_start(T.osc[4 * k:4 * k + 4, :], T.fs[32 * k:32 * k + 4, :]) for k in (2, 3)], [A("fs")], [], sem="dy")
    act(half("ysb", 1), A("ps5", 0, 128), ACT.Copy)
    op("y", lambda: [g.sync.dma_start(T.osc[4 * k:4 * k + 4, :], T.fs[32 * k:32 * k + 4, :]) for k in (0, 1)], [A("fs")], [], sem="dq")
    op("y", lambda: [g.sync.dma_start(T.ol[:], T.nb[0:128:16, 2 * C:3 * C])], [half("nb", 2, C)], [], sem="do")
    op("s", lambda: [g.scalar.dma_start(T.y[:, 128:256], ap(half("ysb", 1)))], [half("ysb", 1)], [], sem="dy")
    for s in count:
        g.wait_ge(T.sem[s], count[s])
